import numpy as np, ml_dtypes
CORES = [6,15,38,47]
N = 4
import mx_ref
BF = ml_dtypes.bfloat16
def gentries(a):
    return np.ascontiguousarray(a.reshape(8, 16, -1).transpose(0, 2, 1)).reshape(8, -1)
def gtable(e):
    e = np.asarray(e); return np.ascontiguousarray(e.reshape(8, -1, 16).transpose(0, 2, 1)).reshape(128, -1).astype(np.int32)
def gcols(t, e):
    v = np.concatenate([t.reshape(8, 16, -1, 4), np.zeros((8, 16, 1, 4), BF)], axis=2)
    return np.ascontiguousarray(np.stack([v[g][:, e[g]] for g in range(8)])).reshape(128, -1)
def gpick(z, e):
    return np.concatenate([z[16 * g:16 * g + 16][:, e[g]] for g in range(8)])
def tile(rs):
    return np.stack(rs, axis=2).reshape(128, -1).astype(BF)
def pick(q, e):
    c = np.concatenate([q[0].reshape(128, -1, 4), np.zeros((128, 1, 4), np.uint8)], axis=1); s = np.concatenate([q[1], np.ones((16, 1), np.uint8)], axis=1)
    return (np.ascontiguousarray(c[:, e].reshape(128, -1)), np.ascontiguousarray(s[:, e]))
def join(*qs):
    return (np.concatenate([q[0] for q in qs], axis=1), np.concatenate([q[1] for q in qs], axis=1))
def put(q, e, v):
    c, s = q[0].reshape(128, -1, 4).copy(), q[1].copy(); c[:, e] = v[0].reshape(128, -1, 4); s[:, e] = v[1]
    return (c.reshape(128, -1), s)
def pk(c, s):
    return (np.ascontiguousarray(c), mx_ref.live(s))
def emit(q):
    return q[0], q[1]
def packed(v, rng):
    q = [mx_ref.quantize(np.ascontiguousarray(v[r])) for r in range(N)]
    return np.stack([a for a, b in q]), np.stack([mx_ref.plane(b, rng) for a, b in q])
def values_of_codes():
    e, c = np.zeros((128, 128, 4), np.float32), np.zeros((128, 2, 4), np.uint8)
    e[np.arange(128), np.arange(128), 0] = 1
    c[:127, :, 0] = np.arange(256).reshape(2, 128).T[:127]
    return mx_ref.matmul(mx_ref.quantize(e.reshape(128, 512).astype(BF)), (c.reshape(128, 8), np.full((16, 2), 127, np.uint8))).T.reshape(-1).astype(np.float64)
CODE_VALUE, SCALE_VALUE = values_of_codes(), 2.0 ** (np.arange(256) - 127.0)
def decode(q):
    return (CODE_VALUE[q[0]].reshape(16, 8, -1, 4) * SCALE_VALUE[q[1]][:, None, :, None] + 0.0).reshape(128, -1).astype(np.float32)
def f(rng, *shape):
    return mx_ref.flush((rng.standard_normal(shape, dtype=np.float32) * np.exp2(rng.integers(-2, 3, shape[:-1] + (1,)))).astype(BF))
def wide(rng, *shape, cols=0):
    v = rng.standard_normal(shape, dtype=np.float32) * np.exp2(rng.integers(-12, 13, shape)).astype(np.float32)
    if cols: v *= np.repeat(np.exp2(rng.integers(-cols, cols + 1, shape[:-2] + (1, shape[-1] // 4))) * (rng.random(shape[:-2] + (1, shape[-1] // 4)) > 0.0625), 4, axis=-1).astype(np.float32)
    return mx_ref.flush(v.astype(BF))
C = 416
STEP = [1, 2, 3]
def numbers_of(rng):
    return {"x": np.array(f(rng, N, 128, 4 * C)), "u": np.array(f(rng, N, 128, 512)), "v": np.array(f(rng, N, 128, 512))}
def drawn(rng):
    e = np.tile(np.arange(C), (N, 8, 1))
    p, k, s, m = rng.permuted(e, axis=2), rng.permuted(e, axis=2), rng.permuted(e, axis=2), np.zeros_like(e)
    np.put_along_axis(m, s[:, :, ::2], s[:, :, 1::2], 2)
    np.put_along_axis(m, s[:, :, 1::2], s[:, :, ::2], 2)
    return p, k, m
def stored(p, k, m):
    return {"pg": np.stack([gtable(p[r]) for r in range(N)]), "kg": np.stack([gtable(k[r]) for r in range(N)]), "mg": np.stack([gtable(m[r]) for r in range(N)])}
def layers(rng):
    return np.array(f(rng, N, 128, 2048)).reshape(N, 8, 16, 4, 8, 16, 4)
def weights(rng, w):
    c, s = packed(np.ascontiguousarray(w).reshape(N, 128, 2048), rng)
    return {"wc": c, "ws": s}
def setup_inputs(rng):
    return {**numbers_of(rng), **stored(*drawn(rng)), **weights(rng, layers(rng))}
def setup_inputs_ties(rng):
    d = numbers_of(rng)
    o = rng.permutation(N)
    s = rng.integers(-1, 2, (N, 2, 8, C))
    s[o[0]] = 0
    s[o[1]] = 1
    s[o[2], 0] = np.where(np.arange(C) % 2 == 1, 1, rng.integers(-1, 1, (8, C)))
    x = d["x"].astype(np.float32).reshape(N, 8, 16, C, 4)
    u = d["u"].astype(np.float32).reshape(N, 128, 128, 4)
    for i in range(2):
        x[:, :, i] = 0
        x[:, :, i, :, 0] = s[:, i]
        u[:, :, i::16] = 0
        for h in range(0, 128, 16): u[:, h + i, h + i, 0] = 1
    p, k, m = drawn(rng)
    p[o[2]] = k[o[2]] = np.arange(C)
    m[o[2]] = np.arange(C) ^ 1
    w = layers(rng)
    w[:, :, :, :, :, :8] = 0
    return {"x": x.reshape(N, 128, 4 * C).astype(BF), "u": u.reshape(N, 128, 512).astype(BF), "v": d["v"], **stored(p, k, m), **weights(rng, w)}
def setup_inputs_near(rng):
    d = numbers_of(rng)
    o = rng.permutation(N)
    k = np.where(o % 2 == 0, 2.0 ** -30, 1.0)
    x = np.zeros((N, 8, 16, C, 4))
    s = rng.integers(-1, 2, (N, 2, 8, C)) * k[:, None, None, None]
    for i in range(2):
        x[:, :, 2 * i, :, 0] = 1.125 * s[:, i]
        x[:, :, 2 * i + 1, :, 0] = -1.25 * s[:, i]
    x[:, :, 9, :, 0] = rng.choice([-1.0, 1.0], (N, 8, C)) * 2.0 ** -17
    x[:, :, 10:] = rng.choice([-1.0, 1.0], (N, 8, 6, C, 4)) * (1 + 0.125 * rng.integers(0, 8, (N, 8, 6, C, 4))) * np.exp2(-12.0 - rng.integers(0, 4, (N, 8, 6, C, 4)))
    u = d["u"].astype(np.float32).reshape(N, 128, 128, 4)
    u[:, :, ::16] = 0
    u[:, :, 1::16] = 0
    w = layers(rng)
    w[:, :, :8] = 0
    w[:, :, :, :, :, :10] = 0
    for r in range(N):
        for g in rng.permutation(8)[:4]: x[r, g, 0, rng.integers(C), 0] = 2.0 ** 30 * rng.choice([-1.0, 1.0])
        if o[r] == 0:
            x[r, :, :8] = 0
            x[r, :, 0, :, 0] = 2.0 ** -30
        for g in range(8):
            h = 16 * g
            if o[r] == 0:
                u[r, h + 4, h, 0] = 2.0 ** -30
                u[r, h + 4, h + 1, 0] = -2.0 ** -30
                w[r, g, 8, 0, g, 4, 0] = 2.0 ** -8
                w[r, g, 9, 0, g, 4, 0] = 2.0 ** -22
            else:
                for i in range(2):
                    u[r, h + 2 * i, h + i, 0] = 1.125 * k[r]
                    u[r, h + 2 * i + 1, h + i, 0] = k[r]
    return {"x": x.astype(np.float32).reshape(N, 128, 4 * C).astype(BF), "u": u.reshape(N, 128, 512).astype(BF), "v": d["v"], **stored(*drawn(rng)), **weights(rng, w)}
def setup_inputs_odd(rng):
    d = numbers_of(rng)
    x = (1.0 + (2 * rng.integers(0, 64, (N, 16, 8, C, 4)) + 1) * 2.0 ** -7) * np.exp2(-rng.integers(0, 7, (N, 16, 8, C, 4)).astype(np.float64)) * rng.choice([-1.0, 1.0], (N, 16, 8, C, 4))
    x[:, ::2, 0, :, 0] = 1.96875 * 2.0 ** 8 * rng.choice([-1.0, 1.0], (8, 1))
    x[:, 1::2, 0, :, 0] = 1.96875 * 2.0 ** 8 * rng.choice([-1.0, 1.0], (N, 8, C))
    u = d["u"].astype(np.float32).reshape(N, 16, 8, 128, 4)
    u[:, :, 0, ::16] = 0
    u[:, :, :, 1::16] = 0
    h = rng.permutation(8) % 4
    for g in range(8):
        x[:, 2 * g, 1, :, 0] = (8 + rng.integers(0, 2, (N, C))) * 2.0 ** (int(h[g]) - 9)
        x[:, 2 * g, 2, :, 0] = -2.0 ** (int(h[g]) - 6)
        u[:, 2 * g, 1:3, 16 * g + 1, 0] = 1
    w = layers(rng)
    for i in (0, 8):
        w[:, :, i] = 0
        w[:, :, :, :, :, i] = 0
    w[:, :, :, 0, :, 1:3] = 0
    for g in range(8): w[:, g, 0, 0, g, 0, 0] = -0.5
    p, k, m = drawn(rng)
    t = int(rng.integers(N))
    p[t] = m[t] = np.arange(C)
    k[t] = rng.permutation(C)
    return {"x": x.astype(np.float32).reshape(N, 128, 4 * C).astype(BF), "u": u.reshape(N, 128, 512).astype(BF), "v": d["v"], **stored(p, k, m), **weights(rng, w)}
def setup_inputs_ends(rng):
    d = numbers_of(rng)
    o, ep, ek, em = [rng.permutation(N) % 4 for i in range(4)]
    s = rng.choice([-1.0, 1.0], (N, 128, C, 4))
    s[o == 0] = -1
    s[o == 1] = rng.choice([-1.0, 1.0], (N, 1, C, 1))[o == 1]
    x = s * (0.90 + 0.02 * rng.random((N, 128, C, 4))) * 2.0 ** 30
    tiny = (1 + 0.125 * rng.integers(0, 8, (N, 128, C, 4))) * 2.0 ** -30
    x[o == 3] = (s * tiny)[o == 3]
    x[:, 8:16] = tiny[:, 8:16]
    u = d["u"].astype(np.float32).reshape(N, 128, 128, 4)
    for r in range(N):
        h = rng.permutation(8)
        size = 2.0 ** -30 if o[r] == 3 else 2.0 ** 30
        u[r, :, ::16] = ((h % 2 * 2 - 1) * size)[None, :, None]
        u[r, :, 1::16] = ((h // 2 % 2 * 2 - 1) * size)[None, :, None]
    v = rng.choice([-1.0, 1.0], (N, 128, 512)) * np.where(o % 2 == 0, 2.0 ** 30, 2.0 ** -30)[:, None, None]
    p, k, m = drawn(rng)
    line = np.arange(C)
    p[ep == 0] = line
    p[ep == 1] = (line + 1) % C
    p[ep == 2] = C - 1 - line
    k[ek == 0] = line
    k[ek == 1] = C - 1 - line
    k[ek == 2] = (line + C - 1) % C
    m[em == 0] = line
    m[em == 1] = C - 1 - line
    m[em == 2] = line ^ 1
    w = np.zeros((N, 128, 4, 128, 4), np.float32)
    i = np.arange(128)
    for b in range(4): w[:, i, b, i, b] = np.where((i >= 8) & (i < 16), np.where(o == 3, 2.0 ** 8, 2.0 ** -8)[:, None], -0.25)
    return {"x": x.astype(np.float32).reshape(N, 128, 4 * C).astype(BF), "u": u.reshape(N, 128, 512).astype(BF), "v": v.astype(np.float32).astype(BF), **stored(p, k, m), **weights(rng, w.astype(BF))}
def setup_inputs_spread(rng):
    d = setup_inputs(rng)
    d["x"] = wide(rng, N, 128, 4 * C, cols=6)
    return d
def check_inputs(d):
    b = []
    for k in ("x", "u", "v"):
        a = np.abs(d[k].astype(np.float32))
        if not (np.isfinite(a).all() and ((a == 0) | (a >= 2.0 ** -30) & (a <= 2.0 ** 30)).all()): b.append("a value of " + k)
    none, least, most = [emit(mx_ref.quantize(np.full((128, 16), k, np.float32).astype(BF)))[1][0, 0] for k in (0.0, 2.0 ** -8, 2.0 ** 8)]
    top = emit(mx_ref.quantize(np.full((128, 16), 1.9921875, np.float32).astype(BF)))[0][0, 0] & 0x7F
    line = np.arange(C)
    for r in range(N):
        for k in ("pg", "kg"):
            if not (np.sort(gentries(d[k][r]), axis=1) == line).all(): b.append(k + ": no permutation")
        m = gentries(d["mg"][r])
        if not ((m >= 0) & (m < C)).all(): b.append("an entry of mg")
        elif not (np.take_along_axis(m, m, 1) == line).all(): b.append("mg: a mate's mate")
        if ((d["wc"][r] == 0x7F) | (d["wc"][r] == 0xFF)).any(): b.append("wc: a code that is no number")
        if ((d["wc"][r] & 0x7F) > top).any(): b.append("wc: a code that quantize_mx does not give")
        s = mx_ref.live(d["ws"][r])
        if ((s != none) & ((s < least) | (s > most))).any(): b.append("ws: a scale out of range")
    return b
def reference(x, u, v, pg, kg, mg, wc, ws):
    qu = [mx_ref.quantize(u[r]) for r in range(N)]
    lay = [pk(wc[r], ws[r]) for r in range(N)]
    p, k, m = [[gentries(a[r]).astype(np.int64) for r in range(N)] for a in (pg, kg, mg)]
    now = [x[r] for r in range(N)]
    for step in STEP:
        own, land, mosaic = [], [], []
        for r in range(N):
            q = mx_ref.quantize(now[r])
            s = mx_ref.matmul(qu[r], q)
            first = (s[::16] > 0).astype(np.int64)
            e = first + 2 * (s[1::16] > 0).astype(np.int64)
            at = np.zeros((8, C), np.int64)
            for g in range(8):
                power = np.ones(C, np.int64) if g == 0 else e[g - 1][at[g - 1]]
                a = k[r][g]
                for i in range(3): a = np.where(i < power, p[r][g][a], a)
                at[g] = a
            bit = np.take_along_axis(first, at, 1)
            p[r] = np.where(bit != np.take_along_axis(bit, m[r], 1), np.take_along_axis(p[r], m[r], 1), p[r])
            land.append(at)
            own.append(decode(q))
            mosaic.append(mx_ref.quantize(gcols(own[r].astype(BF), at)))
        made = []
        for r in range(N):
            h = [mx_ref.matmul(pick(lay[r], np.arange(128 * b, 128 * b + 128)), mosaic[r ^ step]) * np.float32(0.03125) for b in range(4)]
            made.append(tile([own[r][:, b::4] + gpick(h[b], land[r]) for b in range(4)]))
        now = made
    y, pl = np.zeros((N, 128, C), np.float32), np.zeros((N, 8, 2 * C), np.float32)
    oc, osc = np.zeros((N, 128, 4 * C), np.uint8), np.zeros((N, 16, C), np.uint8)
    for r in range(N):
        q = mx_ref.quantize(now[r])
        y[r] = mx_ref.matmul(mx_ref.quantize(v[r]), q)
        pl[r] = np.concatenate([land[r], p[r]], axis=1)
        oc[r], osc[r] = emit(q)
    return {"y": y, "pl": pl, "oc": oc, "osc": osc}

@@ -1,0 +1,530 @@
+from concourse.bass import DstId, RemoteDMATransfer
+from concourse.mybir import dt, AluOpType, ActivationFunctionType
+
+C = 416
+CA = 224
+NL = C // 16
+STEP = (1, 2, 3)
+F32, BF16, I32, U16, CODE, U8 = "float32", "bfloat16", "int32", "uint16", "float8_e4m3fn_x4", "uint8"
+
+SCRATCH, PART = {}, {}
+
+
+def _buf(cols, dtype, *names, where="sbuf"):
+    for name in names:
+        SCRATCH[name] = (where, [128, cols], dtype)
+
+
+def _parts(whole, cols, dtype, *names):
+    SCRATCH[whole] = ("sbuf", [128, cols * len(names)], dtype)
+    for i, name in enumerate(names):
+        PART[name] = (whole, i * cols, cols)
+
+
+_buf(512, F32, *["pb%d" % i for i in range(8)], where="psum")
+_buf(2, I32, "ip")
+_buf(12, I32, "ib")
+_buf(16, F32, "cols", "d00")
+_buf(520, F32, "i520")
+_buf(C, F32, "kk", "yt")
+_buf(16, F32, "j16", "k16", "n16", "t16")
+_buf(C, BF16, "kb", "bw", "scw", "z", "zz", "nd", "ns")
+_buf(64, F32, "im")
+_buf(64, BF16, "maska")
+_buf(128, F32, "thr")
+_buf(NL, I32, "iw", "kgw", "mgw", "pgw")
+_buf(8, I32, "iu")
+_buf(8, U16, "lu0", "lu1")
+_buf(4, U16, "la4")
+_buf(2, U16, "lrep")
+_buf(520, BF16, "w1", "ones")
+_buf(560, BF16, "w2")
+_buf(512, BF16, "pat", "msk", "msk2", "w3", "w3a", "ut", "vt", "at")
+_buf(NL, F32, "jw", "mf", "mj", "t0", "td", "nm", "tau")
+_buf(NL, U16, "lpos", "lm", "ltau", "lpw", "lq")
+_buf(C, I32, "pgf")
+_buf(4 * C, BF16, "xt", "x2", "x3", "x4", "zt")
+_buf(2048, BF16, "mt")
+for _c, _s, _n in (("uq", "uqs", 128), ("vq", "vqs", 128), ("wq", "wqs", 512), ("b3", "b3s", 128), ("mq", "mqs", 512), ("aq", "aqs", 128), ("zq", "zqs", C)):
+    _buf(_n, CODE, _c)
+    _buf(_n, U8, _s)
+_parts("upc", 128, CODE, "up", "uc")
+_parts("upp", 128, U8, "ups", "ucs")
+_parts("ec", 128, CODE, *["e%d" % i for i in range(4)])
+_parts("ep", 128, U8, *["es%d" % i for i in range(4)])
+_parts("bc", 128, CODE, *["b2%d" % i for i in range(4)])
+_parts("bp", 128, U8, *["b2s%d" % i for i in range(4)])
+_parts("hs", C, F32, *["hs%d" % i for i in range(4)])
+_parts("fb", C, BF16, *["fb%d" % i for i in range(4)])
+_parts("fp", C, BF16, *["fp%d" % i for i in range(4)])
+_parts("tg", C, F32, "tg1", "tg2", "tg3")
+_parts("tsum", C, F32, "ts1", "ts2", "ts3")
+_parts("tf", NL, F32, "tf1", "tf2", "tf3")
+_parts("lists", NL, U16, "l0", "l1", "l2", "l3")
+_buf(112, F32, "sc", "d0")
+_buf(4 * NL, F32, "ph", "sl", "cs1", "cs2", "cs3")
+_buf(2 * C, F32, "pl_t")
+for _i in (1, 2, 3, 4):
+    _buf(C, CODE, "qc%d" % _i)
+    _buf(C, U8, "qs%d" % _i)
+for _i in (1, 2, 3):
+    _buf(C, F32, "p%d" % _i)
+    _buf(C, CODE, "rc%d" % _i)
+    _buf(C, U8, "rs%d" % _i)
+    _buf(NL, U16, "la%d" % _i, "lp%d" % _i)
+
+SEMAPHORES = ["s_v", "s_a", "s_p", "s_g", "loc"] + ["d_%d" % i for i in range(40)] + ["r_%s%d" % (k, i) for k in "csl" for i in (1, 2, 3)]
+
+WAKE = 100.0
+LOOK = 0.0
+BIAS = 300.0
+CY = 0.83
+
+
+def _hit(a, b):
+    if a[1] >= b[2] or b[1] >= a[2]:
+        return False
+    if a[3] == b[3] and a[3] > 1:
+        return a[1] % a[3] == b[1] % a[3]
+    return True
+
+
+def rank_program(g, core, T, topo):
+    rank = T.rank_of(core)
+    if rank is None:
+        return
+    A = AluOpType
+    AF = ActivationFunctionType
+    ops, seen, bias = [], {}, [0.0]
+
+    def V(name, lo=0, hi=None, st=1):
+        whole, at, cols = PART.get(name, (name, 0, SCRATCH.get(name, (0, (0, 0)))[1][1]))
+        return (whole, at + lo, at + (cols if hi is None else hi), st)
+
+    def ap(v):
+        return T[v[0]][:, v[1]:v[2]] if v[3] == 1 else T[v[0]][:, v[1]:v[2]:v[3]]
+
+    def ind(v, l):
+        return ap(v).indirect(ap(l))
+
+    def n_of(v):
+        return -(-(v[2] - v[1]) // v[3])
+
+    def add(q, cost, reads, writes, emit, kind="c", sem=None, amount=0, after=()):
+        i = len(ops)
+        deps = {}
+        for mode, views in ((0, reads), (1, writes)):
+            for v in views:
+                if v is None:
+                    continue
+                psum = v[0].startswith("pb")
+                for (j, m, w) in seen.setdefault(v[0], []):
+                    if j == i:
+                        continue
+                    same = ops[j]["q"] == q and len(q) == 1
+                    if psum:
+                        if same and not (m or mode):
+                            continue
+                    elif not (m or mode) or not _hit(v, w):
+                        continue
+                    raw = m == 1 and mode == 0
+                    deps[j] = deps.get(j, False) or raw
+                seen[v[0]].append((i, mode, v))
+        for j in after:
+            deps[j] = True
+        ops.append({"q": q, "cost": cost, "deps": deps, "emit": emit, "kind": kind, "sem": sem, "amount": amount, "bias": bias[0]})
+        return i
+
+    def vcost(n, f=1.0):
+        return max(64.0, n * f) * CY
+
+    def gcost(n):
+        return 50 + 1.3 * n * CY
+
+    def ts(out, in0, s1, s2, op0, op1=None, q="V", f=1.0, lst=None):
+        rd = [in0, lst] + [s for s in (s1, s2) if isinstance(s, tuple)]
+        def emit(e):
+            a1 = ap(s1) if isinstance(s1, tuple) else s1
+            a2 = ap(s2) if isinstance(s2, tuple) else s2
+            src = ap(in0) if lst is None else ind(in0, lst)
+            if op1 is None:
+                return e.tensor_scalar(ap(out), src, a1, None, op0)
+            return e.tensor_scalar(ap(out), src, a1, a2, op0, op1)
+        return add(q, vcost(n_of(out), f) if lst is None else gcost(n_of(out)), rd, [out], emit)
+
+    def tt(out, in0, in1, op, lst=None, f=1.0):
+        def emit(e):
+            return e.tensor_tensor(ap(out), ap(in0) if lst is None else ind(in0, lst), ap(in1), op)
+        return add("V", vcost(n_of(out), f) if lst is None else gcost(n_of(out)), [in0, in1, lst], [out], emit)
+
+    def copy(out, in_):
+        return add("V", vcost(n_of(out)), [in_], [out], lambda e: e.tensor_copy(ap(out), ap(in_)))
+
+    def fill(out, val):
+        return add("V", vcost(n_of(out), 0.5), [], [out], lambda e: e.memset(ap(out), val))
+
+    def scan(out, d0, d1, f=1.0):
+        return add("V", vcost(n_of(out), f), [d0, d1], [out], lambda e: e.tensor_tensor_scan(ap(out), ap(d0), ap(d1), 0.0, A.mult, A.add))
+
+    def act(out, in_, func, lst=None, scale=None):
+        def emit(e):
+            src = ap(in_) if lst is None else ind(in_, lst)
+            if scale is None:
+                return e.activation(ap(out), src, func)
+            return e.activation(ap(out), src, func, scale=ap(scale))
+        return add("A", vcost(n_of(out)) if lst is None else 15 + gcost(n_of(out)), [in_, lst, scale], [out], emit)
+
+    def either(out, in_, lst, relu=False):
+        def emit(e, eng):
+            if eng == "V":
+                if relu:
+                    return e.tensor_scalar(ap(out), ind(in_, lst), 0.0, None, A.max)
+                return e.tensor_copy(ap(out), ind(in_, lst))
+            return e.activation(ap(out), ind(in_, lst), AF.Relu if relu else AF.Copy)
+        return add("VA", gcost(n_of(out)), [in_, lst], [out], emit)
+
+    def out_of_psum(out, in_, scale=None, q="A"):
+        def emit(e, eng=None):
+            if eng == "V" or q == "V":
+                if scale is None:
+                    return e.tensor_copy(ap(out), ap(in_))
+                return e.tensor_scalar(ap(out), ap(in_), scale, None, A.mult)
+            if scale is None:
+                return e.activation(ap(out), ap(in_), AF.Copy)
+            return e.activation(ap(out), ap(in_), AF.Copy, scale=scale)
+        return add(q, vcost(n_of(out)), [in_], [out], emit)
+
+    def quant(c, s, t):
+        return add("V", 12 + 0.22 * n_of(t), [t], [c, s], lambda e: e.quantize_mx(ap(c), ap(s), ap(t)))
+
+    def mm(out, terms, after=()):
+        def emit(e):
+            last = None
+            for k, (a, b, c, d) in enumerate(terms):
+                last = e.matmul_mx(ap(out), ap(a), ap(b), ap(c), ap(d), k == 0, k == len(terms) - 1)
+            return last
+        return add("P", (n_of(out) + 16) * CY * 1.3 * len(terms), [v for t in terms for v in t], [out], emit, after=after)
+
+    def iota(out, pattern, base, cm):
+        small = SCRATCH[out[0]][2] == F32
+        def emit(e):
+            if small:
+                return e.iota(ap(out), pattern, base, cm, allow_small_or_imprecise_dtypes=True)
+            return e.iota(ap(out), pattern, base, cm)
+        return add("G", 130 + 2 * n_of(out) * CY, [], [out], emit)
+
+    def keep(out, in_, pattern, op, base, cm):
+        return add("G", 170 + 2 * n_of(out) * CY, [in_], [out], lambda e: e.affine_select(ap(out), ap(in_), pattern, op, 0.0, base, cm))
+
+    dcount = [0]
+
+    def dma(q, reads, writes, pairs, cost=2000.0):
+        sem = "d_%d" % dcount[0]
+        dcount[0] += 1
+        def emit(e):
+            for o, i in pairs():
+                e.dma_start(o, i).then_inc(T.sem[sem], 16)
+            return None
+        return add(q, cost, reads, writes, emit, "d", sem, 16 * len(pairs()))
+
+    def send(r, what, dst_v, src_v, codes, latency):
+        to = T.cores[rank ^ STEP[r - 1]]
+        rid, pid = topo.addr(to)[0], topo.addr(to)[1]
+        mask, k = topo.mask(core, to), len(topo.engines(core, to))
+        sem = "r_%s%d" % (what, r)
+        def emit(e):
+            o, i = (ap(dst_v).bitcast(dt.uint8), ap(src_v).bitcast(dt.uint8)) if codes else (ap(dst_v), ap(src_v))
+            e.remote_dma(o, i, T.sem[sem], T.sem["loc"], pid, rid, mask)
+            sent[0] += k
+            return None
+        j = add("G", 150.0, [src_v], [], emit, "s")
+        add("R", latency, [], [dst_v], None, "r", sem, k, after=(j,))
+
+    sent = [0]
+    col = lambda i: V("cols", i, i + 1)
+    QC, HC, P4, Q1, SP, G0, THQ, SCQ, R4 = [col(i) for i in range(9)]
+
+    dma("S", [], [V("pgf")], lambda: [(T["pgf"][i::16, :], T.pg[:, :]) for i in range(0, 16, 2)], 2500.0)
+    dma("A", [], [V("pgf"), V("kgw")], lambda: [(T["kgw"][:, :], T.kg[:, :])] + [(T["pgf"][i::16, :], T.pg[:, :]) for i in range(1, 16, 2)], 2500.0)
+    ops[-1]["deps"] = {}
+    dma("A", [], [V("pgw")], lambda: [(T["pgw"][:, :], T.pg[:, :])])
+    dma("S", [], [V("ut")], lambda: [(T["ut"][:, :], T.u[:, :])], 2800.0)
+    dma("S", [], [V("xt", 0, 4 * CA)], lambda: [(T["xt"][:, 0:4 * CA], T.x[:, 0:4 * CA])], 3000.0)
+    dma("A", [], [V("xt", 4 * CA)], lambda: [(T["xt"][:, 4 * CA:4 * C], T.x[:, 4 * CA:4 * C])], 3000.0)
+    dma("S", [], [V("mgw")], lambda: [(T["mgw"][:, :], T.mg[:, :])])
+    dma("S", [], [V("wq")], lambda: [(T["wq"][:, :].bitcast(dt.uint8), T.wc[:, :])], 3000.0)
+    dma("S", [], [V("wqs")], lambda: [(T["wqs"][:, :], T.ws[:, :])])
+    dma("S", [], [V("vt")], lambda: [(T["vt"][:, :], T.v[:, :])])
+
+    ipv = V("ip", 0, 1)
+    iota(ipv, [[0, 1]], 0, 1)
+    iota(V("iw"), [[1, NL]], 0, 0)
+    iota(V("iu"), [[16, 8]], 0, 0)
+    ib = lambda i: V("ib", i, i + 1)
+    ts(ib(0), ipv, 15, None, A.bitwise_and)
+    ts(ib(1), ipv, 4, None, A.logical_shift_right)
+    ts(ib(2), ipv, 3, None, A.bitwise_and)
+    ts(ib(3), ipv, 12, None, A.bitwise_and)
+    ts(ib(4), ipv, 8, 3, A.bitwise_and, A.logical_shift_right)
+    copy(QC, ib(0))
+    copy(HC, ib(1))
+    ts(R4, ib(2), 4, 3, A.mult, A.add)
+    copy(col(9), ib(4))
+    ts(col(10), QC, float(NL), None, A.mult)
+    ts(V("lpos"), V("iw"), col(10), None, A.add)
+    copy(V("l0"), V("kgw"))
+    iota(V("j16"), [[1, 16]], 0, 0)
+    copy(V("lpw"), V("pgw"))
+    ts(Q1, QC, 1.0, None, A.add)
+    ts(V("t16"), V("j16"), Q1, 16383.0, A.is_equal, A.mult)
+    ts(V("n16"), V("j16"), QC, None, A.not_equal)
+    tt(V("k16"), V("n16"), V("t16"), A.add)
+    fill(V("tau"), 0.0)
+    ts(V("lq"), V("tau"), QC, None, A.add)
+    kk2 = V("kk")
+    act(kk2, V("k16"), AF.Copy, lst=V("lq"))
+    ts(col(11), QC, 15.0, 2.0 ** -14 - 1.0, A.is_lt, A.mult)
+    ts(SCQ, col(11), 1.0, None, A.add)
+    ts(V("lu1"), V("iu"), col(9), None, A.add)
+    copy(V("lu0"), V("iu"))
+    quant(V("uq"), V("uqs"), V("ut"))
+    for c, s, l in (("up", "ups", "lu1"), ("uc", "ucs", "lu0")):
+        add("V", gcost(128), [V("uq"), V(l)], [V(c)], lambda e, c=c, l=l: e.tensor_copy(ap(V(c)).bitcast(dt.uint32), ap(V("uq")).bitcast(dt.uint32).indirect(ap(V(l)))))
+        add("V", gcost(128), [V("uqs"), V(l)], [V(s)], lambda e, s=s, l=l: e.tensor_copy(ap(V(s)), ap(V("uqs")).indirect(ap(V(l)))))
+    add("V", gcost(C), [V("pgf"), V("lpos")], [V("p1")], lambda e: e.tensor_copy(ap(V("p1")), ind(V("pgf"), V("lpos"))))
+    copy(V("t0"), V("kgw"))
+
+    def powers(r):
+        before = V("t0")
+        for n in (1, 2, 3):
+            tg, tsv, ln, tf = V("tg%d" % n), V("ts%d" % n), V("l%d" % n), V("tf%d" % n)
+            if r == 1:
+                if n > 1:
+                    either(V("p%d" % n), V("p%d" % (n - 1)), V("lpw"))
+                either(tg, V("p%d" % n), V("l0"))
+            else:
+                act(tg, V("p%d" % r), AF.Copy, lst=V("l%d" % (n - 1)))
+            scan(tsv, kk2, tg)
+            ts(ln, V("ts%d" % n, 15, C, 16), SCQ, None, A.mult)
+            copy(tf, ln)
+            d = V("cs%d" % r, 3 - n, 4 * NL, 4)
+            tt(d, tf, before, A.subtract)
+            if n == 1:
+                ts(V("td"), d, G0, None, A.mult)
+                tt(V("cs%d" % r, 3, 4 * NL, 4), V("td"), before, A.add)
+            before = tf
+
+    ts(G0, ipv, 16, None, A.is_lt)
+    powers(1)
+    fill(V("ones"), 1.0)
+    keep(V("w1"), V("ones"), [[1, 520]], A.is_equal, -4, -4)
+    for b in range(4):
+        quant(V("e%d" % b), V("es%d" % b), V("w1", 4 - b, 516 - b))
+    ts(col(12), QC, 8.0, 2.0, A.is_equal, A.mult)
+    ts(col(13), QC, 0.0, None, A.is_equal)
+    tt(SP, col(12), col(13), A.add)
+    fill(V("pat"), 0.0)
+    for o, val in ((3, 1.0), (6, 1.0), (9, 1.0), (12, 1.0), (2, -1.0), (5, -1.0), (8, -1.0)):
+        fill(V("pat", o, 512, 64), val)
+    keep(V("msk"), V("pat"), [[-16, 8], [0, 64]], A.is_ge, 0, 1)
+    keep(V("msk2"), V("msk"), [[16, 8], [0, 64]], A.is_ge, 15, -1)
+    fill(V("w2", 0, 48), 0.0)
+    act(V("w2", 48, 560), V("msk2"), AF.Copy, scale=SP)
+    for c in range(4):
+        quant(V("b2%d" % c), V("b2s%d" % c), V("w2", 48 - 16 * c, 560 - 16 * c))
+    keep(V("w3a"), V("ones", 0, 512), [[-16, 32], [0, 4], [128, 4]], A.is_ge, 0, 1)
+    keep(V("w3"), V("w3a"), [[16, 32], [0, 4], [-128, 4]], A.is_ge, 15, -1)
+    quant(V("b3"), V("b3s"), V("w3"))
+    iota(V("im"), [[1, 16], [0, 4]], 0, 0)
+    ts(V("maska"), V("im"), QC, None, A.is_equal)
+    for i, val in enumerate((100.0, 3.0, 2.0, 1.0)):
+        fill(V("thr", i, 128, 4), val)
+    fill(V("d00"), 0.0)
+    fill(V("d00", 3, 16, 4), 1.0)
+    ts(V("lrep", 0, 1), ib(3), 3.0, None, A.add)
+    fill(V("im", 0, 4), 0.0)
+    ts(V("la4"), V("im", 0, 4), R4, None, A.add)
+    fill(V("at", 0, 64), 0.0)
+    fill(V("mt", 1536, 2048), 0.0)
+    quant(V("mq", 384), V("mqs", 384), V("mt", 1536, 2048))
+    ts(col(14), QC, 15.0, 2.0 ** -20 - 1.0, A.is_lt, A.mult)
+    ts(THQ, col(14), 1.0, None, A.add)
+    ts(V("t16"), V("t16"), 64.0, None, A.mult)
+    tt(V("n16"), V("t16"), V("n16"), A.add)
+    act(V("kb"), V("n16"), AF.Copy, lst=V("lq"))
+    copy(V("lm"), V("mgw"))
+    copy(V("mf"), V("mgw"))
+    ts(V("jw"), V("iw"), 16.0, QC, A.mult, A.add)
+    tt(V("mj"), V("mf"), V("jw"), A.subtract)
+    ts(V("mj"), V("mj"), THQ, None, A.mult)
+    ts(V("jw"), V("jw"), 0.25, None, A.add)
+
+    def state(r, x, rows=(("up", "ups"),)):
+        for i, (a, b) in enumerate(((0, CA), (CA, C))):
+            quant(V("qc%d" % r, a, b), V("qs%d" % r, a, b), V(x, 4 * a, 4 * b))
+            mm(V("pb%d" % i, 0, b - a), [(V(rows[0][0]), V(rows[0][1]), V("qc%d" % r, a, b), V("qs%d" % r, a, b))])
+
+    for r in (1, 2, 3):
+        x = ("xt", "x2", "x3")[r - 1]
+        qc, qs, la, lp = V("qc%d" % r), V("qs%d" % r), V("la%d" % r), V("lp%d" % r)
+        state(r, x)
+        send(r, "c", V("rc%d" % r), qc, True, 6000.0)
+        send(r, "s", V("rs%d" % r), qs, False, 4000.0)
+        act(V("bw", 0, CA), V("pb0", 0, CA), AF.Sign)
+        act(V("bw", CA, C), V("pb1", 0, C - CA), AF.Sign)
+        for n in range(4):
+            either(V("mt", n, 4 * C, 4), V("bw"), V("l%d" % n), relu=True)
+        quant(V("mq", 0, C), V("mqs", 0, C), V("mt", 0, 4 * C))
+        mm(V("pb6", 0, 128), [(V("mq", 128 * c, 128 * c + 128), V("mqs", 128 * c, 128 * c + 128), V("b2%d" % c), V("b2s%d" % c)) for c in range(4)])
+        first = len(ops) - 1
+        for k in range(7):
+            sck = V("sc", 16 * k, 16 * k + 16)
+            scan(sck, V("d0", 16 * k, 16 * k + 16) if k else V("d00"), V("pb6", 16 * k, 16 * k + 16))
+            if k < 6:
+                tt(V("d0", 16 * k + 16, 16 * k + 32), sck, V("thr", 0, 16), A.is_ge, lst=V("lrep", 0, 1))
+            tt(V("at", 64 * k + 64, 64 * k + 128), sck, V("maska"), A.mult, lst=V("la4"))
+        quant(V("aq"), V("aqs"), V("at"))
+        mm(V("pb7", 0, 128), [(V("aq"), V("aqs"), V("b3"), V("b3s"))])
+        tt(V("ph"), V("pb7", 0, 104), V("thr", 0, 104), A.is_ge)
+        scan(V("sl"), V("ph"), V("cs%d" % r))
+        copy(la, V("sl", 3, 104, 4))
+        send(r, "l", lp, la, False, 2200.0)
+        for b in range(4):
+            mm(V("pb%d" % (2 + b), 0, C), [(V("e%d" % b), V("es%d" % b), qc, qs)], after=(first,))
+            out_of_psum(V("fb%d" % b), V("pb%d" % (2 + b), 0, C))
+        mm(V("pb0", 0, C), [(V("uc"), V("ucs"), qc, qs)])
+        act(V("scw"), V("pb0", 0, C), AF.Sign)
+        for b in range(4):
+            mm(V("pb%d" % (2 + b), 0, C), [(V("e%d" % b), V("es%d" % b), V("rc%d" % r), V("rs%d" % r))])
+            out_of_psum(V("fp%d" % b), V("pb%d" % (2 + b), 0, C))
+        act(V("z"), V("scw"), AF.Relu, lst=la)
+        ts(V("zz"), V("scw"), 0.0, None, A.max, lst=la)
+        tt(V("nd"), V("z"), V("zz"), A.not_equal, lst=V("lm"))
+        scan(V("ns"), V("kb"), V("nd"), f=0.5)
+        tt(V("nm"), V("ns", 15, C, 16), V("mj"), A.mult)
+        tt(V("tau"), V("nm"), V("jw"), A.add)
+        copy(V("ltau"), V("tau"))
+        act(V("p%d" % (r + 1)) if r < 3 else V("pl_t", C, 2 * C), V("p%d" % r), AF.Copy, lst=V("ltau"))
+        if r == 3:
+            iota(V("i520"), [[1, 520]], 0, 0)
+            act(V("pl_t", 0, C), V("i520", 0, C), AF.Copy, lst=la)
+            dma("S", [V("pl_t")], [], lambda: [(T.pl[:, :], T["pl_t"][0::16, :])])
+        for a, e in ((0, CA), (CA, C)):
+            for t in range(4):
+                either(V("zt", 4 * a + t, 4 * e, 4), V("fp%d" % t), V("lp%d" % r, a // 16, e // 16))
+            quant(V("zq", a, e), V("zqs", a, e), V("zt", 4 * a, 4 * e))
+        for b in range(4):
+            bias[0] = BIAS * (3 - b)
+            for i, (a, e) in enumerate(((0, CA), (CA, C))):
+                bank = V("pb%d" % ((2, 3, 4, 5, 0, 1, 6, 7)[4 * i + b]), 0, e - a)
+                mm(bank, [(V("wq", 128 * b, 128 * b + 128), V("wqs", 128 * b, 128 * b + 128), V("zq", a, e), V("zqs", a, e))])
+                out_of_psum(V("hs%d" % b, a, e), bank, scale=0.03125)
+        nx = ("x2", "x3", "x4")[r - 1]
+        for a, e in ((0, CA), (CA, C)):
+            for b in range(4):
+                bias[0] = BIAS * (3 - b)
+                tt(V(nx, 4 * a + b, 4 * e, 4), V("hs%d" % b), V("fb%d" % b, a, e), A.add, lst=V("la%d" % r, a // 16, e // 16))
+        bias[0] = 0.0
+        if r < 3:
+            powers(r + 1)
+    quant(V("vq"), V("vqs"), V("vt"))
+    for i, (a, b) in enumerate(((0, CA), (CA, C))):
+        quant(V("qc4", a, b), V("qs4", a, b), V("x4", 4 * a, 4 * b))
+        dma("S", [V("qc4", a, b)], [], lambda a=a, b=b: [(T.oc[:, 4 * a:4 * b], T["qc4"][:, a:b].bitcast(dt.uint8))])
+        mm(V("pb%d" % i, 0, b - a), [(V("vq"), V("vqs"), V("qc4", a, b), V("qs4", a, b))])
+        out_of_psum(V("yt", a, b), V("pb%d" % i, 0, b - a))
+        dma("S", [V("yt", a, b)], [], lambda a=a, b=b: [(T.y[:, a:b], T["yt"][:, a:b])])
+    dma("S", [V("qs4")], [], lambda: [(T.osc[4 * k:4 * k + 4, :], T["qs4"][32 * k:32 * k + 4, :]) for k in range(4)])
+
+    n = len(ops)
+    users = [[] for _ in range(n)]
+    for i, o in enumerate(ops):
+        for j in o["deps"]:
+            users[j].append(i)
+    prio = [0.0] * n
+    for i in range(n - 1, -1, -1):
+        prio[i] = ops[i]["cost"] + max([prio[u] + WAKE for u in users[i]] + [0.0])
+    prio = [p + o["bias"] for p, o in zip(prio, ops)]
+    free = {k: 0.0 for k in "VAPGSR"}
+    end = [None] * n
+    left = [len(o["deps"]) for o in ops]
+    ready = [i for i in range(n) if not left[i]]
+    order = []
+    while ready:
+        best = None
+        cand = []
+        for i in ready:
+            o = ops[i]
+            at = max([end[j] + WAKE for j in o["deps"]] + [0.0])
+            if o["kind"] == "r":
+                at = end[list(o["deps"])[0]] if len(o["deps"]) == 1 else max(end[j] for j in o["deps"])
+                cand.append((at, i, "R"))
+                continue
+            for q in o["q"]:
+                cand.append((max(at, free[q]), i, q))
+        first = min(c[0] for c in cand)
+        best = max((c for c in cand if c[0] <= first + 20.0), key=lambda c: (prio[c[1]], -c[0]))
+        late = best[0] + ops[best[1]]["cost"]
+        soon = [c for c in cand if c[2] == best[2] and prio[c[1]] > prio[best[1]] and c[0] - best[0] < LOOK * (late - c[0])]
+        if soon:
+            best = max(soon, key=lambda c: (prio[c[1]], -c[0]))
+        at, i, q = best
+        o = ops[i]
+        if o["kind"] == "d":
+            free[q] = at + 60.0 * (o["amount"] // 16)
+            end[i] = free[q] + o["cost"]
+        elif o["kind"] == "r":
+            end[i] = at + o["cost"]
+        else:
+            free[q] = end[i] = at + o["cost"]
+        order.append((i, q, at))
+        ready.remove(i)
+        for u in users[i]:
+            left[u] -= 1
+            if not left[u]:
+                ready.append(u)
+
+    eng = {"V": g.vector, "A": g.scalar, "P": g.tensor, "G": g, "S": g.sync}
+    csem = {"V": "s_v", "A": "s_a", "P": "s_p", "G": "s_g"}
+    count = {k: 0 for k in csem}
+    known = {k: {} for k in "VAPGS"}
+    token, clock, qof = [None] * n, [None] * n, [None] * n
+    for i, q, at in order:
+        o = ops[i]
+        qof[i] = q
+        if o["kind"] == "r":
+            token[i], clock[i] = (o["sem"], o["amount"]), {o["sem"]: o["amount"]}
+            for j in o["deps"]:
+                for s, v in (clock[j] or {}).items():
+                    clock[i][s] = max(clock[i].get(s, 0), 0)
+            continue
+        e = eng[q]
+        need = []
+        for j, raw in o["deps"].items():
+            if token[j] is None:
+                continue
+            need.append(j)
+        need.sort(key=lambda j: -end[j])
+        for j in need:
+            s, v = token[j]
+            if known[q].get(s, 0) >= v:
+                continue
+            e.wait_ge(T.sem[s], v)
+            for s2, v2 in clock[j].items():
+                known[q][s2] = max(known[q].get(s2, 0), v2)
+        call = o["emit"](e, q) if len(o["q"]) > 1 else o["emit"](e)
+        if o["kind"] == "c":
+            count[q] += 1
+            call.then_inc(T.sem[csem[q]], 1)
+            token[i] = (csem[q], count[q])
+        elif o["kind"] == "d":
+            token[i] = (o["sem"], o["amount"])
+        if token[i]:
+            clock[i] = dict(known[q])
+            clock[i][token[i][0]] = max(clock[i].get(token[i][0], 0), token[i][1])
+    for q in csem:
+        g.wait_ge(T.sem[csem[q]], count[q])
+    for o in ops:
+        if o["kind"] in "dr":
+            g.wait_ge(T.sem[o["sem"]], o["amount"])
+    g.wait_ge(T.sem["loc"], sent[0])

@@ -2,9 +2,17 @@ from concourse.bass import DstId, RemoteDMATransfer
 from concourse.mybir import dt, AluOpType, ActivationFunctionType
 
 C = 416
-CA = 224
 NL = C // 16
+PAD = 512 - C
+MID = C // 2
+L = 14
 STEP = (1, 2, 3)
+XP = ((0, 288), (288, C))
+MP = ((0, 288), (288, C))
+ZP = ((0, 160), (160, 288), (288, C))
+FP = XP
+LENT = ()
+PAIRS = ((0, 1), (2, 3), (4, 5), (6,))
 F32, BF16, I32, U16, CODE, U8 = "float32", "bfloat16", "int32", "uint16", "float8_e4m3fn_x4", "uint8"
 
 SCRATCH, PART = {}, {}
@@ -23,62 +31,54 @@ def _parts(whole, cols, dtype, *names):
 
 _buf(512, F32, *["pb%d" % i for i in range(8)], where="psum")
 _buf(2, I32, "ip")
-_buf(12, I32, "ib")
-_buf(16, F32, "cols", "d00")
-_buf(520, F32, "i520")
-_buf(C, F32, "kk", "yt")
-_buf(16, F32, "j16", "k16", "n16", "t16")
-_buf(C, BF16, "kb", "bw", "scw", "z", "zz", "nd", "ns")
-_buf(64, F32, "im")
-_buf(64, BF16, "maska")
-_buf(128, F32, "thr")
-_buf(NL, I32, "iw", "kgw", "mgw", "pgw")
+_buf(4, I32, "ib")
+_buf(16, F32, "cols")
+_buf(8, F32, "sp0", "sp1", "sp", "ih")
+_buf(16, BF16, "pat")
+_buf(128, BF16, "wd0", "wd", "im", "maska")
+_buf(4 * NL, F32, "thr", "ph", "sl", "cs")
+_buf(NL, I32, "iq")
 _buf(8, I32, "iu")
-_buf(8, U16, "lu0", "lu1")
-_buf(4, U16, "la4")
-_buf(2, U16, "lrep")
-_buf(520, BF16, "w1", "ones")
-_buf(560, BF16, "w2")
-_buf(512, BF16, "pat", "msk", "msk2", "w3", "w3a", "ut", "vt", "at")
-_buf(NL, F32, "jw", "mf", "mj", "t0", "td", "nm", "tau")
-_buf(NL, U16, "lpos", "lm", "ltau", "lpw", "lq")
-_buf(C, I32, "pgf")
+_buf(8, U16, "lu0", "la4")
+_buf(NL, U16, "lq")
+_parts("li", NL, I32, "kgw", "pgw", "mgw")
+_parts("lu", NL, U16, "l0", "lpw", "lm")
+_parts("lists", NL, U16, "l1", "l2", "l3")
+_buf(C, BF16, "place", "kb", "bw", "scw", "z", "pa", "pc", "p2", "tb")
+_buf(C, F32, "yt", "s2", "dd", "u1", "kk")
+_buf(520, BF16, "w1")
+_buf(560, BF16, "w2", "ones")
+_buf(512, BF16, "i3", "w3", "ut", "vt", "at")
+_buf(32 * L + 4, F32, "dv")
+_buf(448, F32, "sc")
+_buf(2 * C, F32, "pl_t")
 _buf(4 * C, BF16, "xt", "x2", "x3", "x4", "zt")
 _buf(2048, BF16, "mt")
-for _c, _s, _n in (("uq", "uqs", 128), ("vq", "vqs", 128), ("wq", "wqs", 512), ("b3", "b3s", 128), ("mq", "mqs", 512), ("aq", "aqs", 128), ("zq", "zqs", C)):
+for _c, _s, _n in (("uq", "uqs", 128), ("uc", "ucs", 128), ("vq", "vqs", 128), ("wq", "wqs", 512), ("b2", "b2s", 140), ("b3", "b3s", 128), ("mq", "mqs", 512), ("aq", "aqs", 128), ("zq", "zqs", C)):
     _buf(_n, CODE, _c)
     _buf(_n, U8, _s)
-_parts("upc", 128, CODE, "up", "uc")
-_parts("upp", 128, U8, "ups", "ucs")
 _parts("ec", 128, CODE, *["e%d" % i for i in range(4)])
 _parts("ep", 128, U8, *["es%d" % i for i in range(4)])
-_parts("bc", 128, CODE, *["b2%d" % i for i in range(4)])
-_parts("bp", 128, U8, *["b2s%d" % i for i in range(4)])
 _parts("hs", C, F32, *["hs%d" % i for i in range(4)])
 _parts("fb", C, BF16, *["fb%d" % i for i in range(4)])
 _parts("fp", C, BF16, *["fp%d" % i for i in range(4)])
-_parts("tg", C, F32, "tg1", "tg2", "tg3")
-_parts("tsum", C, F32, "ts1", "ts2", "ts3")
-_parts("tf", NL, F32, "tf1", "tf2", "tf3")
-_parts("lists", NL, U16, "l0", "l1", "l2", "l3")
-_buf(112, F32, "sc", "d0")
-_buf(4 * NL, F32, "ph", "sl", "cs1", "cs2", "cs3")
-_buf(2 * C, F32, "pl_t")
+_parts("tg", C, BF16, "tg1", "tg2", "tg3")
+_parts("tsum", C, BF16, "ts1", "ts2", "ts3")
 for _i in (1, 2, 3, 4):
     _buf(C, CODE, "qc%d" % _i)
     _buf(C, U8, "qs%d" % _i)
 for _i in (1, 2, 3):
-    _buf(C, F32, "p%d" % _i)
     _buf(C, CODE, "rc%d" % _i)
     _buf(C, U8, "rs%d" % _i)
     _buf(NL, U16, "la%d" % _i, "lp%d" % _i)
 
-SEMAPHORES = ["s_v", "s_a", "s_p", "s_g", "loc"] + ["d_%d" % i for i in range(40)] + ["r_%s%d" % (k, i) for k in "csl" for i in (1, 2, 3)]
+SEMAPHORES = ["s_v", "s_a", "s_p", "s_g", "loc"] + ["d_%d" % i for i in range(40)] + ["r_%d" % i for i in range(20)]
 
 WAKE = 100.0
-LOOK = 0.0
-BIAS = 300.0
-CY = 0.83
+CY = 1.04
+GY = 1.62
+PY = 1.25
+TUNE = {"bias": 0.0, "spare": 0.3, "turns": 6}
 
 
 def _hit(a, b):
@@ -102,338 +102,323 @@ def rank_program(g, core, T, topo):
         return (whole, at + lo, at + (cols if hi is None else hi), st)
 
     def ap(v):
+        if not isinstance(v, tuple):
+            return v
         return T[v[0]][:, v[1]:v[2]] if v[3] == 1 else T[v[0]][:, v[1]:v[2]:v[3]]
 
-    def ind(v, l):
-        return ap(v).indirect(ap(l))
+    def src(v, l):
+        return ap(v) if l is None else ap(v).indirect(ap(l))
 
     def n_of(v):
         return -(-(v[2] - v[1]) // v[3])
 
-    def add(q, cost, reads, writes, emit, kind="c", sem=None, amount=0, after=()):
+    def add(cost, reads, writes, emit, kind="c", sem=None, amount=0, after=(), behind=()):
         i = len(ops)
         deps = {}
         for mode, views in ((0, reads), (1, writes)):
             for v in views:
-                if v is None:
+                if not isinstance(v, tuple):
                     continue
                 psum = v[0].startswith("pb")
                 for (j, m, w) in seen.setdefault(v[0], []):
-                    if j == i:
-                        continue
-                    same = ops[j]["q"] == q and len(q) == 1
-                    if psum:
-                        if same and not (m or mode):
-                            continue
-                    elif not (m or mode) or not _hit(v, w):
-                        continue
-                    raw = m == 1 and mode == 0
-                    deps[j] = deps.get(j, False) or raw
+                    if j != i and (m or mode) and (psum or _hit(v, w)):
+                        deps[j] = True
+                    elif j != i and psum:
+                        deps.setdefault(j, "read")
                 seen[v[0]].append((i, mode, v))
         for j in after:
             deps[j] = True
-        ops.append({"q": q, "cost": cost, "deps": deps, "emit": emit, "kind": kind, "sem": sem, "amount": amount, "bias": bias[0]})
+        for j in behind:
+            deps[j] = False
+        ops.append({"cost": cost, "deps": deps, "emit": emit, "kind": kind, "sem": sem, "amount": amount, "bias": bias[0]})
         return i
 
-    def vcost(n, f=1.0):
-        return max(64.0, n * f) * CY
+    def narrow(*views):
+        return all(SCRATCH[v[0]][2] in (BF16, U16) for v in views if isinstance(v, tuple))
 
-    def gcost(n):
-        return 50 + 1.3 * n * CY
+    def costs(qs, out, ins, lst, both=False):
+        n = n_of(out)
+        if lst is not None:
+            c = {"V": 62 + n * GY, "A": 81 + n * GY}
+        else:
+            c = {"V": max(64.0, n * (2.0 if both else 0.5 if narrow(out, *ins) else 1.0)) * CY, "A": max(64.0, n) * CY}
+        return {q: c[q] for q in qs}
 
-    def ts(out, in0, s1, s2, op0, op1=None, q="V", f=1.0, lst=None):
-        rd = [in0, lst] + [s for s in (s1, s2) if isinstance(s, tuple)]
-        def emit(e):
-            a1 = ap(s1) if isinstance(s1, tuple) else s1
-            a2 = ap(s2) if isinstance(s2, tuple) else s2
-            src = ap(in0) if lst is None else ind(in0, lst)
+    def ts(out, in0, s1, s2, op0, op1=None, lst=None, behind=()):
+        def emit(e, q):
             if op1 is None:
-                return e.tensor_scalar(ap(out), src, a1, None, op0)
-            return e.tensor_scalar(ap(out), src, a1, a2, op0, op1)
-        return add(q, vcost(n_of(out), f) if lst is None else gcost(n_of(out)), rd, [out], emit)
+                return e.tensor_scalar(ap(out), src(in0, lst), ap(s1), None, op0)
+            return e.tensor_scalar(ap(out), src(in0, lst), ap(s1), ap(s2), op0, op1)
+        return add(costs("V", out, (in0, s1, s2), lst), [in0, lst, s1, s2], [out], emit, behind=behind)
 
-    def tt(out, in0, in1, op, lst=None, f=1.0):
-        def emit(e):
-            return e.tensor_tensor(ap(out), ap(in0) if lst is None else ind(in0, lst), ap(in1), op)
-        return add("V", vcost(n_of(out), f) if lst is None else gcost(n_of(out)), [in0, in1, lst], [out], emit)
+    def tt(out, in0, in1, op, lst=None):
+        both = not (in0[0].startswith("pb") or in1[0].startswith("pb"))
+        return add(costs("V", out, (in0, in1, V("cols")), lst, both), [in0, in1, lst], [out], lambda e, q: e.tensor_tensor(ap(out), src(in0, lst), ap(in1), op))
 
-    def copy(out, in_):
-        return add("V", vcost(n_of(out)), [in_], [out], lambda e: e.tensor_copy(ap(out), ap(in_)))
+    def scan(out, d0, d1):
+        return add(costs("V", out, (d0, d1), None), [d0, d1], [out], lambda e, q: e.tensor_tensor_scan(ap(out), ap(d0), ap(d1), 0.0, A.mult, A.add))
 
-    def fill(out, val):
-        return add("V", vcost(n_of(out), 0.5), [], [out], lambda e: e.memset(ap(out), val))
-
-    def scan(out, d0, d1, f=1.0):
-        return add("V", vcost(n_of(out), f), [d0, d1], [out], lambda e: e.tensor_tensor_scan(ap(out), ap(d0), ap(d1), 0.0, A.mult, A.add))
-
-    def act(out, in_, func, lst=None, scale=None):
-        def emit(e):
-            src = ap(in_) if lst is None else ind(in_, lst)
-            if scale is None:
-                return e.activation(ap(out), src, func)
-            return e.activation(ap(out), src, func, scale=ap(scale))
-        return add("A", vcost(n_of(out)) if lst is None else 15 + gcost(n_of(out)), [in_, lst, scale], [out], emit)
-
-    def either(out, in_, lst, relu=False):
-        def emit(e, eng):
-            if eng == "V":
+    def move(out, in_, lst=None, scale=None, plus=None, relu=False, qs="VA"):
+        def emit(e, q):
+            o, i = ap(out), src(in_, lst)
+            if q == "V":
                 if relu:
-                    return e.tensor_scalar(ap(out), ind(in_, lst), 0.0, None, A.max)
-                return e.tensor_copy(ap(out), ind(in_, lst))
-            return e.activation(ap(out), ind(in_, lst), AF.Relu if relu else AF.Copy)
-        return add("VA", gcost(n_of(out)), [in_, lst], [out], emit)
-
-    def out_of_psum(out, in_, scale=None, q="A"):
-        def emit(e, eng=None):
-            if eng == "V" or q == "V":
+                    return e.tensor_scalar(o, i, 0.0, None, A.max)
+                if scale is None and plus is None:
+                    return e.tensor_copy(o, i)
+                if plus is None:
+                    return e.tensor_scalar(o, i, ap(scale), None, A.mult)
                 if scale is None:
-                    return e.tensor_copy(ap(out), ap(in_))
-                return e.tensor_scalar(ap(out), ap(in_), scale, None, A.mult)
-            if scale is None:
-                return e.activation(ap(out), ap(in_), AF.Copy)
-            return e.activation(ap(out), ap(in_), AF.Copy, scale=scale)
-        return add(q, vcost(n_of(out)), [in_], [out], emit)
+                    return e.tensor_scalar(o, i, ap(plus), None, A.add)
+                return e.tensor_scalar(o, i, ap(scale), ap(plus), A.mult, A.add)
+            if plus is not None:
+                return e.activation(o, i, AF.Identity, bias=ap(plus), scale=1.0 if scale is None else ap(scale))
+            if scale is not None:
+                return e.activation(o, i, AF.Copy, scale=ap(scale))
+            return e.activation(o, i, AF.Relu if relu else AF.Copy)
+        return add(costs(qs, out, (in_, scale, plus), lst), [in_, lst, scale, plus], [out], emit)
+
+    def signs(out, in_, less=None):
+        def emit(e, q):
+            if q == "V":
+                return e.tensor_scalar(ap(out), ap(in_), 0.0, None, A.is_gt)
+            if less is None:
+                return e.activation(ap(out), ap(in_), AF.Sign)
+            return e.activation(ap(out), ap(in_), AF.Sign, bias=ap(less))
+        return add(costs("VA" if less is None else "A", out, (in_,), None), [in_, less], [out], emit)
+
+    def fill(out, val, qs="VA"):
+        ones = V("ones", 0, n_of(out))
+        def emit(e, q):
+            if q == "V":
+                return e.memset(ap(out), val)
+            return e.activation(ap(out), ap(ones), AF.Copy, scale=val)
+        return add(costs(qs, out, (), None), [ones] if "A" in qs else [], [out], emit)
 
     def quant(c, s, t):
-        return add("V", 12 + 0.22 * n_of(t), [t], [c, s], lambda e: e.quantize_mx(ap(c), ap(s), ap(t)))
+        return add({"V": 15 + 0.275 * n_of(t)}, [t], [c, s], lambda e, q: e.quantize_mx(ap(c), ap(s), ap(t)))
 
-    def mm(out, terms, after=()):
-        def emit(e):
+    def mm(out, terms, after=(), start=True, stop=True, behind=()):
+        def emit(e, q):
             last = None
             for k, (a, b, c, d) in enumerate(terms):
-                last = e.matmul_mx(ap(out), ap(a), ap(b), ap(c), ap(d), k == 0, k == len(terms) - 1)
+                last = e.matmul_mx(ap(out), ap(a), ap(b), ap(c), ap(d), start and k == 0, stop and k == len(terms) - 1)
             return last
-        return add("P", (n_of(out) + 16) * CY * 1.3 * len(terms), [v for t in terms for v in t], [out], emit, after=after)
+        return add({"P": (n_of(out) + 16) * PY * len(terms)}, [v for t in terms for v in t], [out], emit, after=after, behind=behind)
 
     def iota(out, pattern, base, cm):
-        small = SCRATCH[out[0]][2] == F32
-        def emit(e):
-            if small:
+        def emit(e, q):
+            if SCRATCH[out[0]][2] != I32:
                 return e.iota(ap(out), pattern, base, cm, allow_small_or_imprecise_dtypes=True)
             return e.iota(ap(out), pattern, base, cm)
-        return add("G", 130 + 2 * n_of(out) * CY, [], [out], emit)
+        return add({"G": 160 + 2 * n_of(out) * CY}, [], [out], emit)
 
-    def keep(out, in_, pattern, op, base, cm):
-        return add("G", 170 + 2 * n_of(out) * CY, [in_], [out], lambda e: e.affine_select(ap(out), ap(in_), pattern, op, 0.0, base, cm))
+    def keep(out, in_, pattern, op, base, cm, other=0.0):
+        return add({"G": 210 + 2 * n_of(out) * CY}, [in_], [out], lambda e, q: e.affine_select(ap(out), ap(in_), pattern, op, other, base, cm))
 
-    dcount = [0]
+    dcount, rcount, sent = [0], [0], [0]
 
-    def dma(q, reads, writes, pairs, cost=2000.0):
+    def dma(q, reads, writes, pairs, cost=2000.0, behind=()):
         sem = "d_%d" % dcount[0]
         dcount[0] += 1
-        def emit(e):
+        def emit(e, q):
             for o, i in pairs():
                 e.dma_start(o, i).then_inc(T.sem[sem], 16)
-            return None
-        return add(q, cost, reads, writes, emit, "d", sem, 16 * len(pairs()))
+        i = add({q: 60.0 * len(pairs())}, reads, writes, emit, "d", sem, 16 * len(pairs()), behind=behind)
+        ops[i]["late"] = cost
+        return i
 
-    def send(r, what, dst_v, src_v, codes, latency):
+    def send(r, dst_v, src_v, codes, latency, behind=()):
         to = T.cores[rank ^ STEP[r - 1]]
         rid, pid = topo.addr(to)[0], topo.addr(to)[1]
         mask, k = topo.mask(core, to), len(topo.engines(core, to))
-        sem = "r_%s%d" % (what, r)
-        def emit(e):
+        sem = "r_%d" % rcount[0]
+        def emit(e, q):
             o, i = (ap(dst_v).bitcast(dt.uint8), ap(src_v).bitcast(dt.uint8)) if codes else (ap(dst_v), ap(src_v))
             e.remote_dma(o, i, T.sem[sem], T.sem["loc"], pid, rid, mask)
             sent[0] += k
-            return None
-        j = add("G", 150.0, [src_v], [], emit, "s")
-        add("R", latency, [], [dst_v], None, "r", sem, k, after=(j,))
+        j = add({"G": 150.0 if rcount[0] else 1650.0}, [src_v], [], emit, "s", behind=behind)
+        rcount[0] += 1
+        add({"R": latency}, [], [dst_v], None, "r", sem, k, after=(j,))
+        return j
 
-    sent = [0]
     col = lambda i: V("cols", i, i + 1)
-    QC, HC, P4, Q1, SP, G0, THQ, SCQ, R4 = [col(i) for i in range(9)]
+    QC, HC, SC, ISC, R4, LESS, CMID = [col(i) for i in range(7)]
 
-    dma("S", [], [V("pgf")], lambda: [(T["pgf"][i::16, :], T.pg[:, :]) for i in range(0, 16, 2)], 2500.0)
-    dma("A", [], [V("pgf"), V("kgw")], lambda: [(T["kgw"][:, :], T.kg[:, :])] + [(T["pgf"][i::16, :], T.pg[:, :]) for i in range(1, 16, 2)], 2500.0)
-    ops[-1]["deps"] = {}
-    dma("A", [], [V("pgw")], lambda: [(T["pgw"][:, :], T.pg[:, :])])
-    dma("S", [], [V("ut")], lambda: [(T["ut"][:, :], T.u[:, :])], 2800.0)
-    dma("S", [], [V("xt", 0, 4 * CA)], lambda: [(T["xt"][:, 0:4 * CA], T.x[:, 0:4 * CA])], 3000.0)
-    dma("A", [], [V("xt", 4 * CA)], lambda: [(T["xt"][:, 4 * CA:4 * C], T.x[:, 4 * CA:4 * C])], 3000.0)
-    dma("S", [], [V("mgw")], lambda: [(T["mgw"][:, :], T.mg[:, :])])
-    dma("S", [], [V("wq")], lambda: [(T["wq"][:, :].bitcast(dt.uint8), T.wc[:, :])], 3000.0)
-    dma("S", [], [V("wqs")], lambda: [(T["wqs"][:, :], T.ws[:, :])])
-    dma("S", [], [V("vt")], lambda: [(T["vt"][:, :], T.v[:, :])])
+    a, b = XP[0][1], C
+    d0 = dma("S", [], [V("pgw")], lambda: [(ap(V("pgw")), T.pg[:, :])])
+    d1 = dma("A", [], [V("kgw")], lambda: [(ap(V("kgw")), T.kg[:, :])])
+    d1 = dma("A", [], [V("ut")], lambda: [(T["ut"][:, :], T.u[:, :])], 2700.0, (d1,))
+    d0 = dma("S", [], [V("xt", 0, 4 * a)], lambda: [(T["xt"][:, 0:4 * a], T.x[:, 0:4 * a])], 3400.0, (d0,))
+    d1 = dma("A", [], [V("xt", 4 * a)], lambda: [(T["xt"][:, 4 * a:4 * b], T.x[:, 4 * a:4 * b])], 3900.0, (d1,))
+    d0 = dma("S", [], [V("mgw")], lambda: [(ap(V("mgw")), T.mg[:, :])], 4000.0, (d0,))
+    d0 = dma("S", [], [V("wq")], lambda: [(T["wq"][:, :].bitcast(dt.uint8), T.wc[:, :])], 5300.0, (d0,))
+    d0 = dma("S", [], [V("wqs")], lambda: [(T["wqs"][:, :], T.ws[:, :])], 5600.0, (d0,))
+    d0 = dma("S", [], [V("vt")], lambda: [(T["vt"][:, :], T.v[:, :])], 6200.0, (d0,))
 
     ipv = V("ip", 0, 1)
-    iota(ipv, [[0, 1]], 0, 1)
-    iota(V("iw"), [[1, NL]], 0, 0)
-    iota(V("iu"), [[16, 8]], 0, 0)
     ib = lambda i: V("ib", i, i + 1)
+    fill(V("ones"), 1.0, "V")
+    iota(V("place"), [[1, C]], -MID, 0)
+    iota(ipv, [[0, 1]], 0, 1)
     ts(ib(0), ipv, 15, None, A.bitwise_and)
     ts(ib(1), ipv, 4, None, A.logical_shift_right)
     ts(ib(2), ipv, 3, None, A.bitwise_and)
-    ts(ib(3), ipv, 12, None, A.bitwise_and)
-    ts(ib(4), ipv, 8, 3, A.bitwise_and, A.logical_shift_right)
-    copy(QC, ib(0))
-    copy(HC, ib(1))
-    ts(R4, ib(2), 4, 3, A.mult, A.add)
-    copy(col(9), ib(4))
-    ts(col(10), QC, float(NL), None, A.mult)
-    ts(V("lpos"), V("iw"), col(10), None, A.add)
-    copy(V("l0"), V("kgw"))
-    iota(V("j16"), [[1, 16]], 0, 0)
-    copy(V("lpw"), V("pgw"))
-    ts(Q1, QC, 1.0, None, A.add)
-    ts(V("t16"), V("j16"), Q1, 16383.0, A.is_equal, A.mult)
-    ts(V("n16"), V("j16"), QC, None, A.not_equal)
-    tt(V("k16"), V("n16"), V("t16"), A.add)
-    fill(V("tau"), 0.0)
-    ts(V("lq"), V("tau"), QC, None, A.add)
-    kk2 = V("kk")
-    act(kk2, V("k16"), AF.Copy, lst=V("lq"))
-    ts(col(11), QC, 15.0, 2.0 ** -14 - 1.0, A.is_lt, A.mult)
-    ts(SCQ, col(11), 1.0, None, A.add)
-    ts(V("lu1"), V("iu"), col(9), None, A.add)
-    copy(V("lu0"), V("iu"))
+    move(QC, ib(0), qs="V")
+    move(HC, ib(1), qs="V")
+    ts(R4, ib(2), float(L), 5.0, A.mult, A.add)
+    fill(LESS, -2.0 ** -100, "V")
+    fill(CMID, float(MID), "V")
+    iota(V("iq"), [[0, NL]], 0, 1)
+    move(V("lq"), V("iq"), qs="V")
+    keep(V("wd0"), V("ones", 0, 128), [[1, 128]], A.not_equal, 0, -1)
+    keep(V("wd"), V("wd0"), [[1, 128]], A.not_equal, -1, -1, 2.0 ** 20)
+    move(V("kb"), V("wd"), lst=V("lq"))
+    ts(col(8), QC, 15.0, 2.0 ** -21 - 0.5, A.is_lt, A.mult)
+    ts(SC, col(8), 0.5, None, A.add)
+    ts(col(9), QC, 15.0, 2.0 ** 21 - 2.0, A.is_lt, A.mult)
+    ts(ISC, col(9), 2.0, None, A.add)
+    move(V("lu", 0, 2 * NL), V("li", 0, 2 * NL), qs="V")
+    move(V("lm"), V("mgw"), qs="V")
+    ts(V("cs", 3, 4 * NL, 4), V("kgw"), -float(MID), ISC, A.add, A.mult)
+
+    def listed(n):
+        scan(V("ts%d" % n), V("kb"), V("tg%d" % n))
+        now = V("ts%d" % n, 15, C, 16)
+        ts(V("l%d" % n), now, SC, MID + 0.25, A.mult, A.add)
+        tt(V("cs", 3 - n, 4 * NL, 4), now, V("ts%d" % (n - 1), 15, C, 16) if n > 1 else V("cs", 3, 4 * NL, 4), A.subtract)
+
+    for lo, hi in ((0, 224), (224, C)):
+        move(V("pa", lo, hi), V("place"), lst=V("lpw", lo // 16, hi // 16))
+    move(V("tg1"), V("pa"), lst=V("l0"), scale=2.0)
+    move(V("p2"), V("pa"), lst=V("lpw"))
+    listed(1)
+    move(V("tg2"), V("p2"), lst=V("l0"), scale=2.0)
+    listed(2)
+    move(V("tg3"), V("p2"), lst=V("l1"), scale=2.0)
+    listed(3)
+    move(V("pc"), V("pa"))
+    tt(V("s2"), V("pa"), V("pc"), A.add, lst=V("lm"))
+    tt(V("dd"), V("pa"), V("pc"), A.subtract, lst=V("lm"))
     quant(V("uq"), V("uqs"), V("ut"))
-    for c, s, l in (("up", "ups", "lu1"), ("uc", "ucs", "lu0")):
-        add("V", gcost(128), [V("uq"), V(l)], [V(c)], lambda e, c=c, l=l: e.tensor_copy(ap(V(c)).bitcast(dt.uint32), ap(V("uq")).bitcast(dt.uint32).indirect(ap(V(l)))))
-        add("V", gcost(128), [V("uqs"), V(l)], [V(s)], lambda e, s=s, l=l: e.tensor_copy(ap(V(s)), ap(V("uqs")).indirect(ap(V(l)))))
-    add("V", gcost(C), [V("pgf"), V("lpos")], [V("p1")], lambda e: e.tensor_copy(ap(V("p1")), ind(V("pgf"), V("lpos"))))
-    copy(V("t0"), V("kgw"))
-
-    def powers(r):
-        before = V("t0")
-        for n in (1, 2, 3):
-            tg, tsv, ln, tf = V("tg%d" % n), V("ts%d" % n), V("l%d" % n), V("tf%d" % n)
-            if r == 1:
-                if n > 1:
-                    either(V("p%d" % n), V("p%d" % (n - 1)), V("lpw"))
-                either(tg, V("p%d" % n), V("l0"))
-            else:
-                act(tg, V("p%d" % r), AF.Copy, lst=V("l%d" % (n - 1)))
-            scan(tsv, kk2, tg)
-            ts(ln, V("ts%d" % n, 15, C, 16), SCQ, None, A.mult)
-            copy(tf, ln)
-            d = V("cs%d" % r, 3 - n, 4 * NL, 4)
-            tt(d, tf, before, A.subtract)
-            if n == 1:
-                ts(V("td"), d, G0, None, A.mult)
-                tt(V("cs%d" % r, 3, 4 * NL, 4), V("td"), before, A.add)
-            before = tf
-
-    ts(G0, ipv, 16, None, A.is_lt)
-    powers(1)
-    fill(V("ones"), 1.0)
-    keep(V("w1"), V("ones"), [[1, 520]], A.is_equal, -4, -4)
+    iota(V("iu"), [[16, 8]], 0, 0)
+    move(V("lu0"), V("iu"), qs="V")
+    add(costs("V", V("uc"), (), V("lu0")), [V("uq"), V("lu0")], [V("uc")], lambda e, q: e.tensor_copy(ap(V("uc")).bitcast(dt.uint32), ap(V("uq")).bitcast(dt.uint32).indirect(ap(V("lu0")))))
+    add(costs("VA", V("ucs"), (), V("lu0")), [V("uqs"), V("lu0")], [V("ucs")],
+        lambda e, q: e.tensor_copy(ap(V("ucs")), src(V("uqs"), V("lu0"))) if q == "V" else e.activation(ap(V("ucs")), src(V("uqs"), V("lu0")), AF.Copy))
+    keep(V("w1"), V("ones", 0, 520), [[1, 520]], A.is_equal, -4, -4)
     for b in range(4):
         quant(V("e%d" % b), V("es%d" % b), V("w1", 4 - b, 516 - b))
-    ts(col(12), QC, 8.0, 2.0, A.is_equal, A.mult)
-    ts(col(13), QC, 0.0, None, A.is_equal)
-    tt(SP, col(12), col(13), A.add)
+    iota(V("sp0"), [[-16, 8]], 1, 1)
+    keep(V("sp1"), V("sp0"), [[-16, 8]], A.is_ge, 0, 1)
+    keep(V("sp"), V("sp1"), [[16, 8]], A.is_ge, 1, -1)
     fill(V("pat"), 0.0)
-    for o, val in ((3, 1.0), (6, 1.0), (9, 1.0), (12, 1.0), (2, -1.0), (5, -1.0), (8, -1.0)):
-        fill(V("pat", o, 512, 64), val)
-    keep(V("msk"), V("pat"), [[-16, 8], [0, 64]], A.is_ge, 0, 1)
-    keep(V("msk2"), V("msk"), [[16, 8], [0, 64]], A.is_ge, 15, -1)
-    fill(V("w2", 0, 48), 0.0)
-    act(V("w2", 48, 560), V("msk2"), AF.Copy, scale=SP)
-    for c in range(4):
-        quant(V("b2%d" % c), V("b2s%d" % c), V("w2", 48 - 16 * c, 560 - 16 * c))
-    keep(V("w3a"), V("ones", 0, 512), [[-16, 32], [0, 4], [128, 4]], A.is_ge, 0, 1)
-    keep(V("w3"), V("w3a"), [[16, 32], [0, 4], [-128, 4]], A.is_ge, 15, -1)
+    for lo, hi, st, val in ((0, 10, 9, -1.0), (1, 2, 1, 3.0), (2, 3, 1, -3.0), (3, 5, 1, 1.0), (5, 6, 1, -2.0), (6, 15, 4, 1.0)):
+        fill(V("pat", lo, hi, st), val)
+    fill(V("w2"), 0.0)
+    for k in range(7):
+        move(V("w2", 48 + 64 * k, 64 + 64 * k), V("pat"), scale=V("sp", k, k + 1))
+    quant(V("b2"), V("b2s"), V("w2"))
+    iota(V("i3"), [[1, 32], [0, 4], [-8, 4]], PAD // 16, 0)
+    ts(V("w3"), V("i3"), HC, None, A.is_equal)
     quant(V("b3"), V("b3s"), V("w3"))
-    iota(V("im"), [[1, 16], [0, 4]], 0, 0)
+    iota(V("im"), [[0, 2], [1, 16], [0, 4]], 0, 0)
     ts(V("maska"), V("im"), QC, None, A.is_equal)
-    for i, val in enumerate((100.0, 3.0, 2.0, 1.0)):
-        fill(V("thr", i, 128, 4), val)
-    fill(V("d00"), 0.0)
-    fill(V("d00", 3, 16, 4), 1.0)
-    ts(V("lrep", 0, 1), ib(3), 3.0, None, A.add)
-    fill(V("im", 0, 4), 0.0)
-    ts(V("la4"), V("im", 0, 4), R4, None, A.add)
+    iota(V("thr"), [[0, NL], [-1, 4]], 3, 0)
+    iota(V("ih"), [[64, 2], [0, 4]], 0, 0)
+    ts(V("la4"), V("ih"), R4, None, A.add)
+    fill(V("dv"), 0.0)
+    for lo, hi, val in ((5, 28 * L, -1.0), (6, 32 * L, -1.0), (7, 32 * L, 1.0 / 3.0), (8, 32 * L, 1.0), (9, 32 * L, 1.0), (28 * L + 4, 32 * L, 1.0)):
+        fill(V("dv", lo, hi, L), val, "V" if val == 1.0 / 3.0 else "VA")
+    fill(V("sc"), 0.0)
     fill(V("at", 0, 64), 0.0)
-    fill(V("mt", 1536, 2048), 0.0)
-    quant(V("mq", 384), V("mqs", 384), V("mt", 1536, 2048))
-    ts(col(14), QC, 15.0, 2.0 ** -20 - 1.0, A.is_lt, A.mult)
-    ts(THQ, col(14), 1.0, None, A.add)
-    ts(V("t16"), V("t16"), 64.0, None, A.mult)
-    tt(V("n16"), V("t16"), V("n16"), A.add)
-    act(V("kb"), V("n16"), AF.Copy, lst=V("lq"))
-    copy(V("lm"), V("mgw"))
-    copy(V("mf"), V("mgw"))
-    ts(V("jw"), V("iw"), 16.0, QC, A.mult, A.add)
-    tt(V("mj"), V("mf"), V("jw"), A.subtract)
-    ts(V("mj"), V("mj"), THQ, None, A.mult)
-    ts(V("jw"), V("jw"), 0.25, None, A.add)
+    fill(V("mt", 0, 512), 0.0)
+    quant(V("mq", 0, 128), V("mqs", 0, 128), V("mt", 0, 512))
 
-    def state(r, x, rows=(("up", "ups"),)):
-        for i, (a, b) in enumerate(((0, CA), (CA, C))):
-            quant(V("qc%d" % r, a, b), V("qs%d" % r, a, b), V(x, 4 * a, 4 * b))
-            mm(V("pb%d" % i, 0, b - a), [(V(rows[0][0]), V(rows[0][1]), V("qc%d" % r, a, b), V("qs%d" % r, a, b))])
+    def unpack(to, c, s, pieces, banks, skip=(), after=()):
+        k = 0
+        for lo, hi in pieces:
+            for b in range(4):
+                bank = V("pb%d" % (5 if b in skip else banks[k % len(banks)]), 0, hi - lo)
+                mm(bank, [(V("e%d" % b), V("es%d" % b), V(c, lo, hi), V(s, lo, hi))], after=after)
+                if b not in skip:
+                    move(V("%s%d" % (to, b), lo, hi), bank)
+                    k += 1
 
     for r in (1, 2, 3):
-        x = ("xt", "x2", "x3")[r - 1]
-        qc, qs, la, lp = V("qc%d" % r), V("qs%d" % r), V("la%d" % r), V("lp%d" % r)
-        state(r, x)
-        send(r, "c", V("rc%d" % r), qc, True, 6000.0)
-        send(r, "s", V("rs%d" % r), qs, False, 4000.0)
-        act(V("bw", 0, CA), V("pb0", 0, CA), AF.Sign)
-        act(V("bw", CA, C), V("pb1", 0, C - CA), AF.Sign)
-        for n in range(4):
-            either(V("mt", n, 4 * C, 4), V("bw"), V("l%d" % n), relu=True)
-        quant(V("mq", 0, C), V("mqs", 0, C), V("mt", 0, 4 * C))
-        mm(V("pb6", 0, 128), [(V("mq", 128 * c, 128 * c + 128), V("mqs", 128 * c, 128 * c + 128), V("b2%d" % c), V("b2s%d" % c)) for c in range(4)])
-        first = len(ops) - 1
-        for k in range(7):
-            sck = V("sc", 16 * k, 16 * k + 16)
-            scan(sck, V("d0", 16 * k, 16 * k + 16) if k else V("d00"), V("pb6", 16 * k, 16 * k + 16))
-            if k < 6:
-                tt(V("d0", 16 * k + 16, 16 * k + 32), sck, V("thr", 0, 16), A.is_ge, lst=V("lrep", 0, 1))
-            tt(V("at", 64 * k + 64, 64 * k + 128), sck, V("maska"), A.mult, lst=V("la4"))
+        x, qc, qs, la = ("xt", "x2", "x3")[r - 1], "qc%d" % r, "qs%d" % r, "la%d" % r
+        for i, (lo, hi) in enumerate(XP):
+            quant(V(qc, lo, hi), V(qs, lo, hi), V(x, 4 * lo, 4 * hi))
+            mm(V("pb%d" % i, 0, hi - lo), [(V("uq"), V("uqs"), V(qc, lo, hi), V(qs, lo, hi))])
+            signs(V("bw", lo, hi), V("pb%d" % i, 0, hi - lo))
+        j = send(r, V("rc%d" % r, *XP[0]), V(qc, *XP[0]), True, 4000.0)
+        j = send(r, V("rs%d" % r), V(qs), False, 4300.0, (j,))
+        j = send(r, V("rc%d" % r, *XP[1]), V(qc, *XP[1]), True, 4900.0, (j,))
+        done = None
+        for lo, hi in MP:
+            for n in range(4):
+                move(V("mt", 4 * (PAD + lo) + n, 4 * (PAD + hi), 4), V("bw"), lst=V("l%d" % n, lo // 16, hi // 16), relu=True)
+            quant(V("mq", PAD + lo, PAD + hi), V("mqs", PAD + lo, PAD + hi), V("mt", 4 * (PAD + lo), 4 * (PAD + hi)))
+            blocks = range((PAD + lo) // 128 if lo else 0, (PAD + hi) // 128)
+            done = mm(V("pb6", 0, 128), [(V("mq", 128 * c, 128 * c + 128), V("mqs", 128 * c, 128 * c + 128), V("b2", 12 - 4 * c, 140 - 4 * c), V("b2s", 12 - 4 * c, 140 - 4 * c)) for c in blocks],
+                      start=lo == 0, stop=hi == C, behind=() if done is None else (done,))
+        for s, val in enumerate((0.5, 1.5, 3.0, 3.0)):
+            ts(V("dv", s, 28 * L, L), V("pb6", s, 112, 4), val, None, A.mult)
+        for pair in PAIRS:
+            for k in pair:
+                scan(V("sc", 64 * k, 64 * k + 4 * L), V("sc", 64 * k - 61, 64 * k - 61 + 4 * L) if k else V("dv", 28 * L + 3, 32 * L + 3), V("dv", 4 * L * k, 4 * L * k + 4 * L))
+            k, n = pair[0], len(pair)
+            tt(V("at", 64 * k + 64, 64 * (k + n) + 64), V("sc", 64 * k, 64 * (k + n)), V("maska", 0, 64 * n), A.mult, lst=V("la4", 0, 4 * n))
         quant(V("aq"), V("aqs"), V("at"))
         mm(V("pb7", 0, 128), [(V("aq"), V("aqs"), V("b3"), V("b3s"))])
-        tt(V("ph"), V("pb7", 0, 104), V("thr", 0, 104), A.is_ge)
-        scan(V("sl"), V("ph"), V("cs%d" % r))
-        copy(la, V("sl", 3, 104, 4))
-        send(r, "l", lp, la, False, 2200.0)
-        for b in range(4):
-            mm(V("pb%d" % (2 + b), 0, C), [(V("e%d" % b), V("es%d" % b), qc, qs)], after=(first,))
-            out_of_psum(V("fb%d" % b), V("pb%d" % (2 + b), 0, C))
-        mm(V("pb0", 0, C), [(V("uc"), V("ucs"), qc, qs)])
-        act(V("scw"), V("pb0", 0, C), AF.Sign)
-        for b in range(4):
-            mm(V("pb%d" % (2 + b), 0, C), [(V("e%d" % b), V("es%d" % b), V("rc%d" % r), V("rs%d" % r))])
-            out_of_psum(V("fp%d" % b), V("pb%d" % (2 + b), 0, C))
-        act(V("z"), V("scw"), AF.Relu, lst=la)
-        ts(V("zz"), V("scw"), 0.0, None, A.max, lst=la)
-        tt(V("nd"), V("z"), V("zz"), A.not_equal, lst=V("lm"))
-        scan(V("ns"), V("kb"), V("nd"), f=0.5)
-        tt(V("nm"), V("ns", 15, C, 16), V("mj"), A.mult)
-        tt(V("tau"), V("nm"), V("jw"), A.add)
-        copy(V("ltau"), V("tau"))
-        act(V("p%d" % (r + 1)) if r < 3 else V("pl_t", C, 2 * C), V("p%d" % r), AF.Copy, lst=V("ltau"))
+        tt(V("ph"), V("pb7", 0, 4 * NL), V("thr"), A.is_ge)
+        scan(V("sl"), V("ph"), V("cs"))
+        ts(V(la), V("sl", 3, 4 * NL, 4), SC, MID + 0.25, A.mult, A.add)
+        send(r, V("lp%d" % r), V(la), False, 2850.0)
+        mm(V("pb0", 0, C), [(V("uc"), V("ucs"), V(qc), V(qs))], after=(done,))
+        signs(V("scw"), V("pb0", 0, C), LESS)
+        unpack("fb", qc, qs, ((0, C),), (2, 3, 4, 1), LENT, (done,))
+        unpack("fp", "rc%d" % r, "rs%d" % r, FP, (2, 3, 4, 1, 0))
+        move(V("z"), V("scw"), lst=V(la), qs="A")
+        tt(V("u1"), V("scw"), V("dd"), A.mult, lst=V(la))
+        tt(V("dd"), V("z"), V("u1"), A.mult, lst=V("lm"))
+        tt(V("tb"), V("s2"), V("dd"), A.subtract)
         if r == 3:
-            iota(V("i520"), [[1, 520]], 0, 0)
-            act(V("pl_t", 0, C), V("i520", 0, C), AF.Copy, lst=la)
+            move(V("pl_t", 0, C), V("place"), lst=V(la), plus=CMID)
+            move(V("pl_t", C, 2 * C), V("tb"), scale=0.5, plus=CMID)
             dma("S", [V("pl_t")], [], lambda: [(T.pl[:, :], T["pl_t"][0::16, :])])
-        for a, e in ((0, CA), (CA, C)):
+        k = 0
+        for lo, hi in ZP:
             for t in range(4):
-                either(V("zt", 4 * a + t, 4 * e, 4), V("fp%d" % t), V("lp%d" % r, a // 16, e // 16))
-            quant(V("zq", a, e), V("zqs", a, e), V("zt", 4 * a, 4 * e))
-        for b in range(4):
-            bias[0] = BIAS * (3 - b)
-            for i, (a, e) in enumerate(((0, CA), (CA, C))):
-                bank = V("pb%d" % ((2, 3, 4, 5, 0, 1, 6, 7)[4 * i + b]), 0, e - a)
-                mm(bank, [(V("wq", 128 * b, 128 * b + 128), V("wqs", 128 * b, 128 * b + 128), V("zq", a, e), V("zqs", a, e))])
-                out_of_psum(V("hs%d" % b, a, e), bank, scale=0.03125)
-        nx = ("x2", "x3", "x4")[r - 1]
-        for a, e in ((0, CA), (CA, C)):
+                move(V("zt", 4 * lo + t, 4 * hi, 4), V("fp%d" % t), lst=V("lp%d" % r, lo // 16, hi // 16))
+            quant(V("zq", lo, hi), V("zqs", lo, hi), V("zt", 4 * lo, 4 * hi))
             for b in range(4):
-                bias[0] = BIAS * (3 - b)
-                tt(V(nx, 4 * a + b, 4 * e, 4), V("hs%d" % b), V("fb%d" % b, a, e), A.add, lst=V("la%d" % r, a // 16, e // 16))
-        bias[0] = 0.0
+                bias[0] = TUNE["bias"] * (3 - b)
+                bank = V("pb%d" % (2, 3, 4, 1, 0, 6, 7)[k % 7], 0, hi - lo)
+                k += 1
+                mm(bank, [(V("wq", 128 * b, 128 * b + 128), V("wqs", 128 * b, 128 * b + 128), V("zq", lo, hi), V("zqs", lo, hi))])
+                move(V("hs%d" % b, lo, hi), bank, scale=0.03125)
+                bias[0] = 0.0
+        nx = ("x2", "x3", "x4")[r - 1]
+        for lo, hi in XP:
+            for b in range(4):
+                out, lst = V(nx, 4 * lo + b, 4 * hi, 4), V(la, lo // 16, hi // 16)
+                if b in LENT:
+                    move(V("kk", lo, hi), V("hs%d" % b), lst=lst, qs="A")
+                    tt(out, V("pb5", lo, hi), V("kk", lo, hi), A.add)
+                else:
+                    tt(out, V("hs%d" % b), V("fb%d" % b, lo, hi), A.add, lst=lst)
         if r < 3:
-            powers(r + 1)
+            for n in (1, 2, 3):
+                move(V("tg%d" % n), V("tb"), lst=V("l%d" % (n - 1)))
+                listed(n)
     quant(V("vq"), V("vqs"), V("vt"))
-    for i, (a, b) in enumerate(((0, CA), (CA, C))):
+    for i, (a, b) in enumerate(XP):
         quant(V("qc4", a, b), V("qs4", a, b), V("x4", 4 * a, 4 * b))
-        dma("S", [V("qc4", a, b)], [], lambda a=a, b=b: [(T.oc[:, 4 * a:4 * b], T["qc4"][:, a:b].bitcast(dt.uint8))])
+        dma("S", [V("qc4", a, b)], [], lambda a=a, b=b: [(T.oc[:, 4 * a:4 * b], T["qc4"][:, a:b].bitcast(dt.uint8))], 2400.0)
         mm(V("pb%d" % i, 0, b - a), [(V("vq"), V("vqs"), V("qc4", a, b), V("qs4", a, b))])
-        out_of_psum(V("yt", a, b), V("pb%d" % i, 0, b - a))
-        dma("S", [V("yt", a, b)], [], lambda a=a, b=b: [(T.y[:, a:b], T["yt"][:, a:b])])
+        move(V("yt", a, b), V("pb%d" % i, 0, b - a))
+        dma("S", [V("yt", a, b)], [], lambda a=a, b=b: [(T.y[:, a:b], T["yt"][:, a:b])], 2400.0)
     dma("S", [V("qs4")], [], lambda: [(T.osc[4 * k:4 * k + 4, :], T["qs4"][32 * k:32 * k + 4, :]) for k in range(4)])
 
     n = len(ops)
@@ -441,78 +426,70 @@ def rank_program(g, core, T, topo):
     for i, o in enumerate(ops):
         for j in o["deps"]:
             users[j].append(i)
+
+    def place(rank_of, before, after, back):
+        busy = {k: [] for k in "VAPGS"}
+        start, end, free, qof = [None] * n, [None] * n, [None] * n, [None] * n
+        left = [len(before[i]) for i in range(n)]
+        ready = [i for i in range(n) if not left[i]]
+        while ready:
+            i = max(ready, key=lambda j: rank_of[j])
+            ready.remove(i)
+            o = ops[i]
+            late = o.get("late", 0.0)
+            best = None
+            for q, c in o["cost"].items():
+                t = max([(free[j] + late if back else end[j]) + WAKE if wait is True or (wait and qof[j] != q) else free[j] for j, wait in before[i].items()] + [late if back else 0.0])
+                for s, e in busy.get(q, ()):
+                    if t + c <= s:
+                        break
+                    t = max(t, e)
+                worth = t + c + (TUNE["spare"] * c if q == "V" else 0.0)
+                if best is None or worth < best[0]:
+                    best = (worth, t + c, t, q)
+            free[i], start[i], qof[i] = best[1:]
+            end[i] = free[i] + (0.0 if back else late)
+            if qof[i] in busy:
+                busy[qof[i]].append((start[i], free[i]))
+                busy[qof[i]].sort()
+            for u in after[i]:
+                left[u] -= 1
+                if not left[u]:
+                    ready.append(u)
+        return max(end), start, end, qof
+
+    fore = [o["deps"] for o in ops]
+    aft = [{u: ops[u]["deps"][i] for u in users[i]} for i in range(n)]
     prio = [0.0] * n
     for i in range(n - 1, -1, -1):
-        prio[i] = ops[i]["cost"] + max([prio[u] + WAKE for u in users[i]] + [0.0])
+        prio[i] = min(ops[i]["cost"].values()) + ops[i].get("late", 0.0) + max([prio[u] + WAKE for u in users[i]] + [0.0])
     prio = [p + o["bias"] for p, o in zip(prio, ops)]
-    free = {k: 0.0 for k in "VAPGSR"}
-    end = [None] * n
-    left = [len(o["deps"]) for o in ops]
-    ready = [i for i in range(n) if not left[i]]
-    order = []
-    while ready:
-        best = None
-        cand = []
-        for i in ready:
-            o = ops[i]
-            at = max([end[j] + WAKE for j in o["deps"]] + [0.0])
-            if o["kind"] == "r":
-                at = end[list(o["deps"])[0]] if len(o["deps"]) == 1 else max(end[j] for j in o["deps"])
-                cand.append((at, i, "R"))
-                continue
-            for q in o["q"]:
-                cand.append((max(at, free[q]), i, q))
-        first = min(c[0] for c in cand)
-        best = max((c for c in cand if c[0] <= first + 20.0), key=lambda c: (prio[c[1]], -c[0]))
-        late = best[0] + ops[best[1]]["cost"]
-        soon = [c for c in cand if c[2] == best[2] and prio[c[1]] > prio[best[1]] and c[0] - best[0] < LOOK * (late - c[0])]
-        if soon:
-            best = max(soon, key=lambda c: (prio[c[1]], -c[0]))
-        at, i, q = best
-        o = ops[i]
-        if o["kind"] == "d":
-            free[q] = at + 60.0 * (o["amount"] // 16)
-            end[i] = free[q] + o["cost"]
-        elif o["kind"] == "r":
-            end[i] = at + o["cost"]
-        else:
-            free[q] = end[i] = at + o["cost"]
-        order.append((i, q, at))
-        ready.remove(i)
-        for u in users[i]:
-            left[u] -= 1
-            if not left[u]:
-                ready.append(u)
+    plans = []
+    for turn in range(TUNE["turns"]):
+        plans.append(place(prio, fore, aft, False))
+        prio = [p + o["bias"] for p, o in zip(place(plans[-1][2], aft, fore, True)[2], ops)]
+    span, start, end, qof = min(plans, key=lambda p: p[0])
+    TUNE["span"] = [round(p[0]) for p in plans]
 
     eng = {"V": g.vector, "A": g.scalar, "P": g.tensor, "G": g, "S": g.sync}
     csem = {"V": "s_v", "A": "s_a", "P": "s_p", "G": "s_g"}
     count = {k: 0 for k in csem}
     known = {k: {} for k in "VAPGS"}
-    token, clock, qof = [None] * n, [None] * n, [None] * n
-    for i, q, at in order:
-        o = ops[i]
-        qof[i] = q
+    token, clock = [None] * n, [None] * n
+    for i in sorted(range(n), key=lambda j: (start[j], j)):
+        o, q = ops[i], qof[i]
         if o["kind"] == "r":
             token[i], clock[i] = (o["sem"], o["amount"]), {o["sem"]: o["amount"]}
-            for j in o["deps"]:
-                for s, v in (clock[j] or {}).items():
-                    clock[i][s] = max(clock[i].get(s, 0), 0)
             continue
         e = eng[q]
-        need = []
-        for j, raw in o["deps"].items():
-            if token[j] is None:
-                continue
-            need.append(j)
-        need.sort(key=lambda j: -end[j])
-        for j in need:
+        for j in sorted((j for j, wait in o["deps"].items() if token[j] and (wait is True or (wait and qof[j] != q))), key=lambda j: -end[j]):
             s, v = token[j]
             if known[q].get(s, 0) >= v:
                 continue
             e.wait_ge(T.sem[s], v)
             for s2, v2 in clock[j].items():
                 known[q][s2] = max(known[q].get(s2, 0), v2)
-        call = o["emit"](e, q) if len(o["q"]) > 1 else o["emit"](e)
+        call = o["emit"](e, q)
         if o["kind"] == "c":
             count[q] += 1
             call.then_inc(T.sem[csem[q]], 1)

@@ -11,7 +11,9 @@ XP = ((0, 288), (288, C))
 MP = ((0, 288), (288, C))
 ZP = ((0, 160), (160, 288), (288, C))
 FP = XP
-LENT = ()
+TP = (((0, 192), (192, C)),) * 3
+HOLD = (3, 3, 4, 5)
+LENT = ((2, 3),) * 3
 PAIRS = ((0, 1), (2, 3), (4, 5), (6,))
 F32, BF16, I32, U16, CODE, U8 = "float32", "bfloat16", "int32", "uint16", "float8_e4m3fn_x4", "uint8"
 
@@ -34,10 +36,10 @@ _buf(2, I32, "ip")
 _buf(4, I32, "ib")
 _buf(16, F32, "cols")
 _buf(8, F32, "sp0", "sp1", "sp", "ih")
-_buf(16, BF16, "pat")
-_buf(128, BF16, "wd0", "wd", "im", "maska")
+_buf(16, BF16, "pat", "j16", "t16", "n16", "k16")
+_buf(2, BF16, "hc")
+_buf(128, BF16, "im", "maska")
 _buf(4 * NL, F32, "thr", "ph", "sl", "cs")
-_buf(NL, I32, "iq")
 _buf(8, I32, "iu")
 _buf(8, U16, "lu0", "la4")
 _buf(NL, U16, "lq")
@@ -45,7 +47,7 @@ _parts("li", NL, I32, "kgw", "pgw", "mgw")
 _parts("lu", NL, U16, "l0", "lpw", "lm")
 _parts("lists", NL, U16, "l1", "l2", "l3")
 _buf(C, BF16, "place", "kb", "bw", "scw", "z", "pa", "pc", "p2", "tb")
-_buf(C, F32, "yt", "s2", "dd", "u1", "kk")
+_buf(C, F32, "yt", "s2", "dd", "u1", "kk0", "kk1", "kk2", "kk3")
 _buf(520, BF16, "w1")
 _buf(560, BF16, "w2", "ones")
 _buf(512, BF16, "i3", "w3", "ut", "vt", "at")
@@ -78,7 +80,8 @@ WAKE = 100.0
 CY = 1.04
 GY = 1.62
 PY = 1.25
-TUNE = {"bias": 0.0, "spare": 0.3, "turns": 6}
+PLANS = []
+TUNE = {"bias": 0.0, "spare": 0.3, "turns": 6, "fly": 2300.0, "after": 0, "noise": None}
 
 
 def _hit(a, b):
@@ -155,8 +158,8 @@ def rank_program(g, core, T, topo):
         both = not (in0[0].startswith("pb") or in1[0].startswith("pb"))
         return add(costs("V", out, (in0, in1, V("cols")), lst, both), [in0, in1, lst], [out], lambda e, q: e.tensor_tensor(ap(out), src(in0, lst), ap(in1), op))
 
-    def scan(out, d0, d1):
-        return add(costs("V", out, (d0, d1), None), [d0, d1], [out], lambda e, q: e.tensor_tensor_scan(ap(out), ap(d0), ap(d1), 0.0, A.mult, A.add))
+    def scan(out, d0, d1, first=0.0, behind=()):
+        return add(costs("V", out, (d0, d1), None), [d0, d1], [out], lambda e, q: e.tensor_tensor_scan(ap(out), ap(d0), ap(d1), first, A.mult, A.add), behind=behind)
 
     def move(out, in_, lst=None, scale=None, plus=None, relu=False, qs="VA"):
         def emit(e, q):
@@ -243,7 +246,8 @@ def rank_program(g, core, T, topo):
         return j
 
     col = lambda i: V("cols", i, i + 1)
-    QC, HC, SC, ISC, R4, LESS, CMID = [col(i) for i in range(7)]
+    QC, SC, ISC, R4, LESS, CMID = [col(i) for i in range(6)]
+    HC = V("hc", 0, 1)
 
     a, b = XP[0][1], C
     d0 = dma("S", [], [V("pgw")], lambda: [(ap(V("pgw")), T.pg[:, :])])
@@ -259,7 +263,7 @@ def rank_program(g, core, T, topo):
     ipv = V("ip", 0, 1)
     ib = lambda i: V("ib", i, i + 1)
     fill(V("ones"), 1.0, "V")
-    iota(V("place"), [[1, C]], -MID, 0)
+    scan(V("place"), V("ones", 0, C), V("ones", 0, C), -MID - 1.0)
     iota(ipv, [[0, 1]], 0, 1)
     ts(ib(0), ipv, 15, None, A.bitwise_and)
     ts(ib(1), ipv, 4, None, A.logical_shift_right)
@@ -269,11 +273,12 @@ def rank_program(g, core, T, topo):
     ts(R4, ib(2), float(L), 5.0, A.mult, A.add)
     fill(LESS, -2.0 ** -100, "V")
     fill(CMID, float(MID), "V")
-    iota(V("iq"), [[0, NL]], 0, 1)
-    move(V("lq"), V("iq"), qs="V")
-    keep(V("wd0"), V("ones", 0, 128), [[1, 128]], A.not_equal, 0, -1)
-    keep(V("wd"), V("wd0"), [[1, 128]], A.not_equal, -1, -1, 2.0 ** 20)
-    move(V("kb"), V("wd"), lst=V("lq"))
+    ts(V("lq"), V("ones", 0, NL), QC, None, A.mult)
+    ts(V("j16"), V("place", MID, MID + 16), QC, None, A.subtract)
+    ts(V("t16"), V("j16"), 1.0, 2.0 ** 20, A.is_equal, A.mult)
+    ts(V("n16"), V("j16"), 0.0, None, A.not_equal)
+    tt(V("k16"), V("n16"), V("t16"), A.max)
+    move(V("kb"), V("k16"), lst=V("lq"))
     ts(col(8), QC, 15.0, 2.0 ** -21 - 0.5, A.is_lt, A.mult)
     ts(SC, col(8), 0.5, None, A.add)
     ts(col(9), QC, 15.0, 2.0 ** 21 - 2.0, A.is_lt, A.mult)
@@ -339,7 +344,7 @@ def rank_program(g, core, T, topo):
         k = 0
         for lo, hi in pieces:
             for b in range(4):
-                bank = V("pb%d" % (5 if b in skip else banks[k % len(banks)]), 0, hi - lo)
+                bank = V("pb%d" % (HOLD[b] if b in skip else banks[k % len(banks)]), 0, hi - lo)
                 mm(bank, [(V("e%d" % b), V("es%d" % b), V(c, lo, hi), V(s, lo, hi))], after=after)
                 if b not in skip:
                     move(V("%s%d" % (to, b), lo, hi), bank)
@@ -364,21 +369,25 @@ def rank_program(g, core, T, topo):
                       start=lo == 0, stop=hi == C, behind=() if done is None else (done,))
         for s, val in enumerate((0.5, 1.5, 3.0, 3.0)):
             ts(V("dv", s, 28 * L, L), V("pb6", s, 112, 4), val, None, A.mult)
+        masked = {}
         for pair in PAIRS:
             for k in pair:
-                scan(V("sc", 64 * k, 64 * k + 4 * L), V("sc", 64 * k - 61, 64 * k - 61 + 4 * L) if k else V("dv", 28 * L + 3, 32 * L + 3), V("dv", 4 * L * k, 4 * L * k + 4 * L))
+                scan(V("sc", 64 * k, 64 * k + 4 * L), V("sc", 64 * k - 61, 64 * k - 61 + 4 * L) if k else V("dv", 28 * L + 3, 32 * L + 3), V("dv", 4 * L * k, 4 * L * k + 4 * L),
+                     behind=masked.get(k - 2, ()))
             k, n = pair[0], len(pair)
-            tt(V("at", 64 * k + 64, 64 * (k + n) + 64), V("sc", 64 * k, 64 * (k + n)), V("maska", 0, 64 * n), A.mult, lst=V("la4", 0, 4 * n))
+            masked[pair[-1]] = (tt(V("at", 64 * k + 64, 64 * (k + n) + 64), V("sc", 64 * k, 64 * (k + n)), V("maska", 0, 64 * n), A.mult, lst=V("la4", 0, 4 * n)),)
         quant(V("aq"), V("aqs"), V("at"))
         mm(V("pb7", 0, 128), [(V("aq"), V("aqs"), V("b3"), V("b3s"))])
         tt(V("ph"), V("pb7", 0, 4 * NL), V("thr"), A.is_ge)
         scan(V("sl"), V("ph"), V("cs"))
         ts(V(la), V("sl", 3, 4 * NL, 4), SC, MID + 0.25, A.mult, A.add)
-        send(r, V("lp%d" % r), V(la), False, 2850.0)
-        mm(V("pb0", 0, C), [(V("uc"), V("ucs"), V(qc), V(qs))], after=(done,))
+        send(r, V("lp%d" % r), V(la), False, TUNE["fly"])
+        lent = LENT[r - 1]
+        banks = [k for k in (2, 3, 4, 5, 1, 0, 6, 7) if k not in [HOLD[b] for b in lent]]
+        mm(V("pb0", 0, C), [(V("uc"), V("ucs"), V(qc), V(qs))], after=(done,) if TUNE["after"] > 1 else ())
         signs(V("scw"), V("pb0", 0, C), LESS)
-        unpack("fb", qc, qs, ((0, C),), (2, 3, 4, 1), LENT, (done,))
-        unpack("fp", "rc%d" % r, "rs%d" % r, FP, (2, 3, 4, 1, 0))
+        unpack("fb", qc, qs, ((0, C),), banks[:-3], lent, (done,) if TUNE["after"] else ())
+        unpack("fp", "rc%d" % r, "rs%d" % r, FP, banks[:-2])
         move(V("z"), V("scw"), lst=V(la), qs="A")
         tt(V("u1"), V("scw"), V("dd"), A.mult, lst=V(la))
         tt(V("dd"), V("z"), V("u1"), A.mult, lst=V("lm"))
@@ -394,7 +403,7 @@ def rank_program(g, core, T, topo):
             quant(V("zq", lo, hi), V("zqs", lo, hi), V("zt", 4 * lo, 4 * hi))
             for b in range(4):
                 bias[0] = TUNE["bias"] * (3 - b)
-                bank = V("pb%d" % (2, 3, 4, 1, 0, 6, 7)[k % 7], 0, hi - lo)
+                bank = V("pb%d" % banks[k % len(banks)], 0, hi - lo)
                 k += 1
                 mm(bank, [(V("wq", 128 * b, 128 * b + 128), V("wqs", 128 * b, 128 * b + 128), V("zq", lo, hi), V("zqs", lo, hi))])
                 move(V("hs%d" % b, lo, hi), bank, scale=0.03125)
@@ -403,14 +412,15 @@ def rank_program(g, core, T, topo):
         for lo, hi in XP:
             for b in range(4):
                 out, lst = V(nx, 4 * lo + b, 4 * hi, 4), V(la, lo // 16, hi // 16)
-                if b in LENT:
-                    move(V("kk", lo, hi), V("hs%d" % b), lst=lst, qs="A")
-                    tt(out, V("pb5", lo, hi), V("kk", lo, hi), A.add)
+                if b in lent:
+                    move(V("kk%d" % b, lo, hi), V("hs%d" % b), lst=lst, qs="A")
+                    tt(out, V("pb%d" % HOLD[b], lo, hi), V("kk%d" % b, lo, hi), A.add)
                 else:
                     tt(out, V("hs%d" % b), V("fb%d" % b, lo, hi), A.add, lst=lst)
         if r < 3:
             for n in (1, 2, 3):
-                move(V("tg%d" % n), V("tb"), lst=V("l%d" % (n - 1)))
+                for lo, hi in TP[n - 1]:
+                    move(V("tg%d" % n, lo, hi), V("tb"), lst=V("l%d" % (n - 1), lo // 16, hi // 16))
                 listed(n)
     quant(V("vq"), V("vqs"), V("vt"))
     for i, (a, b) in enumerate(XP):
@@ -464,10 +474,11 @@ def rank_program(g, core, T, topo):
     for i in range(n - 1, -1, -1):
         prio[i] = min(ops[i]["cost"].values()) + ops[i].get("late", 0.0) + max([prio[u] + WAKE for u in users[i]] + [0.0])
     prio = [p + o["bias"] for p, o in zip(prio, ops)]
-    plans = []
-    for turn in range(TUNE["turns"]):
+    plans = PLANS
+    for turn in range(0 if plans else TUNE["turns"]):
         plans.append(place(prio, fore, aft, False))
-        prio = [p + o["bias"] for p, o in zip(place(plans[-1][2], aft, fore, True)[2], ops)]
+        last = min(plans, key=lambda p: p[0]) if TUNE["noise"] else plans[-1]
+        prio = [p + o["bias"] + TUNE["noise"]() if TUNE["noise"] else p + o["bias"] for p, o in zip(place(last[2], aft, fore, True)[2], ops)]
     span, start, end, qof = min(plans, key=lambda p: p[0])
     TUNE["span"] = [round(p[0]) for p in plans]
 

@@ -9,11 +9,13 @@ L = 14
 STEP = (1, 2, 3)
 XP = ((0, 288), (288, C))
 MP = ((0, 288), (288, C))
-ZP = ((0, 160), (160, 288), (288, C))
+ZP = ((0, 224), (224, C))
 FP = XP
+ROUTES = ((None, True, 0, 288, 3500.0), (None, False, 0, C, 3850.0), (None, True, 288, C, 5000.0))
+NEAR = (True, True, True)
 TP = (((0, 192), (192, C)),) * 3
 HOLD = (3, 3, 4, 5)
-LENT = ((2, 3),) * 3
+LENT = ((3,),) * 3
 PAIRS = ((0, 1), (2, 3), (4, 5), (6,))
 F32, BF16, I32, U16, CODE, U8 = "float32", "bfloat16", "int32", "uint16", "float8_e4m3fn_x4", "uint8"
 
@@ -46,12 +48,14 @@ _buf(NL, U16, "lq")
 _parts("li", NL, I32, "kgw", "pgw", "mgw")
 _parts("lu", NL, U16, "l0", "lpw", "lm")
 _parts("lists", NL, U16, "l1", "l2", "l3")
-_buf(C, BF16, "place", "kb", "bw", "scw", "z", "pa", "pc", "p2", "tb")
-_buf(C, F32, "yt", "s2", "dd", "u1", "kk0", "kk1", "kk2", "kk3")
+_buf(C, BF16, "place", "kb", "bw", "scw", "z", "pa", "p2")
+_buf(C, F32, "yt", "tb", "s2", "dd", "u1", "kk0", "kk1", "kk2", "kk3")
 _buf(520, BF16, "w1")
 _buf(560, BF16, "w2", "ones")
 _buf(512, BF16, "i3", "w3", "ut", "vt", "at")
 _buf(32 * L + 4, F32, "dv")
+_buf(4 * L + 4, F32, "c0")
+SCRATCH["d3"] = ("sbuf", [128, 28, L], F32)
 _buf(448, F32, "sc")
 _buf(2 * C, F32, "pl_t")
 _buf(4 * C, BF16, "xt", "x2", "x3", "x4", "zt")
@@ -65,7 +69,10 @@ _parts("hs", C, F32, *["hs%d" % i for i in range(4)])
 _parts("fb", C, BF16, *["fb%d" % i for i in range(4)])
 _parts("fp", C, BF16, *["fp%d" % i for i in range(4)])
 _parts("tg", C, BF16, "tg1", "tg2", "tg3")
-_parts("tsum", C, BF16, "ts1", "ts2", "ts3")
+_parts("tsum", C, BF16, "ts0", "ts1", "ts2", "ts3")
+_buf(3 * NL, F32, "df")
+_buf(2 * NL, F32, "ef")
+_buf(NL, F32, "sf", "sg")
 for _i in (1, 2, 3, 4):
     _buf(C, CODE, "qc%d" % _i)
     _buf(C, U8, "qs%d" % _i)
@@ -74,14 +81,19 @@ for _i in (1, 2, 3):
     _buf(C, U8, "rs%d" % _i)
     _buf(NL, U16, "la%d" % _i, "lp%d" % _i)
 
-SEMAPHORES = ["s_v", "s_a", "s_p", "s_g", "loc"] + ["d_%d" % i for i in range(40)] + ["r_%d" % i for i in range(20)]
+SEMAPHORES = ["s_v", "s_a", "s_p", "s_g", "loc"] + ["d_%d" % i for i in range(40)] + ["r_%d_%d" % (r, i) for r in (1, 2, 3) for i in range(8)] + ["r_l%d" % r for r in (1, 2, 3)]
 
-WAKE = 100.0
-CY = 1.04
-GY = 1.62
-PY = 1.25
+WAKE = 80.0
+SAME = 90.0
+CY = 0.82
+GY = 1.33
+AY = 1.17
+PY = 0.97
+QY = 0.279
+FIX = (87.0, 83.0, 37.0, 58.0, 52.0, 25.0)
 PLANS = []
-TUNE = {"bias": 0.0, "spare": 0.3, "turns": 6, "fly": 2300.0, "after": 0, "noise": None}
+CASES = (({"V": 1.25, "A": 1.25, "P": 1.5, "G": 1.3, "R": 1.5}, 1.3, 120.0), ({"V": 0.9, "A": 0.85, "R": 1.3}, 1.0, 70.0))
+TUNE = {"bias": 0.0, "d3": 0, "win": (300.0, 1000.0, 300.0, 1000.0, 0.2, 0.3), "poly": 1, "slack": 300.0, "spare": 0.1, "sg": 1.0, "two": 1, "gfill": 1, "pin": 1, "zq": "VA", "row": 1600.0, "first": 1100.0, "l0": 1550.0, "turns": 4, "fly": 1400.0, "setup": 1, "early": 2, "sum": (0, 0, 1), "adds": 2600.0, "after": 0, "seed": 1, "climb": 6000, "land": (2050.0, 3100.0, 3600.0, 3700.0, 4600.0, 4800.0, 5300.0)}
 
 
 def _hit(a, b):
@@ -92,10 +104,39 @@ def _hit(a, b):
     return True
 
 
+def _carriers(T, topo, core):
+    able = [c for c in topo.cores_of(core) if T.rank_of(c) is None and all(topo.may_write(c, o) for o in T.cores if o != core)]
+    return sorted(able, key=lambda c: topo.die(c) != topo.die(core))
+
+
+def _near_engines(T, topo, core, via):
+    far = topo.engines(core, [o for o in T.cores if o != core][0])
+    return [n for n in topo.engines(core, _carriers(T, topo, core)[via]) if (n in far) != NEAR[via]]
+
+
+def carrier_program(g, core, T, topo):
+    for home in T.cores:
+        mine = _carriers(T, topo, home)
+        if core not in mine:
+            continue
+        sent = 0
+        for r in (1, 2, 3):
+            to = T.cores[T.rank_of(home) ^ STEP[r - 1]]
+            for i, (via, codes, lo, hi, takes) in enumerate(ROUTES):
+                if via == mine.index(core):
+                    sem = T.sem["r_%d_%d" % (r, i)]
+                    piece = T["rc%d" % r][:, lo:hi].bitcast(dt.uint8) if codes else T["rs%d" % r][:, lo:hi]
+                    g.wait_ge(sem, len(_near_engines(T, topo, home, via)))
+                    g.remote_dma(piece, piece, sem, T.sem["loc"], topo.addr(to)[1], topo.addr(to)[0], topo.mask(core, to))
+                    sent += len(topo.engines(core, to))
+        if sent:
+            g.wait_ge(T.sem["loc"], sent)
+
+
 def rank_program(g, core, T, topo):
     rank = T.rank_of(core)
     if rank is None:
-        return
+        return carrier_program(g, core, T, topo)
     A = AluOpType
     AF = ActivationFunctionType
     ops, seen, bias = [], {}, [0.0]
@@ -107,6 +148,8 @@ def rank_program(g, core, T, topo):
     def ap(v):
         if not isinstance(v, tuple):
             return v
+        if v[0] == "d3":
+            return T["d3"][:, v[1] // L:v[2] // L, :] if v[3] == 1 else T["d3"][:, :, v[1]]
         return T[v[0]][:, v[1]:v[2]] if v[3] == 1 else T[v[0]][:, v[1]:v[2]:v[3]]
 
     def src(v, l):
@@ -142,9 +185,9 @@ def rank_program(g, core, T, topo):
     def costs(qs, out, ins, lst, both=False):
         n = n_of(out)
         if lst is not None:
-            c = {"V": 62 + n * GY, "A": 81 + n * GY}
+            c = {"V": FIX[0] + n * GY, "A": FIX[1] + n * GY * AY}
         else:
-            c = {"V": max(64.0, n * (2.0 if both else 0.5 if narrow(out, *ins) else 1.0)) * CY, "A": max(64.0, n) * CY}
+            c = {"V": max(64.0, n * (2.0 if both else 0.5 if narrow(out, *ins) else 1.0)) * CY + FIX[2], "A": max(64.0, n) * CY * AY + FIX[3]}
         return {q: c[q] for q in qs}
 
     def ts(out, in0, s1, s2, op0, op1=None, lst=None, behind=()):
@@ -166,7 +209,7 @@ def rank_program(g, core, T, topo):
             o, i = ap(out), src(in_, lst)
             if q == "V":
                 if relu:
-                    return e.tensor_scalar(o, i, 0.0, None, A.max)
+                    return e.tensor_scalar(o, i, 0.0, None, A.is_gt)
                 if scale is None and plus is None:
                     return e.tensor_copy(o, i)
                 if plus is None:
@@ -178,28 +221,29 @@ def rank_program(g, core, T, topo):
                 return e.activation(o, i, AF.Identity, bias=ap(plus), scale=1.0 if scale is None else ap(scale))
             if scale is not None:
                 return e.activation(o, i, AF.Copy, scale=ap(scale))
-            return e.activation(o, i, AF.Relu if relu else AF.Copy)
+            return e.activation(o, i, AF.Relu, scale=1.0 / TUNE["sg"]) if relu else e.activation(o, i, AF.Copy)
         return add(costs(qs, out, (in_, scale, plus), lst), [in_, lst, scale, plus], [out], emit)
 
-    def signs(out, in_, less=None):
-        def emit(e, q):
-            if q == "V":
-                return e.tensor_scalar(ap(out), ap(in_), 0.0, None, A.is_gt)
-            if less is None:
-                return e.activation(ap(out), ap(in_), AF.Sign)
-            return e.activation(ap(out), ap(in_), AF.Sign, bias=ap(less))
-        return add(costs("VA" if less is None else "A", out, (in_,), None), [in_, less], [out], emit)
+    def signs(out, in_, loose=False):
+        if loose:
+            return add(costs("VA", out, (in_,), None), [in_], [out], lambda e, q: e.tensor_scalar(ap(out), ap(in_), 0.0, None, A.is_gt) if q == "V" else e.activation(ap(out), ap(in_), AF.Sign))
+        return add(costs("A", out, (in_,), None), [in_, TINY], [out], lambda e, q: e.activation(ap(out), ap(in_), AF.Sign, bias=ap(TINY)))
 
-    def fill(out, val, qs="VA"):
+    def fill(out, val, qs="VAG"):
         ones = V("ones", 0, n_of(out))
         def emit(e, q):
             if q == "V":
                 return e.memset(ap(out), val)
+            if q == "G":
+                return e.iota(ap(out), [[0, n_of(out)]], int(val), 0, allow_small_or_imprecise_dtypes=True)
             return e.activation(ap(out), ap(ones), AF.Copy, scale=val)
-        return add(costs(qs, out, (), None), [ones] if "A" in qs else [], [out], emit)
+        cost = costs(qs.replace("G", ""), out, (), None)
+        if "G" in qs and TUNE["gfill"]:
+            cost["G"] = 160 + 2 * n_of(out) * CY
+        return add(cost, [ones] if "A" in qs else [], [out], emit)
 
     def quant(c, s, t):
-        return add({"V": 15 + 0.275 * n_of(t)}, [t], [c, s], lambda e, q: e.quantize_mx(ap(c), ap(s), ap(t)))
+        return add({"V": FIX[4] + QY * n_of(t)}, [t], [c, s], lambda e, q: e.quantize_mx(ap(c), ap(s), ap(t)))
 
     def mm(out, terms, after=(), start=True, stop=True, behind=()):
         def emit(e, q):
@@ -207,7 +251,7 @@ def rank_program(g, core, T, topo):
             for k, (a, b, c, d) in enumerate(terms):
                 last = e.matmul_mx(ap(out), ap(a), ap(b), ap(c), ap(d), start and k == 0, stop and k == len(terms) - 1)
             return last
-        return add({"P": (n_of(out) + 16) * PY * len(terms)}, [v for t in terms for v in t], [out], emit, after=after, behind=behind)
+        return add({"P": ((n_of(out) + 16) * PY + FIX[5]) * len(terms)}, [v for t in terms for v in t], [out], emit, after=after, behind=behind)
 
     def iota(out, pattern, base, cm):
         def emit(e, q):
@@ -221,44 +265,47 @@ def rank_program(g, core, T, topo):
 
     dcount, rcount, sent = [0], [0], [0]
 
-    def dma(q, reads, writes, pairs, cost=2000.0, behind=()):
+    def dma(q, reads, writes, pairs, cost=2000.0, behind=(), adds=False):
         sem = "d_%d" % dcount[0]
         dcount[0] += 1
         def emit(e, q):
             for o, i in pairs():
-                e.dma_start(o, i).then_inc(T.sem[sem], 16)
-        i = add({q: 60.0 * len(pairs())}, reads, writes, emit, "d", sem, 16 * len(pairs()), behind=behind)
+                (e.dma_start(o, i, accum_op=A.add) if adds else e.dma_start(o, i)).then_inc(T.sem[sem], 16)
+        i = add({q: (1000.0 if adds else 60.0) * len(pairs())}, reads, writes, emit, "d", sem, 16 * len(pairs()), behind=behind)
         ops[i]["late"] = cost
         return i
 
-    def send(r, dst_v, src_v, codes, latency, behind=()):
-        to = T.cores[rank ^ STEP[r - 1]]
-        rid, pid = topo.addr(to)[0], topo.addr(to)[1]
-        mask, k = topo.mask(core, to), len(topo.engines(core, to))
-        sem = "r_%d" % rcount[0]
+    def send(r, sem, dst_v, src_v, codes, latency, behind=(), via=None):
+        far = T.cores[rank ^ STEP[r - 1]]
+        to, used = far, topo.engines(core, far)
+        lands = len(used)
+        if via is not None:
+            to, used = _carriers(T, topo, core)[via], _near_engines(T, topo, core, via)
+            lands = len(topo.engines(_carriers(T, topo, far)[via], core))
         def emit(e, q):
             o, i = (ap(dst_v).bitcast(dt.uint8), ap(src_v).bitcast(dt.uint8)) if codes else (ap(dst_v), ap(src_v))
-            e.remote_dma(o, i, T.sem[sem], T.sem["loc"], pid, rid, mask)
-            sent[0] += k
-        j = add({"G": 150.0 if rcount[0] else 1650.0}, [src_v], [], emit, "s", behind=behind)
+            e.remote_dma(o, i, T.sem[sem], T.sem["loc"], topo.addr(to)[1], topo.addr(to)[0], sum(1 << n for n in used))
+            sent[0] += len(used)
+        j = add({"G": 150.0 if rcount[0] else TUNE["first"]}, [src_v], [], emit, "s", behind=behind)
         rcount[0] += 1
-        add({"R": latency}, [], [dst_v], None, "r", sem, k, after=(j,))
+        add({"R": latency}, [], [dst_v], None, "r", sem, lands, after=(j,))
         return j
 
     col = lambda i: V("cols", i, i + 1)
-    QC, SC, ISC, R4, LESS, CMID = [col(i) for i in range(6)]
+    QC, SC, ISC, R4, LESS, CMID, TINY = [col(i) for i in range(7)]
     HC = V("hc", 0, 1)
 
     a, b = XP[0][1], C
-    d0 = dma("S", [], [V("pgw")], lambda: [(ap(V("pgw")), T.pg[:, :])])
-    d1 = dma("A", [], [V("kgw")], lambda: [(ap(V("kgw")), T.kg[:, :])])
-    d1 = dma("A", [], [V("ut")], lambda: [(T["ut"][:, :], T.u[:, :])], 2700.0, (d1,))
-    d0 = dma("S", [], [V("xt", 0, 4 * a)], lambda: [(T["xt"][:, 0:4 * a], T.x[:, 0:4 * a])], 3400.0, (d0,))
-    d1 = dma("A", [], [V("xt", 4 * a)], lambda: [(T["xt"][:, 4 * a:4 * b], T.x[:, 4 * a:4 * b])], 3900.0, (d1,))
-    d0 = dma("S", [], [V("mgw")], lambda: [(ap(V("mgw")), T.mg[:, :])], 4000.0, (d0,))
-    d0 = dma("S", [], [V("wq")], lambda: [(T["wq"][:, :].bitcast(dt.uint8), T.wc[:, :])], 5300.0, (d0,))
-    d0 = dma("S", [], [V("wqs")], lambda: [(T["wqs"][:, :], T.ws[:, :])], 5600.0, (d0,))
-    d0 = dma("S", [], [V("vt")], lambda: [(T["vt"][:, :], T.v[:, :])], 6200.0, (d0,))
+    d0 = dma("S", [], [V("pgw")], lambda: [(ap(V("pgw")), T.pg[:, :])], TUNE["l0"])
+    d1 = dma("A", [], [V("kgw")], lambda: [(ap(V("kgw")), T.kg[:, :])], TUNE["l0"])
+    at = TUNE["land"]
+    d1 = dma("A", [], [V("ut")], lambda: [(T["ut"][:, :], T.u[:, :])], at[0], (d1,))
+    d0 = dma("S", [], [V("xt", 0, 4 * a)], lambda: [(T["xt"][:, 0:4 * a], T.x[:, 0:4 * a])], at[1], (d0,))
+    d1 = dma("A", [], [V("xt", 4 * a)], lambda: [(T["xt"][:, 4 * a:4 * b], T.x[:, 4 * a:4 * b])], at[2], (d1,))
+    d0 = dma("S", [], [V("mgw")], lambda: [(ap(V("mgw")), T.mg[:, :])], at[3], (d0,))
+    d0 = dma("S", [], [V("wq")], lambda: [(T["wq"][:, :].bitcast(dt.uint8), T.wc[:, :])], at[4], (d0,))
+    d0 = dma("S", [], [V("wqs")], lambda: [(T["wqs"][:, :], T.ws[:, :])], at[5], (d0,))
+    d0 = dma("S", [], [V("vt")], lambda: [(T["vt"][:, :], T.v[:, :])], at[6], (d0,))
 
     ipv = V("ip", 0, 1)
     ib = lambda i: V("ib", i, i + 1)
@@ -271,8 +318,11 @@ def rank_program(g, core, T, topo):
     move(QC, ib(0), qs="V")
     move(HC, ib(1), qs="V")
     ts(R4, ib(2), float(L), 5.0, A.mult, A.add)
-    fill(LESS, -2.0 ** -100, "V")
+    if TUNE["two"]:
+        fill(TINY, -2.0 ** -100, "V")
     fill(CMID, float(MID), "V")
+    if TUNE["sg"] == 1.0 and not TUNE["two"]:
+        fill(TINY, -2.0 ** -100, "V")
     ts(V("lq"), V("ones", 0, NL), QC, None, A.mult)
     ts(V("j16"), V("place", MID, MID + 16), QC, None, A.subtract)
     ts(V("t16"), V("j16"), 1.0, 2.0 ** 20, A.is_equal, A.mult)
@@ -285,12 +335,26 @@ def rank_program(g, core, T, topo):
     ts(ISC, col(9), 2.0, None, A.add)
     move(V("lu", 0, 2 * NL), V("li", 0, 2 * NL), qs="V")
     move(V("lm"), V("mgw"), qs="V")
-    ts(V("cs", 3, 4 * NL, 4), V("kgw"), -float(MID), ISC, A.add, A.mult)
+    ts(V("ts0", 15, C, 16) if TUNE["poly"] else V("cs", 3, 4 * NL, 4), V("kgw"), -float(MID), ISC, A.add, A.mult)
+    if TUNE["poly"]:
+        move(col(10), SC, scale=1.0 / 6.0)
 
     def listed(n):
         scan(V("ts%d" % n), V("kb"), V("tg%d" % n))
         now = V("ts%d" % n, 15, C, 16)
         ts(V("l%d" % n), now, SC, MID + 0.25, A.mult, A.add)
+        if TUNE["poly"]:
+            if n == 1:
+                move(V("cs", 3, 4 * NL, 4), now, scale=6.0)
+            if n == 3:
+                tt(V("df"), V("tsum", C + 15, 4 * C, 16), V("tsum", 15, 3 * C, 16), A.subtract)
+                tt(V("ef"), V("df", NL, 3 * NL), V("df", 0, 2 * NL), A.subtract)
+                tt(V("cs", 0, 4 * NL, 4), V("ef", NL, 2 * NL), V("ef", 0, NL), A.subtract)
+                move(V("cs", 1, 4 * NL, 4), V("ef", 0, NL), scale=3.0)
+                tt(V("sf"), V("df", 0, NL), V("df", NL, 2 * NL), A.add)
+                move(V("sg"), V("sf"), scale=3.0)
+                tt(V("cs", 2, 4 * NL, 4), V("sg"), V("cs", 0, 4 * NL, 4), A.subtract)
+            return
         tt(V("cs", 3 - n, 4 * NL, 4), now, V("ts%d" % (n - 1), 15, C, 16) if n > 1 else V("cs", 3, 4 * NL, 4), A.subtract)
 
     for lo, hi in ((0, 224), (224, C)):
@@ -302,12 +366,22 @@ def rank_program(g, core, T, topo):
     listed(2)
     move(V("tg3"), V("p2"), lst=V("l1"), scale=2.0)
     listed(3)
-    move(V("pc"), V("pa"))
-    tt(V("s2"), V("pa"), V("pc"), A.add, lst=V("lm"))
-    tt(V("dd"), V("pa"), V("pc"), A.subtract, lst=V("lm"))
+    if TUNE["setup"]:
+        move(V("s2"), V("pa"), lst=V("lm"))
+        move(V("dd"), V("s2"), scale=-1.0)
+        for name in ("dd", "s2"):
+            dma("G", [V("pa")], [V(name)], lambda name=name: [(ap(V(name)), ap(V("pa")))], TUNE["adds"], adds=True)
+    else:
+        move(V("z"), V("pa"), scale=-1.0)
+        tt(V("s2"), V("pa"), V("z"), A.subtract, lst=V("lm"))
+        tt(V("dd"), V("z"), V("pa"), A.add, lst=V("lm"))
     quant(V("uq"), V("uqs"), V("ut"))
     iota(V("iu"), [[16, 8]], 0, 0)
-    move(V("lu0"), V("iu"), qs="V")
+    if TUNE["two"]:
+        move(V("lu0"), V("iu"), qs="V")
+    else:
+        ts(LESS, QC, 1.0, None, A.is_equal)
+        ts(V("lu0"), V("iu"), LESS, None, A.add)
     add(costs("V", V("uc"), (), V("lu0")), [V("uq"), V("lu0")], [V("uc")], lambda e, q: e.tensor_copy(ap(V("uc")).bitcast(dt.uint32), ap(V("uq")).bitcast(dt.uint32).indirect(ap(V("lu0")))))
     add(costs("VA", V("ucs"), (), V("lu0")), [V("uqs"), V("lu0")], [V("ucs")],
         lambda e, q: e.tensor_copy(ap(V("ucs")), src(V("uqs"), V("lu0"))) if q == "V" else e.activation(ap(V("ucs")), src(V("uqs"), V("lu0")), AF.Copy))
@@ -318,23 +392,35 @@ def rank_program(g, core, T, topo):
     keep(V("sp1"), V("sp0"), [[-16, 8]], A.is_ge, 0, 1)
     keep(V("sp"), V("sp1"), [[16, 8]], A.is_ge, 1, -1)
     fill(V("pat"), 0.0)
-    for lo, hi, st, val in ((0, 10, 9, -1.0), (1, 2, 1, 3.0), (2, 3, 1, -3.0), (3, 5, 1, 1.0), (5, 6, 1, -2.0), (6, 15, 4, 1.0)):
+    for lo, hi, st, val in ((0, 1, 1, -1.0), (1, 5, 3, 3.0), (2, 3, 1, -3.0), (3, 4, 1, 1.0), (5, 10, 4, -6.0), (6, 7, 1, 3.0), (10, 15, 4, 6.0)) if TUNE["d3"] else (
+            (0, 10, 9, -1.0), (1, 2, 1, 3.0), (2, 3, 1, -3.0), (3, 5, 1, 1.0), (5, 6, 1, -2.0), (6, 15, 4, 1.0)):
         fill(V("pat", lo, hi, st), val)
     fill(V("w2"), 0.0)
     for k in range(7):
         move(V("w2", 48 + 64 * k, 64 + 64 * k), V("pat"), scale=V("sp", k, k + 1))
     quant(V("b2"), V("b2s"), V("w2"))
     iota(V("i3"), [[1, 32], [0, 4], [-8, 4]], PAD // 16, 0)
+    for t in range(4 if TUNE["poly"] else 0):
+        fill(V("i3", t, 512, 16), 99.0)
     ts(V("w3"), V("i3"), HC, None, A.is_equal)
     quant(V("b3"), V("b3s"), V("w3"))
     iota(V("im"), [[0, 2], [1, 16], [0, 4]], 0, 0)
     ts(V("maska"), V("im"), QC, None, A.is_equal)
-    iota(V("thr"), [[0, NL], [-1, 4]], 3, 0)
+    if not TUNE["poly"]:
+        iota(V("thr"), [[0, NL], [-1, 4]], 3, 0)
     iota(V("ih"), [[64, 2], [0, 4]], 0, 0)
     ts(V("la4"), V("ih"), R4, None, A.add)
-    fill(V("dv"), 0.0)
-    for lo, hi, val in ((5, 28 * L, -1.0), (6, 32 * L, -1.0), (7, 32 * L, 1.0 / 3.0), (8, 32 * L, 1.0), (9, 32 * L, 1.0), (28 * L + 4, 32 * L, 1.0)):
-        fill(V("dv", lo, hi, L), val, "V" if val == 1.0 / 3.0 else "VA")
+    if TUNE["d3"]:
+        fill(V("d3", 0, 28 * L), 0.0, "V")
+        for lo, val in ((5, -1.0), (6, -1.0), (7, 1.0 / 3.0), (8, 1.0), (9, 1.0)):
+            fill(V("d3", lo, 28 * L, L), val, "V" if val == 1.0 / 3.0 else "VAG")
+        fill(V("c0"), 0.0)
+        for lo, val in ((4, 1.0), (6, -1.0), (7, 1.0 / 3.0), (8, 1.0), (9, 1.0)):
+            fill(V("c0", lo, 4 * L, L), val, "V" if val == 1.0 / 3.0 else "VAG")
+    else:
+        fill(V("dv"), 0.0)
+        for lo, hi, val in ((5, 28 * L, -1.0), (6, 32 * L, -1.0), (7, 32 * L, 1.0 / 3.0), (8, 32 * L, 1.0), (9, 32 * L, 1.0), (28 * L + 4, 32 * L, 1.0)):
+            fill(V("dv", lo, hi, L), val, "V" if val == 1.0 / 3.0 else "VAG")
     fill(V("sc"), 0.0)
     fill(V("at", 0, 64), 0.0)
     fill(V("mt", 0, 512), 0.0)
@@ -354,11 +440,16 @@ def rank_program(g, core, T, topo):
         x, qc, qs, la = ("xt", "x2", "x3")[r - 1], "qc%d" % r, "qs%d" % r, "la%d" % r
         for i, (lo, hi) in enumerate(XP):
             quant(V(qc, lo, hi), V(qs, lo, hi), V(x, 4 * lo, 4 * hi))
-            mm(V("pb%d" % i, 0, hi - lo), [(V("uq"), V("uqs"), V(qc, lo, hi), V(qs, lo, hi))])
-            signs(V("bw", lo, hi), V("pb%d" % i, 0, hi - lo))
-        j = send(r, V("rc%d" % r, *XP[0]), V(qc, *XP[0]), True, 4000.0)
-        j = send(r, V("rs%d" % r), V(qs), False, 4300.0, (j,))
-        j = send(r, V("rc%d" % r, *XP[1]), V(qc, *XP[1]), True, 4900.0, (j,))
+            mm(V("pb%d" % i, 0, hi - lo), [(V("uq" if TUNE["two"] else "uc"), V("uqs" if TUNE["two"] else "ucs"), V(qc, lo, hi), V(qs, lo, hi))])
+            if TUNE["two"]:
+                signs(V("bw", lo, hi), V("pb%d" % i, 0, hi - lo), True)
+            elif TUNE["sg"] == 0.5:
+                ts(V("bw", lo, hi), V("pb%d" % i, 0, hi - lo), 0.0, 0.5, A.is_gt, A.subtract)
+            else:
+                signs(V("bw", lo, hi), V("pb%d" % i, 0, hi - lo))
+        j = ()
+        for i, (via, codes, lo, hi, takes) in enumerate(ROUTES):
+            j = (send(r, "r_%d_%d" % (r, i), V(("rc%d" if codes else "rs%d") % r, lo, hi), V(qc if codes else qs, lo, hi), codes, takes, j, via),)
         done = None
         for lo, hi in MP:
             for n in range(4):
@@ -367,31 +458,52 @@ def rank_program(g, core, T, topo):
             blocks = range((PAD + lo) // 128 if lo else 0, (PAD + hi) // 128)
             done = mm(V("pb6", 0, 128), [(V("mq", 128 * c, 128 * c + 128), V("mqs", 128 * c, 128 * c + 128), V("b2", 12 - 4 * c, 140 - 4 * c), V("b2s", 12 - 4 * c, 140 - 4 * c)) for c in blocks],
                       start=lo == 0, stop=hi == C, behind=() if done is None else (done,))
-        for s, val in enumerate((0.5, 1.5, 3.0, 3.0)):
-            ts(V("dv", s, 28 * L, L), V("pb6", s, 112, 4), val, None, A.mult)
+        if TUNE["d3"]:
+            tab = V("pb6", 0, 112)
+            add(costs("V", tab, (tab,), None), [tab], [V("d3", 0, 28 * L)], lambda e, q, tab=tab: e.tensor_scalar(T["d3"][:, :, 0:4], ap(tab), 0.5, None, A.mult))
+        else:
+            for s, val in enumerate((0.5, 1.5, 3.0, 3.0)):
+                ts(V("dv", s, 28 * L, L), V("pb6", s, 112, 4), val, None, A.mult)
         masked = {}
         for pair in PAIRS:
             for k in pair:
-                scan(V("sc", 64 * k, 64 * k + 4 * L), V("sc", 64 * k - 61, 64 * k - 61 + 4 * L) if k else V("dv", 28 * L + 3, 32 * L + 3), V("dv", 4 * L * k, 4 * L * k + 4 * L),
+                scan(V("sc", 64 * k, 64 * k + 4 * L), V("sc", 64 * k - 61, 64 * k - 61 + 4 * L) if k else V("c0", 3, 4 * L + 3) if TUNE["d3"] else V("dv", 28 * L + 3, 32 * L + 3),
+                     V("d3" if TUNE["d3"] else "dv", 4 * L * k, 4 * L * k + 4 * L),
                      behind=masked.get(k - 2, ()))
             k, n = pair[0], len(pair)
+            if k < TUNE["early"]:
+                for k in pair:
+                    for t in range(4):
+                        move(V("at", 64 * k + 64 + t, 64 * k + 128, 4), V("maska", 0, 64, 4), scale=V("sc", 64 * k + L * t + 5, 64 * k + L * t + 6), qs="A")
+                continue
             masked[pair[-1]] = (tt(V("at", 64 * k + 64, 64 * (k + n) + 64), V("sc", 64 * k, 64 * (k + n)), V("maska", 0, 64 * n), A.mult, lst=V("la4", 0, 4 * n)),)
         quant(V("aq"), V("aqs"), V("at"))
         mm(V("pb7", 0, 128), [(V("aq"), V("aqs"), V("b3"), V("b3s"))])
-        tt(V("ph"), V("pb7", 0, 4 * NL), V("thr"), A.is_ge)
-        scan(V("sl"), V("ph"), V("cs"))
-        ts(V(la), V("sl", 3, 4 * NL, 4), SC, MID + 0.25, A.mult, A.add)
-        send(r, V("lp%d" % r), V(la), False, TUNE["fly"])
+        if TUNE["poly"]:
+            scan(V("sl"), V("pb7", 0, 4 * NL), V("cs"))
+        else:
+            tt(V("ph"), V("pb7", 0, 4 * NL), V("thr"), A.is_ge)
+            scan(V("sl"), V("ph"), V("cs"))
+        ts(V(la), V("sl", 3, 4 * NL, 4), col(10) if TUNE["poly"] else SC, MID + 0.25, A.mult, A.add)
+        send(r, "r_l%d" % r, V("lp%d" % r), V(la), False, TUNE["fly"])
         lent = LENT[r - 1]
         banks = [k for k in (2, 3, 4, 5, 1, 0, 6, 7) if k not in [HOLD[b] for b in lent]]
-        mm(V("pb0", 0, C), [(V("uc"), V("ucs"), V(qc), V(qs))], after=(done,) if TUNE["after"] > 1 else ())
-        signs(V("scw"), V("pb0", 0, C), LESS)
+        sw = V("scw" if TUNE["two"] else "bw")
+        if TUNE["two"]:
+            mm(V("pb0", 0, C), [(V("uc"), V("ucs"), V(qc), V(qs))])
+            signs(sw, V("pb0", 0, C))
+        else:
+            dma("S", [], [V("bw")], lambda: [(T["bw"][1::16, :], T["bw"][0::16, :])], TUNE["row"])
         unpack("fb", qc, qs, ((0, C),), banks[:-3], lent, (done,) if TUNE["after"] else ())
         unpack("fp", "rc%d" % r, "rs%d" % r, FP, banks[:-2])
-        move(V("z"), V("scw"), lst=V(la), qs="A")
-        tt(V("u1"), V("scw"), V("dd"), A.mult, lst=V(la))
+        move(V("z"), sw, lst=V(la), scale=TUNE["sg"] ** -2, qs=TUNE["zq"])
+        tt(V("u1"), sw, V("dd"), A.mult, lst=V(la))
         tt(V("dd"), V("z"), V("u1"), A.mult, lst=V("lm"))
-        tt(V("tb"), V("s2"), V("dd"), A.subtract)
+        if TUNE["sum"][r - 1]:
+            dma("S", [V("s2")], [V("tb")], lambda: [(ap(V("tb")), ap(V("s2")))])
+            dma("G", [V("dd")], [V("tb")], lambda: [(ap(V("tb")), ap(V("dd")))], TUNE["adds"], adds=True)
+        else:
+            tt(V("tb"), V("s2"), V("dd"), A.add)
         if r == 3:
             move(V("pl_t", 0, C), V("place"), lst=V(la), plus=CMID)
             move(V("pl_t", C, 2 * C), V("tb"), scale=0.5, plus=CMID)
@@ -437,7 +549,7 @@ def rank_program(g, core, T, topo):
         for j in o["deps"]:
             users[j].append(i)
 
-    def place(rank_of, before, after, back):
+    def place(rank_of, before, after, back, pin=None):
         busy = {k: [] for k in "VAPGS"}
         start, end, free, qof = [None] * n, [None] * n, [None] * n, [None] * n
         left = [len(before[i]) for i in range(n)]
@@ -449,24 +561,42 @@ def rank_program(g, core, T, topo):
             late = o.get("late", 0.0)
             best = None
             for q, c in o["cost"].items():
-                t = max([(free[j] + late if back else end[j]) + WAKE if wait is True or (wait and qof[j] != q) else free[j] for j, wait in before[i].items()] + [late if back else 0.0])
-                for s, e in busy.get(q, ()):
-                    if t + c <= s:
-                        break
-                    t = max(t, e)
+                if pin and pin[i] not in (None, q):
+                    continue
+                t = max([(free[j] + late if back else end[j]) + (SAME if qof[j] == q else WAKE) if wait is True or (wait and qof[j] != q) else free[j] for j, wait in before[i].items()] + [late if back else 0.0])
+                taken = busy.get(q, ())
+                k, hi = 0, len(taken)
+                while k < hi:
+                    if taken[(k + hi) // 2][1] <= t:
+                        k = (k + hi) // 2 + 1
+                    else:
+                        hi = (k + hi) // 2
+                while k < len(taken) and t + c > taken[k][0]:
+                    t = max(t, taken[k][1])
+                    k += 1
                 worth = t + c + (TUNE["spare"] * c if q == "V" else 0.0)
                 if best is None or worth < best[0]:
-                    best = (worth, t + c, t, q)
-            free[i], start[i], qof[i] = best[1:]
+                    best = (worth, t + c, t, q, k)
+            free[i], start[i], qof[i] = best[1:4]
             end[i] = free[i] + (0.0 if back else late)
             if qof[i] in busy:
-                busy[qof[i]].append((start[i], free[i]))
-                busy[qof[i]].sort()
+                busy[qof[i]].insert(best[4], (start[i], free[i]))
             for u in after[i]:
                 left[u] -= 1
                 if not left[u]:
                     ready.append(u)
         return max(end), start, end, qof
+
+    def replay(plan, by_queue, slow, wake):
+        qof, free, end, left = plan[3], {}, [0.0] * n, [0.0] * n
+        for i in sorted(range(n), key=lambda j: (plan[1][j], j)):
+            q = qof[i]
+            t = max([end[j] + wake if wait is True or (wait and qof[j] != q) else left[j] for j, wait in fore[i].items()] + [free.get(q, 0.0)])
+            left[i] = t + ops[i]["cost"][q] * by_queue.get(q, 1.0)
+            end[i] = left[i] + ops[i].get("late", 0.0) * slow
+            if q != "R":
+                free[q] = left[i]
+        return max(end)
 
     fore = [o["deps"] for o in ops]
     aft = [{u: ops[u]["deps"][i] for u in users[i]} for i in range(n)]
@@ -477,9 +607,34 @@ def rank_program(g, core, T, topo):
     plans = PLANS
     for turn in range(0 if plans else TUNE["turns"]):
         plans.append(place(prio, fore, aft, False))
-        last = min(plans, key=lambda p: p[0]) if TUNE["noise"] else plans[-1]
-        prio = [p + o["bias"] + TUNE["noise"]() if TUNE["noise"] else p + o["bias"] for p, o in zip(place(last[2], aft, fore, True)[2], ops)]
-    span, start, end, qof = min(plans, key=lambda p: p[0])
+        prio = [p + o["bias"] for p, o in zip(place(plans[-1][2], aft, fore, True)[2], ops)]
+    if len(plans) == TUNE["turns"]:
+        seed = [TUNE["seed"]]
+
+        def rnd():
+            seed[0] = (seed[0] * 1103515245 + 12345) % 2 ** 31
+            return seed[0] / 2.0 ** 31
+        top = min(plans, key=lambda p: p[0])
+        best = top[0] + sum(replay(top, *case) for case in CASES)
+        for turn in range(TUNE["climb"]):
+            at, wide, amp = rnd() * top[0], TUNE["win"][0] + TUNE["win"][1] * rnd(), TUNE["win"][2] + TUNE["win"][3] * rnd()
+            pin = [None if at <= s < at + wide and rnd() < TUNE["win"][4] else q for s, q in zip(top[1], top[3])] if TUNE["pin"] else None
+            if TUNE["win"][5]:
+                k = min(range(n), key=lambda j: abs(top[1][j] - at) if len(ops[j]["cost"]) > 1 else 1e9)
+                if rnd() < TUNE["win"][5]:
+                    pin[k] = [q for q in ops[k]["cost"] if q != top[3][k]][0]
+            one = place([-s + (amp * rnd() if at <= s < at + wide else amp / 2) for s in top[1]], fore, aft, False, pin)
+            if not pin and turn % 2:
+                one = place(place(one[2], aft, fore, True)[2], fore, aft, False)
+            if pin and turn % 4 == 3:
+                one = place(place(one[2], aft, fore, True, one[3])[2], fore, aft, False, one[3])
+            if one[0] <= top[0] + TUNE["slack"]:
+                mark = one[0] + sum(replay(one, *case) for case in CASES)
+                if mark <= best:
+                    top, best = one, mark
+        plans.append(top)
+        TUNE["mark"] = round(best)
+    span, start, end, qof = plans[-1]
     TUNE["span"] = [round(p[0]) for p in plans]
 
     eng = {"V": g.vector, "A": g.scalar, "P": g.tensor, "G": g, "S": g.sync}

@@ -1,23 +1,23 @@
-from concourse.bass import DstId, RemoteDMATransfer
-from concourse.mybir import dt, AluOpType, ActivationFunctionType
+import math
+from concourse.mybir import dt, AluOpType, ActivationFunctionType, AxisListType
 
 C = 416
 NL = C // 16
-PAD = 512 - C
 MID = C // 2
 L = 14
+GT = 28
 STEP = (1, 2, 3)
 XP = ((0, 288), (288, C))
-MP = ((0, 288), (288, C))
 ZP = ((0, 224), (224, C))
 FP = XP
-ROUTES = ((None, True, 0, 288, 3500.0), (None, False, 0, C, 3850.0), (None, True, 288, C, 5000.0))
-NEAR = (True, True, True)
+MQ = ((0, 1), (2,), (3,))
+ROUTES = ((True, 0, 288), (False, 0, C), (True, 288, C))
 TP = (((0, 192), (192, C)),) * 3
 HOLD = (3, 3, 4, 5)
 LENT = ((3,),) * 3
-PAIRS = ((0, 1), (2, 3), (4, 5), (6,))
+AT = ((0, 3), (3, 6), (6, 7))
 F32, BF16, I32, U16, CODE, U8 = "float32", "bfloat16", "int32", "uint16", "float8_e4m3fn_x4", "uint8"
+MW = 512
 
 SCRATCH, PART = {}, {}
 
@@ -34,33 +34,33 @@ def _parts(whole, cols, dtype, *names):
 
 
 _buf(512, F32, *["pb%d" % i for i in range(8)], where="psum")
-_buf(2, I32, "ip")
-_buf(4, I32, "ib")
 _buf(16, F32, "cols")
-_buf(8, F32, "sp0", "sp1", "sp", "ih")
-_buf(16, BF16, "pat", "j16", "t16", "n16", "k16")
-_buf(2, BF16, "hc")
-_buf(128, BF16, "im", "maska")
-_buf(4 * NL, F32, "thr", "ph", "sl", "cs")
+_buf(128, BF16, "k0", "k1", "k2", "k3")
+_buf(4 * GT, BF16, "sp0", "sp1", "sp")
 _buf(8, I32, "iu")
-_buf(8, U16, "lu0", "la4")
+_buf(8, U16, "lu0")
 _buf(NL, U16, "lq")
 _parts("li", NL, I32, "kgw", "pgw", "mgw")
-_parts("lu", NL, U16, "l0", "lpw", "lm")
+_parts("lu", NL, U16, "l0", "lpw", "lm", "lm3")
 _parts("lists", NL, U16, "l1", "l2", "l3")
-_buf(C, BF16, "place", "kb", "bw", "scw", "z", "pa", "p2")
-_buf(C, F32, "yt", "tb", "s2", "dd", "u1", "kk0", "kk1", "kk2", "kk3")
-_buf(520, BF16, "w1")
-_buf(560, BF16, "w2", "ones")
-_buf(512, BF16, "i3", "w3", "ut", "vt", "at")
+_buf(C, BF16, "place", "kb", "scw", "z1", "z2", "z3", "zc")
+_buf(3 * C, BF16, "tb", "bw", "swap", "trio")
+_buf(C, F32, "yt", "kk0", "kk1", "kk2", "kk3")
+_buf(520, BF16, "w1", "ones")
+_buf(4 * (3 * GT + 128), BF16, "w2")
+_buf(512, BF16, "w3", "ut", "vt", "at")
 _buf(32 * L + 4, F32, "dv")
-_buf(4 * L + 4, F32, "c0")
-SCRATCH["d3"] = ("sbuf", [128, 28, L], F32)
 _buf(448, F32, "sc")
+_buf(64, BF16, "f0", "f1", "f2")
+_buf(28, U16, "la4")
 _buf(2 * C, F32, "pl_t")
+_buf(4 * NL, F32, "sl")
+_buf(8 * NL, F32, "cs")
+_buf(2 * NL, F32, "su")
+_buf(NL, F32, "sf", "d3")
 _buf(4 * C, BF16, "xt", "x2", "x3", "x4", "zt")
-_buf(2048, BF16, "mt")
-for _c, _s, _n in (("uq", "uqs", 128), ("uc", "ucs", 128), ("vq", "vqs", 128), ("wq", "wqs", 512), ("b2", "b2s", 140), ("b3", "b3s", 128), ("mq", "mqs", 512), ("aq", "aqs", 128), ("zq", "zqs", C)):
+_buf(4 * MW, BF16, "mt")
+for _c, _s, _n in (("uq", "uqs", 128), ("uc", "ucs", 128), ("vq", "vqs", 128), ("wq", "wqs", 512), ("b2", "b2s", 3 * GT + 128), ("b3", "b3s", 128), ("mq", "mqs", MW), ("aq", "aqs", 128), ("zq", "zqs", C)):
     _buf(_n, CODE, _c)
     _buf(_n, U8, _s)
 _parts("ec", 128, CODE, *["e%d" % i for i in range(4)])
@@ -70,9 +70,6 @@ _parts("fb", C, BF16, *["fb%d" % i for i in range(4)])
 _parts("fp", C, BF16, *["fp%d" % i for i in range(4)])
 _parts("tg", C, BF16, "tg1", "tg2", "tg3")
 _parts("tsum", C, BF16, "ts0", "ts1", "ts2", "ts3")
-_buf(3 * NL, F32, "df")
-_buf(2 * NL, F32, "ef")
-_buf(NL, F32, "sf", "sg")
 for _i in (1, 2, 3, 4):
     _buf(C, CODE, "qc%d" % _i)
     _buf(C, U8, "qs%d" % _i)
@@ -83,63 +80,40 @@ for _i in (1, 2, 3):
 
 SEMAPHORES = ["s_v", "s_a", "s_p", "s_g", "loc"] + ["d_%d" % i for i in range(40)] + ["r_%d_%d" % (r, i) for r in (1, 2, 3) for i in range(8)] + ["r_l%d" % r for r in (1, 2, 3)]
 
-WAKE = 80.0
-SAME = 90.0
-CY = 0.82
-GY = 1.33
-AY = 1.17
-PY = 0.97
-QY = 0.279
-FIX = (87.0, 83.0, 37.0, 58.0, 52.0, 25.0)
+NAMES = ("f", "g", "wake", "same", "vfix", "afix", "least", "aleast", "gv", "ar", "pe", "pfix", "rem", "remb", "first", "issue", "dma", "dmab")
+CASES = [dict(zip(NAMES, c)) for c in (
+    (1.09, 1.60, 200.0, 125.0, 10.0, 70.0, 35.0, 15.0, 35.0, 0.90, 0.45, 90.0, 1400.0, 150.0, 1400.0, 100.0, 1100.0, 215.0),
+    (1.25, 0.95, 190.0, 225.0, 3.0, 39.0, 30.0, 14.0, 55.0, 1.00, 0.62, 75.0, 850.0, 120.0, 850.0, 75.0, 1750.0, 220.0),
+    (1.40, 0.86, 63.0, 174.0, 18.0, 18.0, 57.0, 0.0, 30.0, 1.20, 0.46, 33.0, 1300.0, 148.0, 650.0, 30.0, 1150.0, 350.0),
+    (1.09, 2.06, 139.0, 273.0, 44.0, 37.0, 32.0, 64.0, 74.0, 1.13, 0.42, 80.0, 1500.0, 80.0, 1290.0, 217.0, 2200.0, 307.0))]
 PLANS = []
-CASES = (({"V": 1.25, "A": 1.25, "P": 1.5, "G": 1.3, "R": 1.5}, 1.3, 120.0), ({"V": 0.9, "A": 0.85, "R": 1.3}, 1.0, 70.0))
-TUNE = {"bias": 0.0, "d3": 0, "win": (300.0, 1000.0, 300.0, 1000.0, 0.2, 0.3), "poly": 1, "slack": 300.0, "spare": 0.1, "sg": 1.0, "two": 1, "gfill": 1, "pin": 1, "zq": "VA", "row": 1600.0, "first": 1100.0, "l0": 1550.0, "turns": 4, "fly": 1400.0, "setup": 1, "early": 2, "sum": (0, 0, 1), "adds": 2600.0, "after": 0, "seed": 1, "climb": 6000, "land": (2050.0, 3100.0, 3600.0, 3700.0, 4600.0, 4800.0, 5300.0)}
+TUNE = {"tries": 90000, "heat": 300.0, "way": 0.8, "change": 0.3, "hops": 4, "spare": 0.1, "turns": 4, "seed": 1}
+
+
+def _price(m, kind, n=0.0):
+    cycle = 0.83 * m["f"]
+    return {"V": m["vfix"] + max(m["least"], n) * cycle, "A": m["afix"] + max(m["aleast"], n) * cycle * m["ar"],
+            "gV": m["gv"] + n * m["g"], "gA": m["gv"] + 15.0 + n * m["g"] * m["ar"], "G": 150.0 + 2.0 * n * cycle,
+            "quant": m["vfix"] + (12.0 + 0.22 * n) * m["f"], "P": m["pfix"] + (n + 16.0) * m["pe"], "start": 60.0 * n,
+            "send": m["issue"] + n * m["first"], "fly": m["rem"] - m["wake"], "link": n / m["remb"], "dma": m["dma"] + n / m["dmab"], "none": 0.0}[kind]
 
 
 def _hit(a, b):
     if a[1] >= b[2] or b[1] >= a[2]:
         return False
-    if a[3] == b[3] and a[3] > 1:
-        return a[1] % a[3] == b[1] % a[3]
+    common = min(a[3], b[3])
+    if common > 1 and max(a[3], b[3]) % common == 0:
+        return a[1] % common == b[1] % common
     return True
-
-
-def _carriers(T, topo, core):
-    able = [c for c in topo.cores_of(core) if T.rank_of(c) is None and all(topo.may_write(c, o) for o in T.cores if o != core)]
-    return sorted(able, key=lambda c: topo.die(c) != topo.die(core))
-
-
-def _near_engines(T, topo, core, via):
-    far = topo.engines(core, [o for o in T.cores if o != core][0])
-    return [n for n in topo.engines(core, _carriers(T, topo, core)[via]) if (n in far) != NEAR[via]]
-
-
-def carrier_program(g, core, T, topo):
-    for home in T.cores:
-        mine = _carriers(T, topo, home)
-        if core not in mine:
-            continue
-        sent = 0
-        for r in (1, 2, 3):
-            to = T.cores[T.rank_of(home) ^ STEP[r - 1]]
-            for i, (via, codes, lo, hi, takes) in enumerate(ROUTES):
-                if via == mine.index(core):
-                    sem = T.sem["r_%d_%d" % (r, i)]
-                    piece = T["rc%d" % r][:, lo:hi].bitcast(dt.uint8) if codes else T["rs%d" % r][:, lo:hi]
-                    g.wait_ge(sem, len(_near_engines(T, topo, home, via)))
-                    g.remote_dma(piece, piece, sem, T.sem["loc"], topo.addr(to)[1], topo.addr(to)[0], topo.mask(core, to))
-                    sent += len(topo.engines(core, to))
-        if sent:
-            g.wait_ge(T.sem["loc"], sent)
 
 
 def rank_program(g, core, T, topo):
     rank = T.rank_of(core)
     if rank is None:
-        return carrier_program(g, core, T, topo)
+        return
     A = AluOpType
     AF = ActivationFunctionType
-    ops, seen, bias = [], {}, [0.0]
+    ops, seen = [], {}
 
     def V(name, lo=0, hi=None, st=1):
         whole, at, cols = PART.get(name, (name, 0, SCRATCH.get(name, (0, (0, 0)))[1][1]))
@@ -148,8 +122,6 @@ def rank_program(g, core, T, topo):
     def ap(v):
         if not isinstance(v, tuple):
             return v
-        if v[0] == "d3":
-            return T["d3"][:, v[1] // L:v[2] // L, :] if v[3] == 1 else T["d3"][:, :, v[1]]
         return T[v[0]][:, v[1]:v[2]] if v[3] == 1 else T[v[0]][:, v[1]:v[2]:v[3]]
 
     def src(v, l):
@@ -176,7 +148,7 @@ def rank_program(g, core, T, topo):
             deps[j] = True
         for j in behind:
             deps[j] = False
-        ops.append({"cost": cost, "deps": deps, "emit": emit, "kind": kind, "sem": sem, "amount": amount, "bias": bias[0]})
+        ops.append({"cost": cost, "deps": deps, "emit": emit, "kind": kind, "sem": sem, "amount": amount})
         return i
 
     def narrow(*views):
@@ -185,31 +157,31 @@ def rank_program(g, core, T, topo):
     def costs(qs, out, ins, lst, both=False):
         n = n_of(out)
         if lst is not None:
-            c = {"V": FIX[0] + n * GY, "A": FIX[1] + n * GY * AY}
+            c = {"V": ("gV", n), "A": ("gA", n)}
         else:
-            c = {"V": max(64.0, n * (2.0 if both else 0.5 if narrow(out, *ins) else 1.0)) * CY + FIX[2], "A": max(64.0, n) * CY * AY + FIX[3]}
+            c = {"V": ("V", n * (2.0 if both else 0.5 if narrow(out, *ins) else 1.0)), "A": ("A", n)}
         return {q: c[q] for q in qs}
 
-    def ts(out, in0, s1, s2, op0, op1=None, lst=None, behind=()):
+    def ts(out, in0, s1, s2, op0, op1=None, lst=None):
         def emit(e, q):
             if op1 is None:
                 return e.tensor_scalar(ap(out), src(in0, lst), ap(s1), None, op0)
             return e.tensor_scalar(ap(out), src(in0, lst), ap(s1), ap(s2), op0, op1)
-        return add(costs("V", out, (in0, s1, s2), lst), [in0, lst, s1, s2], [out], emit, behind=behind)
+        return add(costs("V", out, (in0, s1, s2), lst), [in0, lst, s1, s2], [out], emit)
 
     def tt(out, in0, in1, op, lst=None):
         both = not (in0[0].startswith("pb") or in1[0].startswith("pb"))
         return add(costs("V", out, (in0, in1, V("cols")), lst, both), [in0, in1, lst], [out], lambda e, q: e.tensor_tensor(ap(out), src(in0, lst), ap(in1), op))
 
-    def scan(out, d0, d1, first=0.0, behind=()):
-        return add(costs("V", out, (d0, d1), None), [d0, d1], [out], lambda e, q: e.tensor_tensor_scan(ap(out), ap(d0), ap(d1), first, A.mult, A.add), behind=behind)
+    def scan(out, d0, d1, first=0.0):
+        return add(costs("V", out, (d0, d1), None), [d0, d1], [out], lambda e, q: e.tensor_tensor_scan(ap(out), ap(d0), ap(d1), first, A.mult, A.add))
 
     def move(out, in_, lst=None, scale=None, plus=None, relu=False, qs="VA"):
         def emit(e, q):
             o, i = ap(out), src(in_, lst)
             if q == "V":
                 if relu:
-                    return e.tensor_scalar(o, i, 0.0, None, A.is_gt)
+                    return e.tensor_scalar(o, i, 0.0, scale, A.is_gt, A.mult)
                 if scale is None and plus is None:
                     return e.tensor_copy(o, i)
                 if plus is None:
@@ -217,20 +189,25 @@ def rank_program(g, core, T, topo):
                 if scale is None:
                     return e.tensor_scalar(o, i, ap(plus), None, A.add)
                 return e.tensor_scalar(o, i, ap(scale), ap(plus), A.mult, A.add)
+            if relu:
+                return e.activation(o, i, AF.Relu, scale=scale)
             if plus is not None:
                 return e.activation(o, i, AF.Identity, bias=ap(plus), scale=1.0 if scale is None else ap(scale))
             if scale is not None:
                 return e.activation(o, i, AF.Copy, scale=ap(scale))
-            return e.activation(o, i, AF.Relu, scale=1.0 / TUNE["sg"]) if relu else e.activation(o, i, AF.Copy)
+            return e.activation(o, i, AF.Copy)
         return add(costs(qs, out, (in_, scale, plus), lst), [in_, lst, scale, plus], [out], emit)
 
     def signs(out, in_, loose=False):
         if loose:
             return add(costs("VA", out, (in_,), None), [in_], [out], lambda e, q: e.tensor_scalar(ap(out), ap(in_), 0.0, None, A.is_gt) if q == "V" else e.activation(ap(out), ap(in_), AF.Sign))
-        return add(costs("A", out, (in_,), None), [in_, TINY], [out], lambda e, q: e.activation(ap(out), ap(in_), AF.Sign, bias=ap(TINY)))
+        return add(costs("VA", out, (in_,), None), [in_, TINY], [out],
+                   lambda e, q: e.tensor_scalar(ap(out), ap(in_), 0.0, 0.5, A.is_gt, A.subtract) if q == "V" else e.activation(ap(out), ap(in_), AF.Sign, bias=ap(TINY)))
 
     def fill(out, val, qs="VAG"):
         ones = V("ones", 0, n_of(out))
+        if val != int(val):
+            qs = qs.replace("G", "")
         def emit(e, q):
             if q == "V":
                 return e.memset(ap(out), val)
@@ -238,12 +215,12 @@ def rank_program(g, core, T, topo):
                 return e.iota(ap(out), [[0, n_of(out)]], int(val), 0, allow_small_or_imprecise_dtypes=True)
             return e.activation(ap(out), ap(ones), AF.Copy, scale=val)
         cost = costs(qs.replace("G", ""), out, (), None)
-        if "G" in qs and TUNE["gfill"]:
-            cost["G"] = 160 + 2 * n_of(out) * CY
+        if "G" in qs:
+            cost["G"] = ("G", n_of(out))
         return add(cost, [ones] if "A" in qs else [], [out], emit)
 
     def quant(c, s, t):
-        return add({"V": FIX[4] + QY * n_of(t)}, [t], [c, s], lambda e, q: e.quantize_mx(ap(c), ap(s), ap(t)))
+        return add({"V": ("quant", n_of(t))}, [t], [c, s], lambda e, q: e.quantize_mx(ap(c), ap(s), ap(t)))
 
     def mm(out, terms, after=(), start=True, stop=True, behind=()):
         def emit(e, q):
@@ -251,187 +228,141 @@ def rank_program(g, core, T, topo):
             for k, (a, b, c, d) in enumerate(terms):
                 last = e.matmul_mx(ap(out), ap(a), ap(b), ap(c), ap(d), start and k == 0, stop and k == len(terms) - 1)
             return last
-        return add({"P": ((n_of(out) + 16) * PY + FIX[5]) * len(terms)}, [v for t in terms for v in t], [out], emit, after=after, behind=behind)
+        return add({"P": [("P", n_of(out))] * len(terms)}, [v for t in terms for v in t], [out], emit, after=after, behind=behind)
 
     def iota(out, pattern, base, cm):
         def emit(e, q):
             if SCRATCH[out[0]][2] != I32:
                 return e.iota(ap(out), pattern, base, cm, allow_small_or_imprecise_dtypes=True)
             return e.iota(ap(out), pattern, base, cm)
-        return add({"G": 160 + 2 * n_of(out) * CY}, [], [out], emit)
+        return add({"G": ("G", n_of(out))}, [], [out], emit)
 
     def keep(out, in_, pattern, op, base, cm, other=0.0):
-        return add({"G": 210 + 2 * n_of(out) * CY}, [in_], [out], lambda e, q: e.affine_select(ap(out), ap(in_), pattern, op, other, base, cm))
+        return add({"G": ("G", n_of(out) + 20)}, [in_], [out], lambda e, q: e.affine_select(ap(out), ap(in_), pattern, op, other, base, cm))
 
-    dcount, rcount, sent = [0], [0], [0]
+    dcount, lands, sent = [0], [], [0]
 
-    def dma(q, reads, writes, pairs, cost=2000.0, behind=(), adds=False):
+    def dma(q, reads, writes, pairs, ahead, behind=()):
         sem = "d_%d" % dcount[0]
         dcount[0] += 1
         def emit(e, q):
             for o, i in pairs():
-                (e.dma_start(o, i, accum_op=A.add) if adds else e.dma_start(o, i)).then_inc(T.sem[sem], 16)
-        i = add({q: (1000.0 if adds else 60.0) * len(pairs())}, reads, writes, emit, "d", sem, 16 * len(pairs()), behind=behind)
-        ops[i]["late"] = cost
+                e.dma_start(o, i).then_inc(T.sem[sem], 16)
+        i = add({q: ("start", len(pairs()))}, reads, writes, emit, "d", sem, 16 * len(pairs()), behind=behind)
+        ops[i]["late"] = ("dma", ahead)
         return i
 
-    def send(r, sem, dst_v, src_v, codes, latency, behind=(), via=None):
-        far = T.cores[rank ^ STEP[r - 1]]
-        to, used = far, topo.engines(core, far)
-        lands = len(used)
-        if via is not None:
-            to, used = _carriers(T, topo, core)[via], _near_engines(T, topo, core, via)
-            lands = len(topo.engines(_carriers(T, topo, far)[via], core))
+    def send(r, sem, dst_v, src_v, codes, behind=()):
+        to = T.cores[rank ^ STEP[r - 1]]
         def emit(e, q):
             o, i = (ap(dst_v).bitcast(dt.uint8), ap(src_v).bitcast(dt.uint8)) if codes else (ap(dst_v), ap(src_v))
-            e.remote_dma(o, i, T.sem[sem], T.sem["loc"], topo.addr(to)[1], topo.addr(to)[0], sum(1 << n for n in used))
-            sent[0] += len(used)
-        j = add({"G": 150.0 if rcount[0] else TUNE["first"]}, [src_v], [], emit, "s", behind=behind)
-        rcount[0] += 1
-        add({"R": latency}, [], [dst_v], None, "r", sem, lands, after=(j,))
+            e.remote_dma(o, i, T.sem[sem], T.sem["loc"], topo.addr(to)[1], topo.addr(to)[0], topo.mask(core, to))
+            sent[0] += len(topo.engines(core, to))
+        j = add({"G": ("send", 0 if lands else 1)}, [src_v], [], emit, "s", behind=behind)
+        ops[j]["late"] = ("fly",)
+        lands.append(add({"R": ("link", 128 * n_of(src_v) * (4 if codes else 2 if SCRATCH[src_v[0]][2] == U16 else 1))}, [], [dst_v], None, "r", sem, len(topo.engines(to, core)), after=(j,), behind=lands[-1:]))
         return j
 
     col = lambda i: V("cols", i, i + 1)
-    QC, SC, ISC, R4, LESS, CMID, TINY = [col(i) for i in range(7)]
-    HC = V("hc", 0, 1)
+    SC, ISC, SC2, CMID, TINY, OWN, SC3 = [col(i) for i in range(7)]
+    KG, PG, MG = V("kgw", 0, NL), V("pgw", 0, NL), V("mgw", 0, NL)
 
     a, b = XP[0][1], C
-    d0 = dma("S", [], [V("pgw")], lambda: [(ap(V("pgw")), T.pg[:, :])], TUNE["l0"])
-    d1 = dma("A", [], [V("kgw")], lambda: [(ap(V("kgw")), T.kg[:, :])], TUNE["l0"])
-    at = TUNE["land"]
+    d0 = dma("S", [], [PG], lambda: [(ap(PG), T.pg[:, :])], 26e3)
+    d1 = dma("A", [], [KG], lambda: [(ap(KG), T.kg[:, :])], 13e3)
+    at = (158e3, 453e3, 584e3, 597e3, 859e3, 925e3, 1056e3)
     d1 = dma("A", [], [V("ut")], lambda: [(T["ut"][:, :], T.u[:, :])], at[0], (d1,))
     d0 = dma("S", [], [V("xt", 0, 4 * a)], lambda: [(T["xt"][:, 0:4 * a], T.x[:, 0:4 * a])], at[1], (d0,))
     d1 = dma("A", [], [V("xt", 4 * a)], lambda: [(T["xt"][:, 4 * a:4 * b], T.x[:, 4 * a:4 * b])], at[2], (d1,))
-    d0 = dma("S", [], [V("mgw")], lambda: [(ap(V("mgw")), T.mg[:, :])], at[3], (d0,))
+    d0 = dma("S", [], [MG], lambda: [(ap(MG), T.mg[:, :])], at[3], (d0,))
     d0 = dma("S", [], [V("wq")], lambda: [(T["wq"][:, :].bitcast(dt.uint8), T.wc[:, :])], at[4], (d0,))
     d0 = dma("S", [], [V("wqs")], lambda: [(T["wqs"][:, :], T.ws[:, :])], at[5], (d0,))
     d0 = dma("S", [], [V("vt")], lambda: [(T["vt"][:, :], T.v[:, :])], at[6], (d0,))
 
-    ipv = V("ip", 0, 1)
-    ib = lambda i: V("ib", i, i + 1)
     fill(V("ones"), 1.0, "V")
     scan(V("place"), V("ones", 0, C), V("ones", 0, C), -MID - 1.0)
-    iota(ipv, [[0, 1]], 0, 1)
-    ts(ib(0), ipv, 15, None, A.bitwise_and)
-    ts(ib(1), ipv, 4, None, A.logical_shift_right)
-    ts(ib(2), ipv, 3, None, A.bitwise_and)
-    move(QC, ib(0), qs="V")
-    move(HC, ib(1), qs="V")
-    ts(R4, ib(2), float(L), 5.0, A.mult, A.add)
-    if TUNE["two"]:
-        fill(TINY, -2.0 ** -100, "V")
+    fill(TINY, -2.0 ** -100, "V")
     fill(CMID, float(MID), "V")
-    if TUNE["sg"] == 1.0 and not TUNE["two"]:
-        fill(TINY, -2.0 ** -100, "V")
-    ts(V("lq"), V("ones", 0, NL), QC, None, A.mult)
-    ts(V("j16"), V("place", MID, MID + 16), QC, None, A.subtract)
-    ts(V("t16"), V("j16"), 1.0, 2.0 ** 20, A.is_equal, A.mult)
-    ts(V("n16"), V("j16"), 0.0, None, A.not_equal)
-    tt(V("k16"), V("n16"), V("t16"), A.max)
-    move(V("kb"), V("k16"), lst=V("lq"))
-    ts(col(8), QC, 15.0, 2.0 ** -21 - 0.5, A.is_lt, A.mult)
-    ts(SC, col(8), 0.5, None, A.add)
-    ts(col(9), QC, 15.0, 2.0 ** 21 - 2.0, A.is_lt, A.mult)
-    ts(ISC, col(9), 2.0, None, A.add)
-    move(V("lu", 0, 2 * NL), V("li", 0, 2 * NL), qs="V")
-    move(V("lm"), V("mgw"), qs="V")
-    ts(V("ts0", 15, C, 16) if TUNE["poly"] else V("cs", 3, 4 * NL, 4), V("kgw"), -float(MID), ISC, A.add, A.mult)
-    if TUNE["poly"]:
-        move(col(10), SC, scale=1.0 / 6.0)
+    iota(OWN, [[0, 1]], 0, 1)
+    ts(V("lq"), V("ones", 0, NL), OWN, None, A.mult)
+    ts(V("k0"), V("place", MID, MID + 128), OWN, None, A.subtract)
+    ts(V("k2"), V("k0"), 1.0, 2.0 ** 20, A.is_equal, A.mult)
+    ts(V("k3"), V("k0"), 0.0, None, A.not_equal)
+    tt(V("k1"), V("k2"), V("k3"), A.max)
+    move(V("kb"), V("k1"), lst=V("lq"))
+    add(costs("V", ISC, (), None), [V("kb", 0, 16)], [ISC], lambda e, q: e.tensor_reduce(ap(ISC), ap(V("kb", 0, 16)), AxisListType.X, A.max))
+    ts(SC, ISC, 1.0, 2.0 ** -20, A.is_equal, A.max)
+    move(SC2, SC, scale=0.5)
+    move(SC3, SC, scale=3.0)
+    move(V("lpw"), PG, qs="V")
+    ts(V("l0"), KG, 3.0, 2.0, A.mult, A.add)
+    move(V("lm"), MG, qs="V")
+    ts(V("lm3"), MG, 3.0, 2.0, A.mult, A.add)
+    ts(V("ts0", 15, C, 16), KG, -float(MID), ISC, A.add, A.mult)
 
-    def listed(n):
-        scan(V("ts%d" % n), V("kb"), V("tg%d" % n))
-        now = V("ts%d" % n, 15, C, 16)
-        ts(V("l%d" % n), now, SC, MID + 0.25, A.mult, A.add)
-        if TUNE["poly"]:
-            if n == 1:
-                move(V("cs", 3, 4 * NL, 4), now, scale=6.0)
-            if n == 3:
-                tt(V("df"), V("tsum", C + 15, 4 * C, 16), V("tsum", 15, 3 * C, 16), A.subtract)
-                tt(V("ef"), V("df", NL, 3 * NL), V("df", 0, 2 * NL), A.subtract)
-                tt(V("cs", 0, 4 * NL, 4), V("ef", NL, 2 * NL), V("ef", 0, NL), A.subtract)
-                move(V("cs", 1, 4 * NL, 4), V("ef", 0, NL), scale=3.0)
-                tt(V("sf"), V("df", 0, NL), V("df", NL, 2 * NL), A.add)
-                move(V("sg"), V("sf"), scale=3.0)
-                tt(V("cs", 2, 4 * NL, 4), V("sg"), V("cs", 0, 4 * NL, 4), A.subtract)
-            return
-        tt(V("cs", 3 - n, 4 * NL, 4), now, V("ts%d" % (n - 1), 15, C, 16) if n > 1 else V("cs", 3, 4 * NL, 4), A.subtract)
+    def lists():
+        for n in (1, 2, 3):
+            for lo, hi in TP[n - 1]:
+                move(V("tg%d" % n, lo, hi), V("tb"), lst=V("l%d" % (n - 1), lo // 16, hi // 16))
+            scan(V("ts%d" % n), V("kb"), V("tg%d" % n))
+            ts(V("l%d" % n), V("ts%d" % n, 15, C, 16), SC3, 3 * MID + 2.25, A.mult, A.add)
+        some = lambda n, k: V("tsum", n * C + 15, (n + k) * C, 16)
+        move(V("cs", 3, 8 * NL, 4), some(1, 2), scale=2.0)
+        tt(V("su"), some(0, 2), some(2, 2), A.add)
+        tt(V("cs", 1, 8 * NL, 4), V("su"), V("cs", 3, 8 * NL, 4), A.subtract)
+        tt(V("d3"), V("cs", 4 * NL + 1, 8 * NL, 4), V("cs", 1, 4 * NL, 4), A.subtract)
+        move(V("cs", 0, 4 * NL, 4), V("d3"), scale=1.0 / 3.0)
+        tt(V("sf"), some(2, 1), some(0, 1), A.subtract)
+        tt(V("cs", 2, 4 * NL, 4), V("sf"), V("cs", 0, 4 * NL, 4), A.subtract)
 
     for lo, hi in ((0, 224), (224, C)):
-        move(V("pa", lo, hi), V("place"), lst=V("lpw", lo // 16, hi // 16))
-    move(V("tg1"), V("pa"), lst=V("l0"), scale=2.0)
-    move(V("p2"), V("pa"), lst=V("lpw"))
-    listed(1)
-    move(V("tg2"), V("p2"), lst=V("l0"), scale=2.0)
-    listed(2)
-    move(V("tg3"), V("p2"), lst=V("l1"), scale=2.0)
-    listed(3)
-    if TUNE["setup"]:
-        move(V("s2"), V("pa"), lst=V("lm"))
-        move(V("dd"), V("s2"), scale=-1.0)
-        for name in ("dd", "s2"):
-            dma("G", [V("pa")], [V(name)], lambda name=name: [(ap(V(name)), ap(V("pa")))], TUNE["adds"], adds=True)
-    else:
-        move(V("z"), V("pa"), scale=-1.0)
-        tt(V("s2"), V("pa"), V("z"), A.subtract, lst=V("lm"))
-        tt(V("dd"), V("z"), V("pa"), A.add, lst=V("lm"))
+        move(V("tb", 3 * lo + 2, 3 * hi, 3), V("place"), lst=V("lpw", lo // 16, hi // 16))
+    lists()
+    move(V("trio", 0, 3 * C, 3), V("tb"), lst=V("lm3"))
+    move(V("trio", 1, 3 * C, 3), V("tb", 2, 3 * C, 3), scale=-1.0)
+    move(V("trio", 2, 3 * C, 3), V("tb", 2, 3 * C, 3))
+    fill(V("swap", 0, 3 * C, 3), 0.0)
+    fill(V("swap", 1, 3 * C, 3), 1.0)
     quant(V("uq"), V("uqs"), V("ut"))
     iota(V("iu"), [[16, 8]], 0, 0)
-    if TUNE["two"]:
-        move(V("lu0"), V("iu"), qs="V")
-    else:
-        ts(LESS, QC, 1.0, None, A.is_equal)
-        ts(V("lu0"), V("iu"), LESS, None, A.add)
+    move(V("lu0"), V("iu"), qs="V")
     add(costs("V", V("uc"), (), V("lu0")), [V("uq"), V("lu0")], [V("uc")], lambda e, q: e.tensor_copy(ap(V("uc")).bitcast(dt.uint32), ap(V("uq")).bitcast(dt.uint32).indirect(ap(V("lu0")))))
     add(costs("VA", V("ucs"), (), V("lu0")), [V("uqs"), V("lu0")], [V("ucs")],
         lambda e, q: e.tensor_copy(ap(V("ucs")), src(V("uqs"), V("lu0"))) if q == "V" else e.activation(ap(V("ucs")), src(V("uqs"), V("lu0")), AF.Copy))
     keep(V("w1"), V("ones", 0, 520), [[1, 520]], A.is_equal, -4, -4)
     for b in range(4):
         quant(V("e%d" % b), V("es%d" % b), V("w1", 4 - b, 516 - b))
-    iota(V("sp0"), [[-16, 8]], 1, 1)
-    keep(V("sp1"), V("sp0"), [[-16, 8]], A.is_ge, 0, 1)
-    keep(V("sp"), V("sp1"), [[16, 8]], A.is_ge, 1, -1)
-    fill(V("pat"), 0.0)
-    for lo, hi, st, val in ((0, 1, 1, -1.0), (1, 5, 3, 3.0), (2, 3, 1, -3.0), (3, 4, 1, 1.0), (5, 10, 4, -6.0), (6, 7, 1, 3.0), (10, 15, 4, 6.0)) if TUNE["d3"] else (
-            (0, 10, 9, -1.0), (1, 2, 1, 3.0), (2, 3, 1, -3.0), (3, 5, 1, 1.0), (5, 6, 1, -2.0), (6, 15, 4, 1.0)):
-        fill(V("pat", lo, hi, st), val)
-    fill(V("w2"), 0.0)
-    for k in range(7):
-        move(V("w2", 48 + 64 * k, 64 + 64 * k), V("pat"), scale=V("sp", k, k + 1))
+    iota(V("sp0"), [[-16, 7], [256, 4], [-256, 4]], 1, 1)
+    keep(V("sp1"), V("sp0"), [[-16, 7], [256, 4], [-256, 4]], A.is_ge, 0, 1)
+    keep(V("sp"), V("sp1"), [[16, 7], [-256, 4], [256, 4]], A.is_ge, 1, -1)
+    for s, val in enumerate((-1.0, 3.0, -6.0, 6.0)):
+        move(V("w2", 4 * GT * s, 4 * GT * (s + 1)), V("sp"), scale=val)
+    fill(V("w2", 16 * GT), 0.0)
     quant(V("b2"), V("b2s"), V("w2"))
-    iota(V("i3"), [[1, 32], [0, 4], [-8, 4]], PAD // 16, 0)
-    for t in range(4 if TUNE["poly"] else 0):
-        fill(V("i3", t, 512, 16), 99.0)
-    ts(V("w3"), V("i3"), HC, None, A.is_equal)
+    keep(V("w3", 0, C), V("ones", 0, C), [[4, NL], [0, 4], [1, 4]], A.is_equal, 0, -1)
+    fill(V("w3", C), 0.0)
+    for t in range(4):
+        fill(V("w3", t, C, 16), 0.0)
     quant(V("b3"), V("b3s"), V("w3"))
-    iota(V("im"), [[0, 2], [1, 16], [0, 4]], 0, 0)
-    ts(V("maska"), V("im"), QC, None, A.is_equal)
-    if not TUNE["poly"]:
-        iota(V("thr"), [[0, NL], [-1, 4]], 3, 0)
-    iota(V("ih"), [[64, 2], [0, 4]], 0, 0)
-    ts(V("la4"), V("ih"), R4, None, A.add)
-    if TUNE["d3"]:
-        fill(V("d3", 0, 28 * L), 0.0, "V")
-        for lo, val in ((5, -1.0), (6, -1.0), (7, 1.0 / 3.0), (8, 1.0), (9, 1.0)):
-            fill(V("d3", lo, 28 * L, L), val, "V" if val == 1.0 / 3.0 else "VAG")
-        fill(V("c0"), 0.0)
-        for lo, val in ((4, 1.0), (6, -1.0), (7, 1.0 / 3.0), (8, 1.0), (9, 1.0)):
-            fill(V("c0", lo, 4 * L, L), val, "V" if val == 1.0 / 3.0 else "VAG")
-    else:
-        fill(V("dv"), 0.0)
-        for lo, hi, val in ((5, 28 * L, -1.0), (6, 32 * L, -1.0), (7, 32 * L, 1.0 / 3.0), (8, 32 * L, 1.0), (9, 32 * L, 1.0), (28 * L + 4, 32 * L, 1.0)):
-            fill(V("dv", lo, hi, L), val, "V" if val == 1.0 / 3.0 else "VAG")
+    fill(V("dv"), 0.0)
+    for lo, hi, val in ((4, GT * L, -1.0), (5, 32 * L, -1.0), (6, GT * L, -1.0), (GT * L + 6, 32 * L, -2.0), (7, 32 * L, 1.0 / 36.0), (8, 32 * L, 1.0), (9, 32 * L, 1.0)):
+        fill(V("dv", lo, hi, L), val, "V" if lo == 7 else "VAG")
     fill(V("sc"), 0.0)
+    iota(V("f0"), [[0, 4], [L, 4], [0, 4]], 4, 0)
+    keep(V("f1"), V("f0"), [[1, 4], [0, 4], [-1, 4]], A.is_equal, 0, 0, 10.0)
+    scan(V("f2"), V("kb", 0, 64), V("f1"))
+    for k in range(max(hi - lo for lo, hi in AT)):
+        ts(V("la4", 4 * k, 4 * k + 4), V("f2", 15, 64, 16), SC, 64 * k + 0.25, A.mult, A.add)
     fill(V("at", 0, 64), 0.0)
-    fill(V("mt", 0, 512), 0.0)
-    quant(V("mq", 0, 128), V("mqs", 0, 128), V("mt", 0, 512))
+    for n in range(4):
+        fill(V("mt", 512 * n + C, 512 * n + 512), 0.0)
 
-    def unpack(to, c, s, pieces, banks, skip=(), after=()):
+    def unpack(to, c, s, pieces, banks, skip=()):
         k = 0
         for lo, hi in pieces:
             for b in range(4):
                 bank = V("pb%d" % (HOLD[b] if b in skip else banks[k % len(banks)]), 0, hi - lo)
-                mm(bank, [(V("e%d" % b), V("es%d" % b), V(c, lo, hi), V(s, lo, hi))], after=after)
+                mm(bank, [(V("e%d" % b), V("es%d" % b), V(c, lo, hi), V(s, lo, hi))])
                 if b not in skip:
                     move(V("%s%d" % (to, b), lo, hi), bank)
                     k += 1
@@ -440,86 +371,58 @@ def rank_program(g, core, T, topo):
         x, qc, qs, la = ("xt", "x2", "x3")[r - 1], "qc%d" % r, "qs%d" % r, "la%d" % r
         for i, (lo, hi) in enumerate(XP):
             quant(V(qc, lo, hi), V(qs, lo, hi), V(x, 4 * lo, 4 * hi))
-            mm(V("pb%d" % i, 0, hi - lo), [(V("uq" if TUNE["two"] else "uc"), V("uqs" if TUNE["two"] else "ucs"), V(qc, lo, hi), V(qs, lo, hi))])
-            if TUNE["two"]:
-                signs(V("bw", lo, hi), V("pb%d" % i, 0, hi - lo), True)
-            elif TUNE["sg"] == 0.5:
-                ts(V("bw", lo, hi), V("pb%d" % i, 0, hi - lo), 0.0, 0.5, A.is_gt, A.subtract)
-            else:
-                signs(V("bw", lo, hi), V("pb%d" % i, 0, hi - lo))
+            mm(V("pb%d" % i, 0, hi - lo), [(V("uq"), V("uqs"), V(qc, lo, hi), V(qs, lo, hi))])
+            signs(V("bw", 3 * lo + 2, 3 * hi, 3), V("pb%d" % i, 0, hi - lo), True)
         j = ()
-        for i, (via, codes, lo, hi, takes) in enumerate(ROUTES):
-            j = (send(r, "r_%d_%d" % (r, i), V(("rc%d" if codes else "rs%d") % r, lo, hi), V(qc if codes else qs, lo, hi), codes, takes, j, via),)
+        for i, (codes, lo, hi) in enumerate(ROUTES):
+            j = (send(r, "r_%d_%d" % (r, i), V(("rc%d" if codes else "rs%d") % r, lo, hi), V(qc if codes else qs, lo, hi), codes, j),)
         done = None
-        for lo, hi in MP:
-            for n in range(4):
-                move(V("mt", 4 * (PAD + lo) + n, 4 * (PAD + hi), 4), V("bw"), lst=V("l%d" % n, lo // 16, hi // 16), relu=True)
-            quant(V("mq", PAD + lo, PAD + hi), V("mqs", PAD + lo, PAD + hi), V("mt", 4 * (PAD + lo), 4 * (PAD + hi)))
-            blocks = range((PAD + lo) // 128 if lo else 0, (PAD + hi) // 128)
-            done = mm(V("pb6", 0, 128), [(V("mq", 128 * c, 128 * c + 128), V("mqs", 128 * c, 128 * c + 128), V("b2", 12 - 4 * c, 140 - 4 * c), V("b2s", 12 - 4 * c, 140 - 4 * c)) for c in blocks],
-                      start=lo == 0, stop=hi == C, behind=() if done is None else (done,))
-        if TUNE["d3"]:
-            tab = V("pb6", 0, 112)
-            add(costs("V", tab, (tab,), None), [tab], [V("d3", 0, 28 * L)], lambda e, q, tab=tab: e.tensor_scalar(T["d3"][:, :, 0:4], ap(tab), 0.5, None, A.mult))
-        else:
-            for s, val in enumerate((0.5, 1.5, 3.0, 3.0)):
-                ts(V("dv", s, 28 * L, L), V("pb6", s, 112, 4), val, None, A.mult)
-        masked = {}
-        for pair in PAIRS:
-            for k in pair:
-                scan(V("sc", 64 * k, 64 * k + 4 * L), V("sc", 64 * k - 61, 64 * k - 61 + 4 * L) if k else V("c0", 3, 4 * L + 3) if TUNE["d3"] else V("dv", 28 * L + 3, 32 * L + 3),
-                     V("d3" if TUNE["d3"] else "dv", 4 * L * k, 4 * L * k + 4 * L),
-                     behind=masked.get(k - 2, ()))
-            k, n = pair[0], len(pair)
-            if k < TUNE["early"]:
-                for k in pair:
-                    for t in range(4):
-                        move(V("at", 64 * k + 64 + t, 64 * k + 128, 4), V("maska", 0, 64, 4), scale=V("sc", 64 * k + L * t + 5, 64 * k + L * t + 6), qs="A")
-                continue
-            masked[pair[-1]] = (tt(V("at", 64 * k + 64, 64 * (k + n) + 64), V("sc", 64 * k, 64 * (k + n)), V("maska", 0, 64 * n), A.mult, lst=V("la4", 0, 4 * n)),)
+        for rows in MQ:
+            lo, hi = 128 * rows[0], 128 * rows[-1] + 128
+            for n in rows:
+                move(V("mt", 512 * n, 512 * n + C), V("bw"), lst=V("l%d" % n), scale=(1.0, 3.0, 6.0, 6.0)[n], relu=True)
+            quant(V("mq", lo, hi), V("mqs", lo, hi), V("mt", 4 * lo, 4 * hi))
+            done = mm(V("pb6", 0, 128), [(V("mq", 128 * n, 128 * n + 128), V("mqs", 128 * n, 128 * n + 128), V("b2", GT * (3 - n), GT * (3 - n) + 128), V("b2s", GT * (3 - n), GT * (3 - n) + 128)) for n in rows],
+                      start=done is None, stop=rows == MQ[-1], behind=() if done is None else (done,))
+        for s in range(4):
+            ts(V("dv", s, GT * L, L), V("pb6", GT * s, GT * (s + 1)), (-1.0, 1.0)[s % 2], None, A.mult)
+        for k in range(7):
+            scan(V("sc", 64 * k, 64 * k + 4 * L), V("sc", 64 * k - 61, 64 * k - 61 + 4 * L) if k else V("dv", GT * L + 3, 32 * L + 3), V("dv", 4 * L * k, 4 * L * k + 4 * L))
+        for lo, hi in AT:
+            move(V("at", 64 * lo + 64, 64 * hi + 64), V("sc", 64 * lo, 64 * hi), lst=V("la4", 0, 4 * (hi - lo)))
         quant(V("aq"), V("aqs"), V("at"))
         mm(V("pb7", 0, 128), [(V("aq"), V("aqs"), V("b3"), V("b3s"))])
-        if TUNE["poly"]:
-            scan(V("sl"), V("pb7", 0, 4 * NL), V("cs"))
-        else:
-            tt(V("ph"), V("pb7", 0, 4 * NL), V("thr"), A.is_ge)
-            scan(V("sl"), V("ph"), V("cs"))
-        ts(V(la), V("sl", 3, 4 * NL, 4), col(10) if TUNE["poly"] else SC, MID + 0.25, A.mult, A.add)
-        send(r, "r_l%d" % r, V("lp%d" % r), V(la), False, TUNE["fly"])
+        scan(V("sl"), V("pb7", 0, 4 * NL), V("cs", 0, 4 * NL))
+        ts(V(la), V("sl", 3, 4 * NL, 4), SC2, MID + 0.25, A.mult, A.add)
+        send(r, "r_l%d" % r, V("lp%d" % r), V(la), False, j)
         lent = LENT[r - 1]
         banks = [k for k in (2, 3, 4, 5, 1, 0, 6, 7) if k not in [HOLD[b] for b in lent]]
-        sw = V("scw" if TUNE["two"] else "bw")
-        if TUNE["two"]:
-            mm(V("pb0", 0, C), [(V("uc"), V("ucs"), V(qc), V(qs))])
-            signs(sw, V("pb0", 0, C))
-        else:
-            dma("S", [], [V("bw")], lambda: [(T["bw"][1::16, :], T["bw"][0::16, :])], TUNE["row"])
-        unpack("fb", qc, qs, ((0, C),), banks[:-3], lent, (done,) if TUNE["after"] else ())
+        mm(V("pb0", 0, C), [(V("uc"), V("ucs"), V(qc), V(qs))])
+        signs(V("scw"), V("pb0", 0, C))
+        unpack("fb", qc, qs, ((0, C),), banks[:-3], lent)
         unpack("fp", "rc%d" % r, "rs%d" % r, FP, banks[:-2])
-        move(V("z"), sw, lst=V(la), scale=TUNE["sg"] ** -2, qs=TUNE["zq"])
-        tt(V("u1"), sw, V("dd"), A.mult, lst=V(la))
-        tt(V("dd"), V("z"), V("u1"), A.mult, lst=V("lm"))
-        if TUNE["sum"][r - 1]:
-            dma("S", [V("s2")], [V("tb")], lambda: [(ap(V("tb")), ap(V("s2")))])
-            dma("G", [V("dd")], [V("tb")], lambda: [(ap(V("tb")), ap(V("dd")))], TUNE["adds"], adds=True)
+        z = V("z%d" % r)
+        if r == 1:
+            move(z, V("scw"), lst=V(la))
         else:
-            tt(V("tb"), V("s2"), V("dd"), A.add)
+            tt(z, V("scw"), V("z%d" % (r - 1)), A.mult, lst=V(la))
+        move(V("zc"), z)
+        tt(V("swap", 2, 3 * C, 3), z, V("zc"), A.not_equal, lst=V("lm"))
+        scan(V("tb"), V("swap"), V("trio"))
         if r == 3:
             move(V("pl_t", 0, C), V("place"), lst=V(la), plus=CMID)
-            move(V("pl_t", C, 2 * C), V("tb"), scale=0.5, plus=CMID)
-            dma("S", [V("pl_t")], [], lambda: [(T.pl[:, :], T["pl_t"][0::16, :])])
+            move(V("pl_t", C, 2 * C), V("tb", 2, 3 * C, 3), plus=CMID)
+            dma("S", [V("pl_t")], [], lambda: [(T.pl[:, :], T["pl_t"][0::16, :])], 100e3)
         k = 0
         for lo, hi in ZP:
             for t in range(4):
                 move(V("zt", 4 * lo + t, 4 * hi, 4), V("fp%d" % t), lst=V("lp%d" % r, lo // 16, hi // 16))
             quant(V("zq", lo, hi), V("zqs", lo, hi), V("zt", 4 * lo, 4 * hi))
             for b in range(4):
-                bias[0] = TUNE["bias"] * (3 - b)
                 bank = V("pb%d" % banks[k % len(banks)], 0, hi - lo)
                 k += 1
                 mm(bank, [(V("wq", 128 * b, 128 * b + 128), V("wqs", 128 * b, 128 * b + 128), V("zq", lo, hi), V("zqs", lo, hi))])
                 move(V("hs%d" % b, lo, hi), bank, scale=0.03125)
-                bias[0] = 0.0
         nx = ("x2", "x3", "x4")[r - 1]
         for lo, hi in XP:
             for b in range(4):
@@ -530,18 +433,15 @@ def rank_program(g, core, T, topo):
                 else:
                     tt(out, V("hs%d" % b), V("fb%d" % b, lo, hi), A.add, lst=lst)
         if r < 3:
-            for n in (1, 2, 3):
-                for lo, hi in TP[n - 1]:
-                    move(V("tg%d" % n, lo, hi), V("tb"), lst=V("l%d" % (n - 1), lo // 16, hi // 16))
-                listed(n)
+            lists()
     quant(V("vq"), V("vqs"), V("vt"))
     for i, (a, b) in enumerate(XP):
         quant(V("qc4", a, b), V("qs4", a, b), V("x4", 4 * a, 4 * b))
-        dma("S", [V("qc4", a, b)], [], lambda a=a, b=b: [(T.oc[:, 4 * a:4 * b], T["qc4"][:, a:b].bitcast(dt.uint8))], 2400.0)
+        dma("S", [V("qc4", a, b)], [], lambda a=a, b=b: [(T.oc[:, 4 * a:4 * b], T["qc4"][:, a:b].bitcast(dt.uint8))], 150e3)
         mm(V("pb%d" % i, 0, b - a), [(V("vq"), V("vqs"), V("qc4", a, b), V("qs4", a, b))])
         move(V("yt", a, b), V("pb%d" % i, 0, b - a))
-        dma("S", [V("yt", a, b)], [], lambda a=a, b=b: [(T.y[:, a:b], T["yt"][:, a:b])], 2400.0)
-    dma("S", [V("qs4")], [], lambda: [(T.osc[4 * k:4 * k + 4, :], T["qs4"][32 * k:32 * k + 4, :]) for k in range(4)])
+        dma("S", [V("yt", a, b)], [], lambda a=a, b=b: [(T.y[:, a:b], T["yt"][:, a:b])], 150e3)
+    dma("S", [V("qs4")], [], lambda: [(T.osc[4 * k:4 * k + 4, :], T["qs4"][32 * k:32 * k + 4, :]) for k in range(4)], 100e3)
 
     n = len(ops)
     users = [[] for _ in range(n)]
@@ -549,7 +449,7 @@ def rank_program(g, core, T, topo):
         for j in o["deps"]:
             users[j].append(i)
 
-    def place(rank_of, before, after, back, pin=None):
+    def place(rank_of, before, after, back):
         busy = {k: [] for k in "VAPGS"}
         start, end, free, qof = [None] * n, [None] * n, [None] * n, [None] * n
         left = [len(before[i]) for i in range(n)]
@@ -557,13 +457,9 @@ def rank_program(g, core, T, topo):
         while ready:
             i = max(ready, key=lambda j: rank_of[j])
             ready.remove(i)
-            o = ops[i]
-            late = o.get("late", 0.0)
-            best = None
-            for q, c in o["cost"].items():
-                if pin and pin[i] not in (None, q):
-                    continue
-                t = max([(free[j] + late if back else end[j]) + (SAME if qof[j] == q else WAKE) if wait is True or (wait and qof[j] != q) else free[j] for j, wait in before[i].items()] + [late if back else 0.0])
+            lag, best = late[0][i], None
+            for q, c in cost[0][i].items():
+                t = max([(free[j] + lag if back else end[j]) + CASES[0]["same" if qof[j] == q else "wake"] if wait is True or (wait and qof[j] != q) else free[j] for j, wait in before[i].items()] + [lag if back else 0.0])
                 taken = busy.get(q, ())
                 k, hi = 0, len(taken)
                 while k < hi:
@@ -578,7 +474,7 @@ def rank_program(g, core, T, topo):
                 if best is None or worth < best[0]:
                     best = (worth, t + c, t, q, k)
             free[i], start[i], qof[i] = best[1:4]
-            end[i] = free[i] + (0.0 if back else late)
+            end[i] = free[i] + (0.0 if back else lag)
             if qof[i] in busy:
                 busy[qof[i]].insert(best[4], (start[i], free[i]))
             for u in after[i]:
@@ -587,53 +483,133 @@ def rank_program(g, core, T, topo):
                     ready.append(u)
         return max(end), start, end, qof
 
-    def replay(plan, by_queue, slow, wake):
-        qof, free, end, left = plan[3], {}, [0.0] * n, [0.0] * n
-        for i in sorted(range(n), key=lambda j: (plan[1][j], j)):
-            q = qof[i]
-            t = max([end[j] + wake if wait is True or (wait and qof[j] != q) else left[j] for j, wait in fore[i].items()] + [free.get(q, 0.0)])
-            left[i] = t + ops[i]["cost"][q] * by_queue.get(q, 1.0)
-            end[i] = left[i] + ops[i].get("late", 0.0) * slow
-            if q != "R":
-                free[q] = left[i]
-        return max(end)
+    def refine(plan):
+        qof, seq = list(plan[3]), sorted(range(n), key=lambda j: (plan[1][j], j))
+        above, hard, soft = [0] * n, [None] * n, [None] * n
+        for i in range(n):
+            firm = [j for j, wait in fore[i].items() if wait is True]
+            implied = 0
+            for j in firm:
+                implied |= above[j]
+            hard[i] = [j for j in firm if not implied >> j & 1]
+            soft[i] = [(j, wait) for j, wait in fore[i].items() if wait is not True and not implied >> j & 1]
+            above[i] = implied | sum(1 << j for j in firm)
+        nxt = [[] for _ in range(n)]
+        for i in range(n):
+            for j in hard[i] + [j for j, wait in soft[i]]:
+                nxt[j].append(i)
 
-    fore = [o["deps"] for o in ops]
-    aft = [{u: ops[u]["deps"][i] for u in users[i]} for i in range(n)]
-    prio = [0.0] * n
-    for i in range(n - 1, -1, -1):
-        prio[i] = min(ops[i]["cost"].values()) + ops[i].get("late", 0.0) + max([prio[u] + WAKE for u in users[i]] + [0.0])
-    prio = [p + o["bias"] for p, o in zip(prio, ops)]
-    plans = PLANS
-    for turn in range(0 if plans else TUNE["turns"]):
-        plans.append(place(prio, fore, aft, False))
-        prio = [p + o["bias"] for p, o in zip(place(plans[-1][2], aft, fore, True)[2], ops)]
-    if len(plans) == TUNE["turns"]:
+        def replay(case, p, left, end):
+            free, wake, same, dear, lag = dict.fromkeys("VAPGSR"), CASES[case]["wake"], CASES[case]["same"], cost[case], late[case]
+            k, missing = p - 1, 6
+            while k >= 0 and missing:
+                if free[qof[seq[k]]] is None:
+                    free[qof[seq[k]]] = left[seq[k]]
+                    missing -= 1
+                k -= 1
+            for i in seq[p:]:
+                q = qof[i]
+                t = free[q] or 0.0
+                for j in hard[i]:
+                    e = end[j] + (same if qof[j] == q else wake)
+                    if e > t:
+                        t = e
+                for j, wait in soft[i]:
+                    e = end[j] + wake if wait and qof[j] != q else left[j]
+                    if e > t:
+                        t = e
+                left[i] = free[q] = t = t + dear[i][q]
+                end[i] = t + lag[i]
+            return max(end)
+
+        def longest(case):
+            left, end = state[case]
+            wake, way, last, before = max(CASES[case]["wake"], CASES[case]["same"]), [], {}, [None] * n
+            for i in seq:
+                before[i] = last.get(qof[i])
+                last[qof[i]] = i
+            i = max(range(n), key=lambda j: end[j])
+            while i is not None:
+                way.append(i)
+                t = left[i] - cost[case][i][qof[i]]
+                near = [j for j in hard[i] if end[j] + wake > t - 1.0] + [j for j, wait in soft[i] if end[j] + wake > t - 1.0]
+                if before[i] is not None and left[before[i]] > t - 1.0:
+                    near.insert(0, before[i])
+                i = near[int(rnd() * len(near))] if near else None
+            return way
+
         seed = [TUNE["seed"]]
 
         def rnd():
             seed[0] = (seed[0] * 1103515245 + 12345) % 2 ** 31
             return seed[0] / 2.0 ** 31
-        top = min(plans, key=lambda p: p[0])
-        best = top[0] + sum(replay(top, *case) for case in CASES)
-        for turn in range(TUNE["climb"]):
-            at, wide, amp = rnd() * top[0], TUNE["win"][0] + TUNE["win"][1] * rnd(), TUNE["win"][2] + TUNE["win"][3] * rnd()
-            pin = [None if at <= s < at + wide and rnd() < TUNE["win"][4] else q for s, q in zip(top[1], top[3])] if TUNE["pin"] else None
-            if TUNE["win"][5]:
-                k = min(range(n), key=lambda j: abs(top[1][j] - at) if len(ops[j]["cost"]) > 1 else 1e9)
-                if rnd() < TUNE["win"][5]:
-                    pin[k] = [q for q in ops[k]["cost"] if q != top[3][k]][0]
-            one = place([-s + (amp * rnd() if at <= s < at + wide else amp / 2) for s in top[1]], fore, aft, False, pin)
-            if not pin and turn % 2:
-                one = place(place(one[2], aft, fore, True)[2], fore, aft, False)
-            if pin and turn % 4 == 3:
-                one = place(place(one[2], aft, fore, True, one[3])[2], fore, aft, False, one[3])
-            if one[0] <= top[0] + TUNE["slack"]:
-                mark = one[0] + sum(replay(one, *case) for case in CASES)
-                if mark <= best:
-                    top, best = one, mark
-        plans.append(top)
-        TUNE["mark"] = round(best)
+        state, pos = [([0.0] * n, [0.0] * n) for case in CASES], [0] * n
+        now = sum(replay(k, 0, *state[k]) for k in range(len(CASES)))
+        best, way = (now, list(seq), list(qof)), []
+        for turn in range(TUNE["tries"]):
+            heat = TUNE["heat"] * (1.0 - turn / TUNE["tries"]) ** 2 + 1.0
+            if turn % 25 == 0:
+                left = state[0][0]
+                seq.sort(key=lambda j: left[j] - cost[0][j][qof[j]])
+                way = longest(int(rnd() * len(CASES)))
+                for k in range(n):
+                    pos[seq[k]] = k
+            i = way[int(rnd() * len(way))] if rnd() < TUNE["way"] else int(rnd() * n)
+            q, at = qof[i], pos[i]
+            if q == "R":
+                continue
+            if len(ops[i]["cost"]) > 1 and rnd() < TUNE["change"]:
+                others = [k for k in ops[i]["cost"] if k != q]
+                qof[i] = others[int(rnd() * len(others))]
+            ahead, hops, to = rnd() < 0.5, int(rnd() ** 2 * TUNE["hops"]) + (qof[i] == q), at
+            stop = set(hard[i] + [j for j, wait in soft[i]]) if ahead else set(nxt[i])
+            k = at
+            while hops:
+                k += -1 if ahead else 1
+                if k < 0 or k >= n or seq[k] in stop:
+                    break
+                if qof[seq[k]] == qof[i]:
+                    to, hops = k, hops - 1
+            if to == at and qof[i] == q:
+                continue
+            seq.insert(to, seq.pop(at))
+            lo, hi = min(at, to), max(at, to)
+            for k in range(lo, hi + 1):
+                pos[seq[k]] = k
+            trial = [(list(left), list(end)) for left, end in state]
+            bound, mark = now - heat * math.log(1.0 - rnd()), 0.0
+            for k in range(len(CASES)):
+                mark += replay(k, lo, *trial[k])
+            if mark <= bound:
+                state, now = trial, mark
+                if now < best[0]:
+                    best = (now, list(seq), list(qof))
+            else:
+                seq.insert(at, seq.pop(to))
+                qof[i] = q
+                for k in range(lo, hi + 1):
+                    pos[seq[k]] = k
+        now, seq, qof = best
+        spans = [replay(k, 0, *state[k]) for k in range(len(CASES))]
+        TUNE["mark"] = [round(v) for v in spans]
+        start = [0] * n
+        for k, i in enumerate(seq):
+            start[i] = k
+        return spans[0], start, state[0][1], qof
+
+    cost = [[{q: sum(_price(m, *part) for part in (c if isinstance(c, list) else [c])) for q, c in o["cost"].items()} for o in ops] for m in CASES]
+    late = [[_price(m, *o.get("late", ("none",))) for o in ops] for m in CASES]
+    fore = [o["deps"] for o in ops]
+    aft = [{u: ops[u]["deps"][i] for u in users[i]} for i in range(n)]
+    prio = [0.0] * n
+    for i in range(n - 1, -1, -1):
+        prio[i] = min(cost[0][i].values()) + late[0][i] + max([prio[u] + CASES[0]["wake"] for u in users[i]] + [0.0])
+    plans = PLANS
+    for turn in range(0 if plans else TUNE["turns"]):
+        plans.append(place(prio, fore, aft, False))
+        prio = place(plans[-1][2], aft, fore, True)[2]
+    if len(plans) == TUNE["turns"]:
+        plans.append(refine(min(plans, key=lambda p: p[0])))
     span, start, end, qof = plans[-1]
     TUNE["span"] = [round(p[0]) for p in plans]
 

@@ -7,16 +7,21 @@ MID = C // 2
 L = 14
 GT = 28
 STEP = (1, 2, 3)
-XP = ((0, 288), (288, C))
+LOADS = ("pkuxXmwsv", "SAASASSSS")
+XP = (((0, 288), (288, C)),) * 3 + (((0, 160), (160, 288), (288, C)),)
+NP = XP[1:]
 ZP = ((0, 224), (224, C))
-FP = XP
+HOME = (False, False, False)
+HP = ((0, 224), (224, C))
+CUTS = {"fb": (1, 1, 1, 1), "fp": (1, 1, 1, 1)}
+FP = ((0, 288), (288, C))
 MQ = ((0, 1), (2,), (3,))
-ROUTES = ((True, 0, 288), (False, 0, C), (True, 288, C))
+RP = (((0, C),),) * 3 + (((0, 224), (224, C)),)
 TP = (((0, 192), (192, C)),) * 3
 HOLD = (3, 3, 4, 5)
 LENT = ((3,),) * 3
-AT = ((0, 3), (3, 6), (6, 7))
-F32, BF16, I32, U16, CODE, U8 = "float32", "bfloat16", "int32", "uint16", "float8_e4m3fn_x4", "uint8"
+AT = tuple((k, k + 1) for k in range(7))
+F32, BF16, F16, I32, U16, CODE, U8 = "float32", "bfloat16", "float16", "int32", "uint16", "float8_e4m3fn_x4", "uint8"
 MW = 512
 
 SCRATCH, PART = {}, {}
@@ -41,26 +46,28 @@ _buf(8, I32, "iu")
 _buf(8, U16, "lu0")
 _buf(NL, U16, "lq")
 _parts("li", NL, I32, "kgw", "pgw", "mgw")
-_parts("lu", NL, U16, "l0", "lpw", "lm", "lm3")
+_parts("lu", NL, U16, "l0", "lpw", "lm", "lm2", "lpp", "lz")
 _parts("lists", NL, U16, "l1", "l2", "l3")
 _buf(C, BF16, "place", "kb", "scw", "z1", "z2", "z3", "zc")
-_buf(3 * C, BF16, "tb", "bw", "swap", "trio")
+_buf(2 * C, BF16, "tb", "bw", "p2")
+_buf(2 * C, F16, "swap", "pair")
 _buf(C, F32, "yt", "kk0", "kk1", "kk2", "kk3")
 _buf(520, BF16, "w1", "ones")
 _buf(4 * (3 * GT + 128), BF16, "w2")
 _buf(512, BF16, "w3", "ut", "vt", "at")
-_buf(32 * L + 4, F32, "dv")
-_buf(448, F32, "sc")
+_buf(24 * L + 448, F32, "chain")
+PART.update(dv=("chain", 0, 24 * L), sc=("chain", 24 * L, 448))
 _buf(64, BF16, "f0", "f1", "f2")
 _buf(28, U16, "la4")
-_buf(2 * C, F32, "pl_t")
+_buf(C, F32, "pl_t")
+_buf(32, F32, "lw", "lt")
 _buf(4 * NL, F32, "sl")
 _buf(8 * NL, F32, "cs")
 _buf(2 * NL, F32, "su")
 _buf(NL, F32, "sf", "d3")
 _buf(4 * C, BF16, "xt", "x2", "x3", "x4", "zt")
 _buf(4 * MW, BF16, "mt")
-for _c, _s, _n in (("uq", "uqs", 128), ("uc", "ucs", 128), ("vq", "vqs", 128), ("wq", "wqs", 512), ("b2", "b2s", 3 * GT + 128), ("b3", "b3s", 128), ("mq", "mqs", MW), ("aq", "aqs", 128), ("zq", "zqs", C)):
+for _c, _s, _n in (("uq", "uqs", 128), ("uc", "ucs", 128), ("vq", "vqs", 128), ("wq", "wqs", 512), ("b2", "b2s", 3 * GT + 128), ("b3", "b3s", 128), ("mq", "mqs", MW), ("aq", "aqs", 128), ("zq1", "zs1", C), ("zq2", "zs2", C), ("zq3", "zs3", C)):
     _buf(_n, CODE, _c)
     _buf(_n, U8, _s)
 _parts("ec", 128, CODE, *["e%d" % i for i in range(4)])
@@ -80,22 +87,23 @@ for _i in (1, 2, 3):
 
 SEMAPHORES = ["s_v", "s_a", "s_p", "s_g", "loc"] + ["d_%d" % i for i in range(40)] + ["r_%d_%d" % (r, i) for r in (1, 2, 3) for i in range(8)] + ["r_l%d" % r for r in (1, 2, 3)]
 
-NAMES = ("f", "g", "wake", "same", "vfix", "afix", "least", "aleast", "gv", "ar", "pe", "pfix", "rem", "remb", "first", "issue", "dma", "dmab")
+NAMES = ("f", "g", "wake", "same", "vfix", "afix", "least", "aleast", "gv", "ar", "pe", "pfix", "rem", "remb", "first", "issue", "dma", "dmab", "start", "rrow")
 CASES = [dict(zip(NAMES, c)) for c in (
-    (1.09, 1.60, 200.0, 125.0, 10.0, 70.0, 35.0, 15.0, 35.0, 0.90, 0.45, 90.0, 1400.0, 150.0, 1400.0, 100.0, 1100.0, 215.0),
-    (1.25, 0.95, 190.0, 225.0, 3.0, 39.0, 30.0, 14.0, 55.0, 1.00, 0.62, 75.0, 850.0, 120.0, 850.0, 75.0, 1750.0, 220.0),
-    (1.40, 0.86, 63.0, 174.0, 18.0, 18.0, 57.0, 0.0, 30.0, 1.20, 0.46, 33.0, 1300.0, 148.0, 650.0, 30.0, 1150.0, 350.0),
-    (1.09, 2.06, 139.0, 273.0, 44.0, 37.0, 32.0, 64.0, 74.0, 1.13, 0.42, 80.0, 1500.0, 80.0, 1290.0, 217.0, 2200.0, 307.0))]
+    (1.05, 1.05, 207.0, 212.0, 29.0, 55.0, 30.0, 55.0, 30.0, 0.95, 0.49, 77.0, 1040.0, 74.0, 530.0, 210.0, 2025.0, 235.0, 30.0, 1.0),
+    (1.00, 0.86, 188.0, 212.0, 27.0, 56.0, 30.0, 4.0, 30.0, 0.96, 0.49, 72.0, 980.0, 75.0, 960.0, 120.0, 1980.0, 267.0, 30.0, 2.0),
+    (1.06, 1.54, 58.0, 194.0, 35.0, 92.0, 33.0, 42.0, 30.0, 0.99, 0.63, 117.0, 920.0, 70.0, 1580.0, 364.0, 1000.0, 350.0, 105.0, 1.0),
+    (1.50, 1.61, 256.0, 265.0, 30.0, 74.0, 30.0, 48.0, 51.0, 0.99, 0.63, 58.0, 1630.0, 62.0, 520.0, 223.0, 2710.0, 350.0, 39.0, 5.0),
+    (1.08, 2.06, 140.0, 280.0, 43.0, 49.0, 31.0, 22.0, 74.0, 1.11, 0.64, 95.0, 1580.0, 50.0, 2430.0, 294.0, 1830.0, 350.0, 30.0, 0.0))]
 PLANS = []
-TUNE = {"tries": 90000, "heat": 300.0, "way": 0.8, "change": 0.3, "hops": 4, "spare": 0.1, "turns": 4, "seed": 1}
+TUNE = {"xor": (0, C), "trade": 0.4, "two": 1, "sq": "A", "twice": 1, "stay": 60, "wide": 36, "near": 150.0, "tries": 330000, "heat": 200.0, "way": 0.8, "change": 0.3, "hops": 4, "spare": 0.1, "turns": 4, "seed": 6}
 
 
 def _price(m, kind, n=0.0):
     cycle = 0.83 * m["f"]
     return {"V": m["vfix"] + max(m["least"], n) * cycle, "A": m["afix"] + max(m["aleast"], n) * cycle * m["ar"],
             "gV": m["gv"] + n * m["g"], "gA": m["gv"] + 15.0 + n * m["g"] * m["ar"], "G": 150.0 + 2.0 * n * cycle,
-            "quant": m["vfix"] + (12.0 + 0.22 * n) * m["f"], "P": m["pfix"] + (n + 16.0) * m["pe"], "start": 60.0 * n,
-            "send": m["issue"] + n * m["first"], "fly": m["rem"] - m["wake"], "link": n / m["remb"], "dma": m["dma"] + n / m["dmab"], "none": 0.0}[kind]
+            "quant": m["vfix"] + (12.0 + 0.22 * n) * m["f"], "P": m["pfix"] + (n + 16.0) * m["pe"], "start": m["start"] * n,
+            "send": m["issue"] + n * m["first"], "fly": m["rem"] - m["wake"], "link": n / m["remb"] + 16.0 * m["rrow"], "dma": m["dma"] - m["wake"], "move": n / m["dmab"], "none": 0.0}[kind]
 
 
 def _hit(a, b):
@@ -113,7 +121,7 @@ def rank_program(g, core, T, topo):
         return
     A = AluOpType
     AF = ActivationFunctionType
-    ops, seen = [], {}
+    ops, seen, loading = [], {}, []
 
     def V(name, lo=0, hi=None, st=1):
         whole, at, cols = PART.get(name, (name, 0, SCRATCH.get(name, (0, (0, 0)))[1][1]))
@@ -146,13 +154,13 @@ def rank_program(g, core, T, topo):
                 seen[v[0]].append((i, mode, v))
         for j in after:
             deps[j] = True
-        for j in behind:
+        for j in list(behind) + (loading[-1:] if "A" in cost else []):
             deps[j] = False
         ops.append({"cost": cost, "deps": deps, "emit": emit, "kind": kind, "sem": sem, "amount": amount})
         return i
 
     def narrow(*views):
-        return all(SCRATCH[v[0]][2] in (BF16, U16) for v in views if isinstance(v, tuple))
+        return all(SCRATCH[v[0]][2] in (BF16, F16, U16) for v in views if isinstance(v, tuple))
 
     def costs(qs, out, ins, lst, both=False):
         n = n_of(out)
@@ -198,10 +206,10 @@ def rank_program(g, core, T, topo):
             return e.activation(o, i, AF.Copy)
         return add(costs(qs, out, (in_, scale, plus), lst), [in_, lst, scale, plus], [out], emit)
 
-    def signs(out, in_, loose=False):
+    def signs(out, in_, loose=False, qs="VA"):
         if loose:
             return add(costs("VA", out, (in_,), None), [in_], [out], lambda e, q: e.tensor_scalar(ap(out), ap(in_), 0.0, None, A.is_gt) if q == "V" else e.activation(ap(out), ap(in_), AF.Sign))
-        return add(costs("VA", out, (in_,), None), [in_, TINY], [out],
+        return add(costs(qs, out, (in_,), None), [in_, TINY], [out],
                    lambda e, q: e.tensor_scalar(ap(out), ap(in_), 0.0, 0.5, A.is_gt, A.subtract) if q == "V" else e.activation(ap(out), ap(in_), AF.Sign, bias=ap(TINY)))
 
     def fill(out, val, qs="VAG"):
@@ -240,17 +248,19 @@ def rank_program(g, core, T, topo):
     def keep(out, in_, pattern, op, base, cm, other=0.0):
         return add({"G": ("G", n_of(out) + 20)}, [in_], [out], lambda e, q: e.affine_select(ap(out), ap(in_), pattern, op, other, base, cm))
 
-    dcount, lands, sent = [0], [], [0]
+    dcount, lands, sent, landing = [0], [], [0], {}
 
-    def dma(q, reads, writes, pairs, ahead, behind=()):
+    def dma(q, reads, writes, pairs, size, behind=()):
         sem = "d_%d" % dcount[0]
         dcount[0] += 1
         def emit(e, q):
             for o, i in pairs():
                 e.dma_start(o, i).then_inc(T.sem[sem], 16)
-        i = add({q: ("start", len(pairs()))}, reads, writes, emit, "d", sem, 16 * len(pairs()), behind=behind)
-        ops[i]["late"] = ("dma", ahead)
-        return i
+        i = add({q: ("start", len(pairs()))}, reads, writes, emit, "s", behind=[j for j in behind if q in ops[j]["cost"]])
+        ops[i]["late"] = ("dma",)
+        j = add({"D": ("move", size)}, reads, writes, None, "r", sem, 16 * len(pairs()), after=(i,), behind=[j for j in behind if "D" in ops[j]["cost"]])
+        landing[i] = j
+        return i, j
 
     def send(r, sem, dst_v, src_v, codes, behind=()):
         to = T.cores[rank ^ STEP[r - 1]]
@@ -264,48 +274,46 @@ def rank_program(g, core, T, topo):
         return j
 
     col = lambda i: V("cols", i, i + 1)
-    SC, ISC, SC2, CMID, TINY, OWN, SC3 = [col(i) for i in range(7)]
+    SC, ISC, HALF, OWN, TWICE = [col(i) for i in range(5)]
+    TINY = -2.0 ** -100
     KG, PG, MG = V("kgw", 0, NL), V("pgw", 0, NL), V("mgw", 0, NL)
 
-    a, b = XP[0][1], C
-    d0 = dma("S", [], [PG], lambda: [(ap(PG), T.pg[:, :])], 26e3)
-    d1 = dma("A", [], [KG], lambda: [(ap(KG), T.kg[:, :])], 13e3)
-    at = (158e3, 453e3, 584e3, 597e3, 859e3, 925e3, 1056e3)
-    d1 = dma("A", [], [V("ut")], lambda: [(T["ut"][:, :], T.u[:, :])], at[0], (d1,))
-    d0 = dma("S", [], [V("xt", 0, 4 * a)], lambda: [(T["xt"][:, 0:4 * a], T.x[:, 0:4 * a])], at[1], (d0,))
-    d1 = dma("A", [], [V("xt", 4 * a)], lambda: [(T["xt"][:, 4 * a:4 * b], T.x[:, 4 * a:4 * b])], at[2], (d1,))
-    d0 = dma("S", [], [MG], lambda: [(ap(MG), T.mg[:, :])], at[3], (d0,))
-    d0 = dma("S", [], [V("wq")], lambda: [(T["wq"][:, :].bitcast(dt.uint8), T.wc[:, :])], at[4], (d0,))
-    d0 = dma("S", [], [V("wqs")], lambda: [(T["wqs"][:, :], T.ws[:, :])], at[5], (d0,))
-    d0 = dma("S", [], [V("vt")], lambda: [(T["vt"][:, :], T.v[:, :])], at[6], (d0,))
+    a, b = XP[0][0][1], C
+    loads = {"p": (PG, lambda: [(ap(PG), T.pg[:, :])], 512 * NL), "k": (KG, lambda: [(ap(KG), T.kg[:, :])], 512 * NL), "m": (MG, lambda: [(ap(MG), T.mg[:, :])], 512 * NL),
+             "u": (V("ut"), lambda: [(T["ut"][:, :], T.u[:, :])], 128 * 1024), "v": (V("vt"), lambda: [(T["vt"][:, :], T.v[:, :])], 128 * 1024),
+             "x": (V("xt", 0, 4 * a), lambda: [(T["xt"][:, 0:4 * a], T.x[:, 0:4 * a])], 1024 * a),
+             "X": (V("xt", 4 * a), lambda: [(T["xt"][:, 4 * a:4 * b], T.x[:, 4 * a:4 * b])], 1024 * (b - a)),
+             "w": (V("wq"), lambda: [(T["wq"][:, :].bitcast(dt.uint8), T.wc[:, :])], 128 * 2048), "s": (V("wqs"), lambda: [(T["wqs"][:, :], T.ws[:, :])], 128 * 512)}
+    done = []
+    for name, q in zip(*LOADS):
+        done.extend(dma(q, [], [loads[name][0]], loads[name][1], loads[name][2], done))
+        if q == "A":
+            loading.append(done[-2])
 
     fill(V("ones"), 1.0, "V")
     scan(V("place"), V("ones", 0, C), V("ones", 0, C), -MID - 1.0)
-    fill(TINY, -2.0 ** -100, "V")
-    fill(CMID, float(MID), "V")
+    fill(V("lw", NL), 0.0)
     iota(OWN, [[0, 1]], 0, 1)
     ts(V("lq"), V("ones", 0, NL), OWN, None, A.mult)
-    ts(V("k0"), V("place", MID, MID + 128), OWN, None, A.subtract)
-    ts(V("k2"), V("k0"), 1.0, 2.0 ** 20, A.is_equal, A.mult)
-    ts(V("k3"), V("k0"), 0.0, None, A.not_equal)
-    tt(V("k1"), V("k2"), V("k3"), A.max)
+    keep(V("k0"), V("ones", 0, 128), [[1, 128]], A.not_equal, 0, -1)
+    keep(V("k1"), V("k0"), [[1, 128]], A.not_equal, -1, -1, 2.0 ** 20)
     move(V("kb"), V("k1"), lst=V("lq"))
     add(costs("V", ISC, (), None), [V("kb", 0, 16)], [ISC], lambda e, q: e.tensor_reduce(ap(ISC), ap(V("kb", 0, 16)), AxisListType.X, A.max))
     ts(SC, ISC, 1.0, 2.0 ** -20, A.is_equal, A.max)
-    move(SC2, SC, scale=0.5)
-    move(SC3, SC, scale=3.0)
+    move(HALF, SC, scale=0.5)
+    move(TWICE, SC, scale=2.0)
     move(V("lpw"), PG, qs="V")
-    ts(V("l0"), KG, 3.0, 2.0, A.mult, A.add)
+    ts(V("l0"), KG, 2.0, 1.0, A.mult, A.add)
     move(V("lm"), MG, qs="V")
-    ts(V("lm3"), MG, 3.0, 2.0, A.mult, A.add)
+    ts(V("lm2"), MG, 2.0, 1.0, A.mult, A.add)
     ts(V("ts0", 15, C, 16), KG, -float(MID), ISC, A.add, A.mult)
 
-    def lists():
+    def lists(steps=(("tb", 0), ("tb", 1), ("tb", 2))):
         for n in (1, 2, 3):
             for lo, hi in TP[n - 1]:
-                move(V("tg%d" % n, lo, hi), V("tb"), lst=V("l%d" % (n - 1), lo // 16, hi // 16))
+                move(V("tg%d" % n, lo, hi), V(steps[n - 1][0]), lst=V("l%d" % steps[n - 1][1], lo // 16, hi // 16))
             scan(V("ts%d" % n), V("kb"), V("tg%d" % n))
-            ts(V("l%d" % n), V("ts%d" % n, 15, C, 16), SC3, 3 * MID + 2.25, A.mult, A.add)
+            ts(V("l%d" % n), V("ts%d" % n, 15, C, 16), TWICE, 2 * MID + 1.25, A.mult, A.add)
         some = lambda n, k: V("tsum", n * C + 15, (n + k) * C, 16)
         move(V("cs", 3, 8 * NL, 4), some(1, 2), scale=2.0)
         tt(V("su"), some(0, 2), some(2, 2), A.add)
@@ -316,16 +324,25 @@ def rank_program(g, core, T, topo):
         tt(V("cs", 2, 4 * NL, 4), V("sf"), V("cs", 0, 4 * NL, 4), A.subtract)
 
     for lo, hi in ((0, 224), (224, C)):
-        move(V("tb", 3 * lo + 2, 3 * hi, 3), V("place"), lst=V("lpw", lo // 16, hi // 16))
-    lists()
-    move(V("trio", 0, 3 * C, 3), V("tb"), lst=V("lm3"))
-    move(V("trio", 1, 3 * C, 3), V("tb", 2, 3 * C, 3), scale=-1.0)
-    move(V("trio", 2, 3 * C, 3), V("tb", 2, 3 * C, 3))
-    fill(V("swap", 0, 3 * C, 3), 0.0)
-    fill(V("swap", 1, 3 * C, 3), 1.0)
+        move(V("tb", 2 * lo + 1, 2 * hi, 2), V("place"), lst=V("lpw", lo // 16, hi // 16))
+    if TUNE["twice"]:
+        ts(V("lpp"), PG, 2.0, 1.0, A.mult, A.add)
+        for lo, hi in ((0, 224), (224, C)):
+            move(V("p2", 2 * lo + 1, 2 * hi, 2), V("tb"), lst=V("lpp", lo // 16, hi // 16))
+        lists((("tb", 0), ("p2", 0), ("p2", 1)))
+    else:
+        lists()
+    move(V("pair", 1, 2 * C, 2), V("tb", 1, 2 * C, 2), qs="V")
+    tt(V("pair", 0, 2 * C, 2), V("tb"), V("pair", 1, 2 * C, 2), A.subtract, lst=V("lm2"))
+    ts(V("swap", 0, 2 * C, 2), V("ones", 0, C), 0.0, None, A.mult)
     quant(V("uq"), V("uqs"), V("ut"))
     iota(V("iu"), [[16, 8]], 0, 0)
-    move(V("lu0"), V("iu"), qs="V")
+    if TUNE["two"]:
+        move(V("lu0"), V("iu"), qs="V")
+    else:
+        ts(col(7), V("kb", 1, 2), 0.0, None, A.is_equal)
+        ts(V("lu0"), V("iu"), col(7), None, A.add)
+        fill(V("bw", 0, 2 * C, 2), 0.0)
     add(costs("V", V("uc"), (), V("lu0")), [V("uq"), V("lu0")], [V("uc")], lambda e, q: e.tensor_copy(ap(V("uc")).bitcast(dt.uint32), ap(V("uq")).bitcast(dt.uint32).indirect(ap(V("lu0")))))
     add(costs("VA", V("ucs"), (), V("lu0")), [V("uqs"), V("lu0")], [V("ucs")],
         lambda e, q: e.tensor_copy(ap(V("ucs")), src(V("uqs"), V("lu0"))) if q == "V" else e.activation(ap(V("ucs")), src(V("uqs"), V("lu0")), AF.Copy))
@@ -345,10 +362,12 @@ def rank_program(g, core, T, topo):
         fill(V("w3", t, C, 16), 0.0)
     quant(V("b3"), V("b3s"), V("w3"))
     fill(V("dv"), 0.0)
-    for lo, hi, val in ((4, GT * L, -1.0), (5, 32 * L, -1.0), (6, GT * L, -1.0), (GT * L + 6, 32 * L, -2.0), (7, 32 * L, 1.0 / 36.0), (8, 32 * L, 1.0), (9, 32 * L, 1.0)):
-        fill(V("dv", lo, hi, L), val, "V" if lo == 7 else "VAG")
-    fill(V("sc"), 0.0)
-    iota(V("f0"), [[0, 4], [L, 4], [0, 4]], 4, 0)
+    fill(V("sc", 0, 64), 0.0)
+    for k in range(3):
+        fill(V("sc", 64 + 4 * L + k, None, 64), 0.0)
+    for lo, hi, val in ((4, 24 * L, -2.0), (5, 24 * L, 1.0), (6, 24 * L, 1.0), (7, GT * L, 1.0 / 36.0), (8, GT * L, 1.0), (9, GT * L, 1.0)):
+        fill(V("chain", lo, hi, L), val, "V" if lo == 7 else "VAG")
+    iota(V("f0"), [[0, 4], [L, 4], [0, 4]], 5, 0)
     keep(V("f1"), V("f0"), [[1, 4], [0, 4], [-1, 4]], A.is_equal, 0, 0, 10.0)
     scan(V("f2"), V("kb", 0, 64), V("f1"))
     for k in range(max(hi - lo for lo, hi in AT)):
@@ -357,74 +376,110 @@ def rank_program(g, core, T, topo):
     for n in range(4):
         fill(V("mt", 512 * n + C, 512 * n + 512), 0.0)
 
-    def unpack(to, c, s, pieces, banks, skip=()):
+    def unpack(to, c, s, pieces, banks, skip=(), every=False):
         k = 0
         for lo, hi in pieces:
             for b in range(4):
                 bank = V("pb%d" % (HOLD[b] if b in skip else banks[k % len(banks)]), 0, hi - lo)
                 mm(bank, [(V("e%d" % b), V("es%d" % b), V(c, lo, hi), V(s, lo, hi))])
-                if b not in skip:
-                    move(V("%s%d" % (to, b), lo, hi), bank)
-                    k += 1
+                if every or b not in skip:
+                    cuts = [(hi - lo) * u // CUTS[to][b] for u in range(CUTS[to][b] + 1)]
+                    for u, w in zip(cuts, cuts[1:]):
+                        move(V("%s%d" % (to, b), lo + u, lo + w), V(bank[0], u, w))
+                k += b not in skip
 
     for r in (1, 2, 3):
         x, qc, qs, la = ("xt", "x2", "x3")[r - 1], "qc%d" % r, "qs%d" % r, "la%d" % r
-        for i, (lo, hi) in enumerate(XP):
+        for i, (lo, hi) in enumerate(XP[r - 1]):
             quant(V(qc, lo, hi), V(qs, lo, hi), V(x, 4 * lo, 4 * hi))
-            mm(V("pb%d" % i, 0, hi - lo), [(V("uq"), V("uqs"), V(qc, lo, hi), V(qs, lo, hi))])
-            signs(V("bw", 3 * lo + 2, 3 * hi, 3), V("pb%d" % i, 0, hi - lo), True)
-        j = ()
-        for i, (codes, lo, hi) in enumerate(ROUTES):
+            mm(V("pb%d" % i, 0, hi - lo), [(V("uq" if TUNE["two"] else "uc"), V("uqs" if TUNE["two"] else "ucs"), V(qc, lo, hi), V(qs, lo, hi))])
+            signs(V("bw", 2 * lo + 1, 2 * hi, 2), V("pb%d" % i, 0, hi - lo), TUNE["two"], "VA" if TUNE["two"] else TUNE["sq"])
+        j, home = (), HOME[r - 1]
+        for i, (codes, lo, hi) in enumerate(() if home else ((True,) + XP[r - 1][0], (False, 0, C), (True,) + XP[r - 1][1])):
             j = (send(r, "r_%d_%d" % (r, i), V(("rc%d" if codes else "rs%d") % r, lo, hi), V(qc if codes else qs, lo, hi), codes, j),)
-        done = None
+        term = lambda n, at: (V("mq", 128 * n, 128 * n + 128), V("mqs", 128 * n, 128 * n + 128), V("b2", GT * at, GT * at + 128), V("b2s", GT * at, GT * at + 128))
+        done = {}
         for rows in MQ:
             lo, hi = 128 * rows[0], 128 * rows[-1] + 128
             for n in rows:
-                move(V("mt", 512 * n, 512 * n + C), V("bw"), lst=V("l%d" % n), scale=(1.0, 3.0, 6.0, 6.0)[n], relu=True)
+                for a, b in RP[n]:
+                    move(V("mt", 512 * n + a, 512 * n + b), V("bw"), lst=V("l%d" % n, a // 16, b // 16), scale=(6.0, 6.0, 3.0, 1.0)[n], relu=True)
             quant(V("mq", lo, hi), V("mqs", lo, hi), V("mt", 4 * lo, 4 * hi))
-            done = mm(V("pb6", 0, 128), [(V("mq", 128 * n, 128 * n + 128), V("mqs", 128 * n, 128 * n + 128), V("b2", GT * (3 - n), GT * (3 - n) + 128), V("b2s", GT * (3 - n), GT * (3 - n) + 128)) for n in rows],
-                      start=done is None, stop=rows == MQ[-1], behind=() if done is None else (done,))
+            if 1 in rows:
+                mm(V("pb0", 0, 128), [term(1, 3)])
+                for s in range(3):
+                    move(V("sc", 4 + s, 4 * L, L), V("pb0", 0, 4), scale=1.0 / 36.0, plus=s - 2.0 or None)
+            for bank, last in (("pb1", 2), ("pb6", 3)):
+                some = [n for n in rows if n <= last]
+                if some:
+                    done[bank] = (mm(V(bank, 0, 128), [term(n, n) for n in some], start=bank not in done, stop=last in some, behind=done.get(bank, ())),)
         for s in range(4):
-            ts(V("dv", s, GT * L, L), V("pb6", GT * s, GT * (s + 1)), (-1.0, 1.0)[s % 2], None, A.mult)
-        for k in range(7):
-            scan(V("sc", 64 * k, 64 * k + 4 * L), V("sc", 64 * k - 61, 64 * k - 61 + 4 * L) if k else V("dv", GT * L + 3, 32 * L + 3), V("dv", 4 * L * k, 4 * L * k + 4 * L))
+            move(V("dv", s, None, L), V("pb1" if s else "pb6", GT * s + 4, GT * (s + 1)))
+        for k in range(1, 7):
+            scan(V("sc", 64 * k, 64 * k + 4 * L), V("sc", 64 * k - 61, 64 * k - 61 + 4 * L), V("dv", 4 * L * (k - 1), 4 * L * k))
         for lo, hi in AT:
             move(V("at", 64 * lo + 64, 64 * hi + 64), V("sc", 64 * lo, 64 * hi), lst=V("la4", 0, 4 * (hi - lo)))
         quant(V("aq"), V("aqs"), V("at"))
         mm(V("pb7", 0, 128), [(V("aq"), V("aqs"), V("b3"), V("b3s"))])
         scan(V("sl"), V("pb7", 0, 4 * NL), V("cs", 0, 4 * NL))
-        ts(V(la), V("sl", 3, 4 * NL, 4), SC2, MID + 0.25, A.mult, A.add)
-        send(r, "r_l%d" % r, V("lp%d" % r), V(la), False, j)
+        ts(V(la), V("sl", 3, 4 * NL, 4), HALF, MID + 0.25, A.mult, A.add)
+        if not home:
+            send(r, "r_l%d" % r, V("lp%d" % r), V(la), False, j)
         lent = LENT[r - 1]
         banks = [k for k in (2, 3, 4, 5, 1, 0, 6, 7) if k not in [HOLD[b] for b in lent]]
-        mm(V("pb0", 0, C), [(V("uc"), V("ucs"), V(qc), V(qs))])
-        signs(V("scw"), V("pb0", 0, C))
-        unpack("fb", qc, qs, ((0, C),), banks[:-3], lent)
-        unpack("fp", "rc%d" % r, "rs%d" % r, FP, banks[:-2])
-        z = V("z%d" % r)
-        if r == 1:
-            move(z, V("scw"), lst=V(la))
+        sw, lz = V("scw"), V(la)
+        if TUNE["two"]:
+            mm(V("pb0", 0, C), [(V("uc"), V("ucs"), V(qc), V(qs))])
+            if TUNE["xor"]:
+                for lo, hi in zip(TUNE["xor"], TUNE["xor"][1:]):
+                    ts(V("scw", lo, hi), V("pb0", lo, hi), 0.0, None, A.is_gt)
+            else:
+                signs(sw, V("pb0", 0, C))
         else:
-            tt(z, V("scw"), V("z%d" % (r - 1)), A.mult, lst=V(la))
-        move(V("zc"), z)
-        tt(V("swap", 2, 3 * C, 3), z, V("zc"), A.not_equal, lst=V("lm"))
-        scan(V("tb"), V("swap"), V("trio"))
+            sw, lz = V("bw"), V("lz")
+            dma("S", [], [sw], lambda: [(T["bw"][1::16, :], T["bw"][0::16, :])], 32 * C)
+            ts(lz, V("sl", 3, 4 * NL, 4), SC, 2 * MID + 1.25, A.mult, A.add)
+        unpack("fb", qc, qs, ((0, C),), banks[:-3], lent, home)
+        if not home:
+            unpack("fp", "rc%d" % r, "rs%d" % r, FP, banks[:-2])
+        z = V("z%d" % r)
+        if TUNE["xor"]:
+            move(z, sw, lst=lz)
+            if r == 1:
+                move(V("zc"), sw, lst=lz)
+            else:
+                tt(V("zc"), sw, V("swap", 1, 2 * C, 2), A.not_equal, lst=lz)
+        else:
+            if r == 1:
+                move(z, sw, lst=lz)
+            else:
+                tt(z, sw, V("z%d" % (r - 1)), A.mult, lst=lz)
+            move(V("zc"), z)
+        tt(V("swap", 1, 2 * C, 2), z, V("zc"), A.not_equal, lst=V("lm"))
+        scan(V("tb"), V("swap"), V("pair"))
         if r == 3:
-            move(V("pl_t", 0, C), V("place"), lst=V(la), plus=CMID)
-            move(V("pl_t", C, 2 * C), V("tb", 2, 3 * C, 3), plus=CMID)
-            dma("S", [V("pl_t")], [], lambda: [(T.pl[:, :], T["pl_t"][0::16, :])], 100e3)
+            move(V("lw", 0, NL), V(la), qs="V")
+            add(costs("V", V("lt"), (), None), [V("lw")], [V("lt")], lambda e, q: e.transpose(ap(V("lt")), ap(V("lw"))))
+            dma("S", [V("lt")], [], lambda: [(T.pl[k:k + 1, 0:C], T["lt"][32 * (k // 2):32 * (k // 2) + NL, 16 * (k % 2):16 * (k % 2) + 16]) for k in range(8)], 64 * C)
+            move(V("pl_t"), V("tb", 1, 2 * C, 2), plus=float(MID))
+            dma("S", [V("pl_t")], [], lambda: [(T.pl[:, C:2 * C], T["pl_t"][0::16, :])], 32 * C)
         k = 0
-        for lo, hi in ZP:
+        for i, (lo, hi) in enumerate(HP if home else ZP):
             for t in range(4):
-                move(V("zt", 4 * lo + t, 4 * hi, 4), V("fp%d" % t), lst=V("lp%d" % r, lo // 16, hi // 16))
-            quant(V("zq", lo, hi), V("zqs", lo, hi), V("zt", 4 * lo, 4 * hi))
+                move(V("zt", 4 * lo + t, 4 * hi, 4), V(("fb%d" if home else "fp%d") % t), lst=V(la if home else "lp%d" % r, lo // 16, hi // 16))
+            zq, zs = V("zq%d" % r, lo, hi), V("zs%d" % r, lo, hi)
+            quant(zq, zs, V("zt", 4 * lo, 4 * hi))
+            if home:
+                j = (send(r, "r_%d_%d" % (r, 2 * i), V("rs%d" % r, lo, hi), zs, False, j),)
+                j = (send(r, "r_%d_%d" % (r, 2 * i + 1), V("rc%d" % r, lo, hi), zq, True, j),)
+                zq, zs = V("rc%d" % r, lo, hi), V("rs%d" % r, lo, hi)
             for b in range(4):
                 bank = V("pb%d" % banks[k % len(banks)], 0, hi - lo)
                 k += 1
-                mm(bank, [(V("wq", 128 * b, 128 * b + 128), V("wqs", 128 * b, 128 * b + 128), V("zq", lo, hi), V("zqs", lo, hi))])
+                mm(bank, [(V("wq", 128 * b, 128 * b + 128), V("wqs", 128 * b, 128 * b + 128), zq, zs)])
                 move(V("hs%d" % b, lo, hi), bank, scale=0.03125)
         nx = ("x2", "x3", "x4")[r - 1]
-        for lo, hi in XP:
+        for lo, hi in NP[r - 1]:
             for b in range(4):
                 out, lst = V(nx, 4 * lo + b, 4 * hi, 4), V(la, lo // 16, hi // 16)
                 if b in lent:
@@ -435,13 +490,13 @@ def rank_program(g, core, T, topo):
         if r < 3:
             lists()
     quant(V("vq"), V("vqs"), V("vt"))
-    for i, (a, b) in enumerate(XP):
+    for i, (a, b) in enumerate(XP[3]):
         quant(V("qc4", a, b), V("qs4", a, b), V("x4", 4 * a, 4 * b))
-        dma("S", [V("qc4", a, b)], [], lambda a=a, b=b: [(T.oc[:, 4 * a:4 * b], T["qc4"][:, a:b].bitcast(dt.uint8))], 150e3)
+        dma("S", [V("qc4", a, b)], [], lambda a=a, b=b: [(T.oc[:, 4 * a:4 * b], T["qc4"][:, a:b].bitcast(dt.uint8))], 512 * (b - a))
         mm(V("pb%d" % i, 0, b - a), [(V("vq"), V("vqs"), V("qc4", a, b), V("qs4", a, b))])
         move(V("yt", a, b), V("pb%d" % i, 0, b - a))
-        dma("S", [V("yt", a, b)], [], lambda a=a, b=b: [(T.y[:, a:b], T["yt"][:, a:b])], 150e3)
-    dma("S", [V("qs4")], [], lambda: [(T.osc[4 * k:4 * k + 4, :], T["qs4"][32 * k:32 * k + 4, :]) for k in range(4)], 100e3)
+        dma("S", [V("yt", a, b)], [], lambda a=a, b=b: [(T.y[:, a:b], T["yt"][:, a:b])], 512 * (b - a))
+    dma("S", [V("qs4")], [], lambda: [(T.osc[4 * k:4 * k + 4, :], T["qs4"][32 * k:32 * k + 4, :]) for k in range(4)], 16 * C)
 
     n = len(ops)
     users = [[] for _ in range(n)]
@@ -450,7 +505,7 @@ def rank_program(g, core, T, topo):
             users[j].append(i)
 
     def place(rank_of, before, after, back):
-        busy = {k: [] for k in "VAPGS"}
+        busy = {k: [] for k in "VAPGSD"}
         start, end, free, qof = [None] * n, [None] * n, [None] * n, [None] * n
         left = [len(before[i]) for i in range(n)]
         ready = [i for i in range(n) if not left[i]]
@@ -485,6 +540,7 @@ def rank_program(g, core, T, topo):
 
     def refine(plan):
         qof, seq = list(plan[3]), sorted(range(n), key=lambda j: (plan[1][j], j))
+        seq = [k for j in seq if qof[j] != "D" for k in ([j, landing[j]] if j in landing else [j])]
         above, hard, soft = [0] * n, [None] * n, [None] * n
         for i in range(n):
             firm = [j for j, wait in fore[i].items() if wait is True]
@@ -494,14 +550,14 @@ def rank_program(g, core, T, topo):
             hard[i] = [j for j in firm if not implied >> j & 1]
             soft[i] = [(j, wait) for j, wait in fore[i].items() if wait is not True and not implied >> j & 1]
             above[i] = implied | sum(1 << j for j in firm)
-        nxt = [[] for _ in range(n)]
+        every = [0] * n
         for i in range(n):
-            for j in hard[i] + [j for j, wait in soft[i]]:
-                nxt[j].append(i)
+            for j in fore[i]:
+                every[i] |= every[j] | 1 << j
 
         def replay(case, p, left, end):
-            free, wake, same, dear, lag = dict.fromkeys("VAPGSR"), CASES[case]["wake"], CASES[case]["same"], cost[case], late[case]
-            k, missing = p - 1, 6
+            free, wake, same, dear, lag = dict.fromkeys("VAPGSRD"), CASES[case]["wake"], CASES[case]["same"], cost[case], late[case]
+            k, missing = p - 1, 7
             while k >= 0 and missing:
                 if free[qof[seq[k]]] is None:
                     free[qof[seq[k]]] = left[seq[k]]
@@ -522,73 +578,126 @@ def rank_program(g, core, T, topo):
                 end[i] = t + lag[i]
             return max(end)
 
-        def longest(case):
-            left, end = state[case]
-            wake, way, last, before = max(CASES[case]["wake"], CASES[case]["same"]), [], {}, [None] * n
-            for i in seq:
-                before[i] = last.get(qof[i])
-                last[qof[i]] = i
-            i = max(range(n), key=lambda j: end[j])
-            while i is not None:
-                way.append(i)
-                t = left[i] - cost[case][i][qof[i]]
-                near = [j for j in hard[i] if end[j] + wake > t - 1.0] + [j for j, wait in soft[i] if end[j] + wake > t - 1.0]
-                if before[i] is not None and left[before[i]] > t - 1.0:
-                    near.insert(0, before[i])
-                i = near[int(rnd() * len(near))] if near else None
-            return way
+        def behind(case, i, q, tail, among):
+            wake, same, lag, far = CASES[case]["wake"], CASES[case]["same"], late[case][i], late[case][i]
+            for j, wait in uses[i]:
+                if among(j):
+                    far = max(far, tail[j] + (lag + (same if qof[j] == q else wake) if wait is True or (wait and qof[j] != q) else 0.0))
+            return far
+
+        def stretch(case, lo, hi):
+            left, tail, follows, after = state[case][0], [0.0] * n, {}, {}
+            for k in range(n - 1, -1, -1):
+                if k == hi - 1:
+                    after = dict(follows)
+                i = seq[k]
+                tail[i] = follows[qof[i]] = cost[case][i][qof[i]] + max(behind(case, i, qof[i], tail, lambda j: True), follows.get(qof[i], 0.0))
+            out = lambda j: pos[j] >= hi
+            free, fixed = dict.fromkeys("VAPGSRD", 0.0), 0.0
+            for i in seq[:lo]:
+                free[qof[i]] = left[i]
+                fixed = max(fixed, left[i] + behind(case, i, qof[i], tail, out))
+            span = max(left[i] - cost[case][i][qof[i]] + tail[i] for i in seq[lo:hi])
+            way = [i for i in seq[lo:hi] if left[i] - cost[case][i][qof[i]] + tail[i] > span - TUNE["near"]]
+            return free, fixed, after, {i: {q: behind(case, i, q, tail, out) for q in cost[case][i]} for i in seq[lo:hi]}, way
+
+        def whole(case, lo, hi, free, far, after, ways, way):
+            (left, end), free, wake, same, dear, lag = state[case], dict(free), CASES[case]["wake"], CASES[case]["same"], cost[case], late[case]
+            for i in seq[lo:hi]:
+                q = qof[i]
+                t = free[q]
+                for j in hard[i]:
+                    e = end[j] + (same if qof[j] == q else wake)
+                    if e > t:
+                        t = e
+                for j, wait in soft[i]:
+                    e = end[j] + wake if wait and qof[j] != q else left[j]
+                    if e > t:
+                        t = e
+                left[i] = free[q] = t = t + dear[i][q]
+                end[i] = t + lag[i]
+                t += ways[i][q]
+                if t > far:
+                    far = t
+            for q, t in after.items():
+                if free[q] + t > far:
+                    far = free[q] + t
+            return far
 
         seed = [TUNE["seed"]]
 
         def rnd():
             seed[0] = (seed[0] * 1103515245 + 12345) % 2 ** 31
             return seed[0] / 2.0 ** 31
-        state, pos = [([0.0] * n, [0.0] * n) for case in CASES], [0] * n
-        now = sum(replay(k, 0, *state[k]) for k in range(len(CASES)))
-        best, way = (now, list(seq), list(qof)), []
+        uses = [[] for _ in range(n)]
+        for i in range(n):
+            for j, wait in [(j, True) for j in hard[i]] + soft[i]:
+                uses[j].append((i, wait))
+        state, pos, each = [([0.0] * n, [0.0] * n) for case in CASES], [0] * n, range(len(CASES))
+        now = sum(replay(k, 0, *state[k]) for k in each)
+        best = (now, list(seq), list(qof))
         for turn in range(TUNE["tries"]):
             heat = TUNE["heat"] * (1.0 - turn / TUNE["tries"]) ** 2 + 1.0
-            if turn % 25 == 0:
+            if turn % TUNE["stay"] == 0:
+                for k in each:
+                    replay(k, 0, *state[k])
                 left = state[0][0]
                 seq.sort(key=lambda j: left[j] - cost[0][j][qof[j]])
-                way = longest(int(rnd() * len(CASES)))
                 for k in range(n):
                     pos[seq[k]] = k
-            i = way[int(rnd() * len(way))] if rnd() < TUNE["way"] else int(rnd() * n)
+                first = max(0, min(n - TUNE["wide"], int(rnd() * (n + TUNE["wide"] // 2)) - TUNE["wide"] * 3 // 4))
+                last = first + TUNE["wide"]
+                known = [stretch(k, first, last) for k in each]
+            way = known[int(rnd() * len(CASES))][4]
+            i = way[int(rnd() * len(way))] if rnd() < TUNE["way"] else seq[first + int(rnd() * TUNE["wide"])]
             q, at = qof[i], pos[i]
-            if q == "R":
+            if q in "RD":
                 continue
+            mate = None
             if len(ops[i]["cost"]) > 1 and rnd() < TUNE["change"]:
                 others = [k for k in ops[i]["cost"] if k != q]
                 qof[i] = others[int(rnd() * len(others))]
+                near = [j for j in seq[max(first, at - 6):min(last, at + 7)] if j != i and qof[j] == qof[i] and q in ops[j]["cost"]]
+                if near and rnd() < TUNE["trade"]:
+                    mate = near[int(rnd() * len(near))]
+                    qof[mate] = q
             ahead, hops, to = rnd() < 0.5, int(rnd() ** 2 * TUNE["hops"]) + (qof[i] == q), at
-            stop = set(hard[i] + [j for j, wait in soft[i]]) if ahead else set(nxt[i])
             k = at
             while hops:
                 k += -1 if ahead else 1
-                if k < 0 or k >= n or seq[k] in stop:
+                if k < first or k >= last:
                     break
-                if qof[seq[k]] == qof[i]:
+                if qof[seq[k]] == qof[i] and not (every[i] >> seq[k] & 1 if ahead else every[seq[k]] >> i & 1):
                     to, hops = k, hops - 1
             if to == at and qof[i] == q:
                 continue
-            seq.insert(to, seq.pop(at))
-            lo, hi = min(at, to), max(at, to)
-            for k in range(lo, hi + 1):
-                pos[seq[k]] = k
-            trial = [(list(left), list(end)) for left, end in state]
-            bound, mark = now - heat * math.log(1.0 - rnd()), 0.0
-            for k in range(len(CASES)):
-                mark += replay(k, lo, *trial[k])
-            if mark <= bound:
-                state, now = trial, mark
+            lo, hi = min(at, to), max(at, to) + 1
+            was = seq[lo:hi]
+            tied = [j == i or (every[i] >> j & 1 if ahead else every[j] >> i & 1) for j in was]
+            moved = [j for j, t in zip(was, tied) if bool(t) == ahead] + [j for j, t in zip(was, tied) if bool(t) != ahead]
+            if [j for j in moved if j in landing] != [j for j in was if j in landing]:
+                moved, lo, hi = seq[first:lo] + moved + seq[hi:last], first, last
+                was = seq[lo:hi]
+                own = {landing[j] for j in moved if j in landing}
+                if max(pos[j] for j in own) >= last:
+                    if mate is not None:
+                        qof[mate] = qof[i]
+                    qof[i] = q
+                    continue
+                moved = [k for j in moved if j not in own for k in ([j, landing[j]] if j in landing else [j])]
+            seq[lo:hi] = moved
+            mark = sum(whole(k, first, last, *known[k]) for k in each)
+            if mark <= now - heat * math.log(1.0 - rnd()):
+                now = mark
+                for k in range(lo, hi):
+                    pos[seq[k]] = k
                 if now < best[0]:
                     best = (now, list(seq), list(qof))
             else:
-                seq.insert(at, seq.pop(to))
+                seq[lo:hi] = was
+                if mate is not None:
+                    qof[mate] = qof[i]
                 qof[i] = q
-                for k in range(lo, hi + 1):
-                    pos[seq[k]] = k
         now, seq, qof = best
         spans = [replay(k, 0, *state[k]) for k in range(len(CASES))]
         TUNE["mark"] = [round(v) for v in spans]

@@ -4,25 +4,29 @@ from concourse.mybir import dt, AluOpType, ActivationFunctionType, AxisListType
 C = 416
 NL = C // 16
 MID = C // 2
-L = 14
-GT = 28
+L = 10
+GT = 24
+BW = 6 * GT + 4
+B2 = BW + 3 * GT + 128
+POLY = ((3.0, -6.0, -3.0, 1.0), (-1.0, 3.0, -2.0), (1.0, 0.0, -1.0), (-3.0, 3.0, 6.0))
 STEP = (1, 2, 3)
-LOADS = ("pkuxXmwsv", "SAASASSSS")
+LOADS = ("pkuxXm", "SAASAS")
+LATER = ("ws", "v", "")
 XP = (((0, 288), (288, C)),) * 3 + (((0, 160), (160, 288), (288, C)),)
 NP = XP[1:]
 ZP = ((0, 224), (224, C))
-HOME = (False, False, False)
-HP = ((0, 224), (224, C))
 CUTS = {"fb": (1, 1, 1, 1), "fp": (1, 1, 1, 1)}
 FP = ((0, 288), (288, C))
-MQ = ((0, 1), (2,), (3,))
-RP = (((0, C),),) * 3 + (((0, 224), (224, C)),)
-TP = (((0, 192), (192, C)),) * 3
+MQ = ((0,), (1,))
+RP = (((0, 224), (224, C)),) * 2
+TP = (((0, C),),) * 3
+TP1 = (((0, 192), (192, C)),) * 3
+AT = ((0, 2), (2, 4), (4, 5), (5, 6))
 HOLD = (3, 3, 4, 5)
 LENT = ((3,),) * 3
-AT = tuple((k, k + 1) for k in range(7))
+BANKS = {"fb": (2, 3, 4), "fp": (2, 3, 4, 6), "h": (2, 3, 4, 1, 0, 6, 7)}
 F32, BF16, F16, I32, U16, CODE, U8 = "float32", "bfloat16", "float16", "int32", "uint16", "float8_e4m3fn_x4", "uint8"
-MW = 512
+MW = 256
 
 SCRATCH, PART = {}, {}
 
@@ -40,34 +44,37 @@ def _parts(whole, cols, dtype, *names):
 
 _buf(512, F32, *["pb%d" % i for i in range(8)], where="psum")
 _buf(16, F32, "cols")
-_buf(128, BF16, "k0", "k1", "k2", "k3")
-_buf(4 * GT, BF16, "sp0", "sp1", "sp")
+_buf(128, BF16, "k0", "k1")
+_buf(4 * GT + 48, BF16, "sp", "sw")
+_buf(6, I32, "ip")
+_buf(8, F32, "fw")
 _buf(8, I32, "iu")
-_buf(8, U16, "lu0")
-_buf(NL, U16, "lq")
+_buf(8, U16, "lu1")
+_buf(7, U16, "lq")
 _parts("li", NL, I32, "kgw", "pgw", "mgw")
-_parts("lu", NL, U16, "l0", "lpw", "lm", "lm2", "lpp", "lz")
-_parts("lists", NL, U16, "l1", "l2", "l3")
-_buf(C, BF16, "place", "kb", "scw", "z1", "z2", "z3", "zc")
-_buf(2 * C, BF16, "tb", "bw", "p2")
-_buf(2 * C, F16, "swap", "pair")
+_parts("lu", NL, U16, "l0", "lpw", "lm", "lm2", "lpp")
+_parts("lists", NL, U16, "l1", "l2")
+_buf(C, BF16, "place", "kb", "z", "zc", "tp", "bo")
+_buf(2 * C, BF16, "tb", "bw", "bp", "swap")
+_buf(2 * C, F16, "pair")
 _buf(C, F32, "yt", "kk0", "kk1", "kk2", "kk3")
 _buf(520, BF16, "w1", "ones")
-_buf(4 * (3 * GT + 128), BF16, "w2")
-_buf(512, BF16, "w3", "ut", "vt", "at")
-_buf(24 * L + 448, F32, "chain")
-PART.update(dv=("chain", 0, 24 * L), sc=("chain", 24 * L, 448))
+_buf(4 * B2, BF16, "w2")
+_buf(512, BF16, "w3", "ut", "vt")
+_buf(576, BF16, "at")
+_buf(28 * L, F32, "chain")
+PART.update(six=("chain", 20, 12), sc=("chain", 4 * L, GT * L))
 _buf(64, BF16, "f0", "f1", "f2")
-_buf(28, U16, "la4")
+_buf(24, U16, "la4")
 _buf(C, F32, "pl_t")
 _buf(32, F32, "lw", "lt")
 _buf(4 * NL, F32, "sl")
 _buf(8 * NL, F32, "cs")
-_buf(2 * NL, F32, "su")
+_buf(3 * NL, F32, "su")
 _buf(NL, F32, "sf", "d3")
 _buf(4 * C, BF16, "xt", "x2", "x3", "x4", "zt")
 _buf(4 * MW, BF16, "mt")
-for _c, _s, _n in (("uq", "uqs", 128), ("uc", "ucs", 128), ("vq", "vqs", 128), ("wq", "wqs", 512), ("b2", "b2s", 3 * GT + 128), ("b3", "b3s", 128), ("mq", "mqs", MW), ("aq", "aqs", 128), ("zq1", "zs1", C), ("zq2", "zs2", C), ("zq3", "zs3", C)):
+for _c, _s, _n in (("uq", "uqs", 128), ("vq", "vqs", 128), ("wq", "wqs", 512), ("ud", "uds", 128), ("b2", "b2s", B2), ("b3", "b3s", 128), ("mq", "mqs", MW), ("aq", "aqs", 128), ("zq1", "zs1", C), ("zq2", "zs2", C), ("zq3", "zs3", C)):
     _buf(_n, CODE, _c)
     _buf(_n, U8, _s)
 _parts("ec", 128, CODE, *["e%d" % i for i in range(4)])
@@ -76,7 +83,7 @@ _parts("hs", C, F32, *["hs%d" % i for i in range(4)])
 _parts("fb", C, BF16, *["fb%d" % i for i in range(4)])
 _parts("fp", C, BF16, *["fp%d" % i for i in range(4)])
 _parts("tg", C, BF16, "tg1", "tg2", "tg3")
-_parts("tsum", C, BF16, "ts0", "ts1", "ts2", "ts3")
+_parts("tsum", C, BF16, "ts1", "ts0", "ts3", "ts2")
 for _i in (1, 2, 3, 4):
     _buf(C, CODE, "qc%d" % _i)
     _buf(C, U8, "qs%d" % _i)
@@ -94,8 +101,27 @@ CASES = [dict(zip(NAMES, c)) for c in (
     (1.06, 1.54, 58.0, 194.0, 35.0, 92.0, 33.0, 42.0, 30.0, 0.99, 0.63, 117.0, 920.0, 70.0, 1580.0, 364.0, 1000.0, 350.0, 105.0, 1.0),
     (1.50, 1.61, 256.0, 265.0, 30.0, 74.0, 30.0, 48.0, 51.0, 0.99, 0.63, 58.0, 1630.0, 62.0, 520.0, 223.0, 2710.0, 350.0, 39.0, 5.0),
     (1.08, 2.06, 140.0, 280.0, 43.0, 49.0, 31.0, 22.0, 74.0, 1.11, 0.64, 95.0, 1580.0, 50.0, 2430.0, 294.0, 1830.0, 350.0, 30.0, 0.0))]
+WORTH = (1.0, 0.6, 1.6, 0.8, 1.2)
+CHAIN = " ".join("+sc.%d" % k for k in range(1, 21)) + " +at +at.1 +at.2 +at.3"
+START = {"S": "dma dma.3 dma.5 +dma +dma.1 +dma.2",
+         "A": "dma.1 dma.2 dma.4 mt chain w2.8 six six.2 fw.1 fw.4 fw.3 kb tb.1 tb uds tg1 tg1.1 w2 w2.2 w2.3 cols.4 +bw +bw.1 tg2.1 tg2 w2.5 +mt +mt.1 +mt.2 tg3.1 tg3 cols.3 +fb0 cs at.1 +fb2 +at.4 +at.5 +at.6 cs.4 +at.7 cs.2 +fp3 +fb1",
+         "V": "ones ip.3 ip.4 ip.2 ip.1 mt.1 cols.8 w2.9 lq cols.5 fw cols.6 place fw.5 six.3 cols.9 fw.2 six.1 cols.7 lu1 lpw l0 lpp sw kb.1 uq w2.1 cols.1 w2.4 w2.7 ud kb.2 +qc cols.2 pair +qc.1 e3 ts1 +bo l1 +bo.1 "
+              "f2 e2 +bp w2.6 ts2 la4.1 e0 l2 b2 +mt.3 +mq ts0 +mq.1 e1 lm2 la4 +sc ts3 +sc.1 +sc.2 +sc.3 +sc.4 sf +sc.5 +sc.6 +sc.7 +sc.8 su +sc.9 +sc.10 +sc.11 +sc.12 +sc.13 +sc.14 +sc.15 +sc.16 "
+              "+sc.17 +sc.18 +sc.19 +sc.20 cs.1 +at +at.1 +at.2 +at.3 d3 b3 +aq cs.3 +fp2 +sl lm +la",
+         "G": "ip iu cols k0 sp k1 sp.1 w1 f0 sc f1 +send at +send.1 w3 w3.3 w3.1 +send.2 swap w3.5 w3.2 w3.4 lw",
+         "P": "+ud*qc.1 +ud*qc +ud*qc.2 +ud*qc.3 +e0*qc +mq*b2 +mq*b2.1 +mq*b2.2 +e2*qc +e3*qc +e1*qc +e3*rc +e2*rc +aq*b3 +e0*rc +e3*rc.1 +e1*rc"}
+ROUND = {"S": "+dma", "G": "send.3 +send +send.1 +send.2",
+         "A": "z fp1 fp2.1 fp3.1 fp1.1 zt zt.2 zt.4 zt.5 zt.6 tg1 hs3 hs1 hs1.1 hs3.1 hs0.1 kk3 kk3.1 tg2 +bw +bw.1 tg3 +mt +mt.2 +fb1 +fb0 +fb2 +at.4 cs.3 +at.5 +at.6 +at.7 cs.1 +fp0 +fp1 +fp3",
+         "V": "-pair.1 zc fp0.1 swap zt.3 zt.1 zt.7 zq tb zq.1 hs0 hs2 hs2.1 ts1 x.2 x.6 x.1 l1 x x.3 x.7 x.4 +qc x.5 tp +qc.1 ts2 +bo l2 lpp +bo.1 +bp ts3 +mt.1 +mt.3 +mq +mq.1 su +sc sf cs " + CHAIN + " d3 +aq cs.2 +fp2 +sl +la",
+         "P": "e1*rc e3*rc.1 e0*rc.1 e1*rc.1 e2*rc.1 wq*zq.3 wq*zq wq*zq.2 wq*zq.6 wq*zq.1 wq*zq.5 wq*zq.7 wq*zq.4 +ud*qc.1 +ud*qc +ud*qc.2 +ud*qc.3 +e1*qc +e0*qc +e2*qc +mq*b2 +mq*b2.1 +mq*b2.2 +e3*qc +e0*rc +e3*rc +e1*rc +e2*rc +aq*b3 +e0*rc.1"}
+END = {"S": "dma.1 dma.2 +dma +dma.1 +dma.2 +dma.3 +dma.4 +dma.6 +dma.5", "G": "send.3",
+       "A": "z fp2.1 fp3.1 fp1.1 zt.2 zt zt.7 zt.5 hs0 hs1 hs0.1 hs2.1 hs3.1 hs2 kk3 kk3.1 pl_t kk3.2 +yt +yt.1",
+       "V": "fp0.1 zc lw swap -vq zt.3 zt.1 zt.4 zq zt.6 lt zq.1 hs3 tb hs1.1 x.8 x.5 x x.1 x.2 x.3 x.4 +qc x.6 x.7 x.9 +qc.1 x.10 x.11 +qc.2 +yt.2",
+       "P": "e3*rc.1 e1*rc.1 e2*rc.1 wq*zq wq*zq.3 wq*zq.1 wq*zq.4 wq*zq.5 wq*zq.6 wq*zq.7 wq*zq.2 +vq*qc +vq*qc.1 +vq*qc.2"}
+ORDER = [(0, START), (1, ROUND), (2, ROUND), (3, END)]
 PLANS = []
-TUNE = {"xor": (0, C), "trade": 0.4, "two": 1, "sq": "A", "twice": 1, "stay": 60, "wide": 36, "near": 150.0, "tries": 330000, "heat": 200.0, "way": 0.8, "change": 0.3, "hops": 4, "spare": 0.1, "turns": 4, "seed": 6}
+TUNE = {"late": 2, "trade": 0.4, "stay": 60, "wide": 60, "near": 250.0, "tries": 1200000, "heat": 110.0, "way": 0.5, "change": 0.3,
+        "hops": 14, "spare": 0.1, "seed": 6, "pace": 0.7, "quit": 150.0}
 
 
 def _price(m, kind, n=0.0):
@@ -121,7 +147,7 @@ def rank_program(g, core, T, topo):
         return
     A = AluOpType
     AF = ActivationFunctionType
-    ops, seen, loading = [], {}, []
+    ops, seen, loading, phase, named = [], {}, [], [0], {}
 
     def V(name, lo=0, hi=None, st=1):
         whole, at, cols = PART.get(name, (name, 0, SCRATCH.get(name, (0, (0, 0)))[1][1]))
@@ -130,6 +156,8 @@ def rank_program(g, core, T, topo):
     def ap(v):
         if not isinstance(v, tuple):
             return v
+        if len(v) > 4:
+            return T[v[0]][:, v[2] - 1:v[1] - 1:-v[3]]
         return T[v[0]][:, v[1]:v[2]] if v[3] == 1 else T[v[0]][:, v[1]:v[2]:v[3]]
 
     def src(v, l):
@@ -137,6 +165,10 @@ def rank_program(g, core, T, topo):
 
     def n_of(v):
         return -(-(v[2] - v[1]) // v[3])
+
+    def label(v):
+        name = ([p for p, (whole, at, cols) in PART.items() if whole == v[0] and at <= v[1] < at + cols] + [v[0]])[0]
+        return name[:-1] if name[:-1] in ("qc", "rc", "zq", "x", "z") and name[-1].isdigit() or name in ("la1", "la2", "la3") else name
 
     def add(cost, reads, writes, emit, kind="c", sem=None, amount=0, after=(), behind=()):
         i = len(ops)
@@ -156,11 +188,17 @@ def rank_program(g, core, T, topo):
             deps[j] = True
         for j in list(behind) + (loading[-1:] if "A" in cost else []):
             deps[j] = False
+        if kind != "r":
+            name = label(reads[0]) + "*" + label(reads[2]) if "P" in cost else label(writes[0]) if kind == "c" else "send" if "G" in cost else "dma"
+            k = 0
+            while (phase[0], name, k) in named:
+                k += 1
+            named[phase[0], name, k] = i
         ops.append({"cost": cost, "deps": deps, "emit": emit, "kind": kind, "sem": sem, "amount": amount})
         return i
 
     def narrow(*views):
-        return all(SCRATCH[v[0]][2] in (BF16, F16, U16) for v in views if isinstance(v, tuple))
+        return all(SCRATCH[v[0]][2] in (BF16, F16, U16) for v in views if isinstance(v, tuple) and n_of(v) > 1)
 
     def costs(qs, out, ins, lst, both=False):
         n = n_of(out)
@@ -184,12 +222,12 @@ def rank_program(g, core, T, topo):
     def scan(out, d0, d1, first=0.0):
         return add(costs("V", out, (d0, d1), None), [d0, d1], [out], lambda e, q: e.tensor_tensor_scan(ap(out), ap(d0), ap(d1), first, A.mult, A.add))
 
-    def move(out, in_, lst=None, scale=None, plus=None, relu=False, qs="VA"):
+    def move(out, in_, lst=None, scale=None, plus=None, relu=False, qs="VA", rows=128):
         def emit(e, q):
-            o, i = ap(out), src(in_, lst)
+            o, i = (ap(out), src(in_, lst)) if rows == 128 else (T[out[0]][0:rows, out[1]:out[2]:out[3]], T[in_[0]][0:rows, in_[1]:in_[2]:in_[3]])
             if q == "V":
                 if relu:
-                    return e.tensor_scalar(o, i, 0.0, scale, A.is_gt, A.mult)
+                    return e.tensor_scalar(o, i, 0.0, None, A.is_gt)
                 if scale is None and plus is None:
                     return e.tensor_copy(o, i)
                 if plus is None:
@@ -198,7 +236,7 @@ def rank_program(g, core, T, topo):
                     return e.tensor_scalar(o, i, ap(plus), None, A.add)
                 return e.tensor_scalar(o, i, ap(scale), ap(plus), A.mult, A.add)
             if relu:
-                return e.activation(o, i, AF.Relu, scale=scale)
+                return e.activation(o, i, AF.Relu)
             if plus is not None:
                 return e.activation(o, i, AF.Identity, bias=ap(plus), scale=1.0 if scale is None else ap(scale))
             if scale is not None:
@@ -206,11 +244,9 @@ def rank_program(g, core, T, topo):
             return e.activation(o, i, AF.Copy)
         return add(costs(qs, out, (in_, scale, plus), lst), [in_, lst, scale, plus], [out], emit)
 
-    def signs(out, in_, loose=False, qs="VA"):
-        if loose:
-            return add(costs("VA", out, (in_,), None), [in_], [out], lambda e, q: e.tensor_scalar(ap(out), ap(in_), 0.0, None, A.is_gt) if q == "V" else e.activation(ap(out), ap(in_), AF.Sign))
-        return add(costs(qs, out, (in_,), None), [in_, TINY], [out],
-                   lambda e, q: e.tensor_scalar(ap(out), ap(in_), 0.0, 0.5, A.is_gt, A.subtract) if q == "V" else e.activation(ap(out), ap(in_), AF.Sign, bias=ap(TINY)))
+    def signs(out, in_, mask):
+        return add(costs("VA" if mask == HIGH else "V", out, (in_,), None), [in_, mask], [out],
+                   lambda e, q: e.tensor_scalar(ap(out), ap(in_), 0.0, ap(mask), A.is_gt, A.mult) if q == "V" else e.activation(ap(out), ap(in_), AF.Sign, scale=ap(mask)))
 
     def fill(out, val, qs="VAG"):
         ones = V("ones", 0, n_of(out))
@@ -230,13 +266,8 @@ def rank_program(g, core, T, topo):
     def quant(c, s, t):
         return add({"V": ("quant", n_of(t))}, [t], [c, s], lambda e, q: e.quantize_mx(ap(c), ap(s), ap(t)))
 
-    def mm(out, terms, after=(), start=True, stop=True, behind=()):
-        def emit(e, q):
-            last = None
-            for k, (a, b, c, d) in enumerate(terms):
-                last = e.matmul_mx(ap(out), ap(a), ap(b), ap(c), ap(d), start and k == 0, stop and k == len(terms) - 1)
-            return last
-        return add({"P": [("P", n_of(out))] * len(terms)}, [v for t in terms for v in t], [out], emit, after=after, behind=behind)
+    def mm(out, a, b, c, d, start=True, stop=True, behind=()):
+        return add({"P": ("P", n_of(out))}, [a, b, c, d], [out], lambda e, q: e.matmul_mx(ap(out), ap(a), ap(b), ap(c), ap(d), start, stop), behind=behind)
 
     def iota(out, pattern, base, cm):
         def emit(e, q):
@@ -274,8 +305,7 @@ def rank_program(g, core, T, topo):
         return j
 
     col = lambda i: V("cols", i, i + 1)
-    SC, ISC, HALF, OWN, TWICE = [col(i) for i in range(5)]
-    TINY = -2.0 ** -100
+    SC, ISC, HALF, OWN, TWICE, WEIGHT, FIRST, HIGH, LOW, ODD = [col(i) for i in range(10)]
     KG, PG, MG = V("kgw", 0, NL), V("pgw", 0, NL), V("mgw", 0, NL)
 
     a, b = XP[0][0][1], C
@@ -294,10 +324,12 @@ def rank_program(g, core, T, topo):
     scan(V("place"), V("ones", 0, C), V("ones", 0, C), -MID - 1.0)
     fill(V("lw", NL), 0.0)
     iota(OWN, [[0, 1]], 0, 1)
-    ts(V("lq"), V("ones", 0, NL), OWN, None, A.mult)
+    ts(V("lq"), V("ones", 0, 7), OWN, None, A.mult)
     keep(V("k0"), V("ones", 0, 128), [[1, 128]], A.not_equal, 0, -1)
     keep(V("k1"), V("k0"), [[1, 128]], A.not_equal, -1, -1, 2.0 ** 20)
-    move(V("kb"), V("k1"), lst=V("lq"))
+    move(V("kb", 0, 112), V("k1"), lst=V("lq"))
+    move(V("kb", 112, 224), V("kb", 0, 112))
+    move(V("kb", 224), V("kb", 0, C - 224))
     add(costs("V", ISC, (), None), [V("kb", 0, 16)], [ISC], lambda e, q: e.tensor_reduce(ap(ISC), ap(V("kb", 0, 16)), AxisListType.X, A.max))
     ts(SC, ISC, 1.0, 2.0 ** -20, A.is_equal, A.max)
     move(HALF, SC, scale=0.5)
@@ -306,155 +338,146 @@ def rank_program(g, core, T, topo):
     ts(V("l0"), KG, 2.0, 1.0, A.mult, A.add)
     move(V("lm"), MG, qs="V")
     ts(V("lm2"), MG, 2.0, 1.0, A.mult, A.add)
+    ts(V("lpp"), PG, 2.0, 1.0, A.mult, A.add)
     ts(V("ts0", 15, C, 16), KG, -float(MID), ISC, A.add, A.mult)
+    move(V("cs", 3, 4 * NL, 4), V("ts0", 15, C, 16), scale=2.0)
 
-    def lists(steps=(("tb", 0), ("tb", 1), ("tb", 2))):
+    def as_list(out, sums, flat):
+        scan(sums, V("kb"), flat)
+        if out:
+            ts(out, V(sums[0], sums[1] + 15, sums[2], 16), TWICE, 2 * MID + 1.25, A.mult, A.add)
+
+    def lists(pieces):
         for n in (1, 2, 3):
-            for lo, hi in TP[n - 1]:
-                move(V("tg%d" % n, lo, hi), V(steps[n - 1][0]), lst=V("l%d" % steps[n - 1][1], lo // 16, hi // 16))
-            scan(V("ts%d" % n), V("kb"), V("tg%d" % n))
-            ts(V("l%d" % n), V("ts%d" % n, 15, C, 16), TWICE, 2 * MID + 1.25, A.mult, A.add)
+            for lo, hi in pieces[n - 1]:
+                move(V("tg%d" % n, lo, hi), V("tb"), lst=V("l%d" % (n - 1), lo // 16, hi // 16))
+            as_list(V("l%d" % n) if n < 3 else None, V("ts%d" % n), V("tg%d" % n))
         some = lambda n, k: V("tsum", n * C + 15, (n + k) * C, 16)
-        move(V("cs", 3, 8 * NL, 4), some(1, 2), scale=2.0)
-        tt(V("su"), some(0, 2), some(2, 2), A.add)
-        tt(V("cs", 1, 8 * NL, 4), V("su"), V("cs", 3, 8 * NL, 4), A.subtract)
+        tt(V("su"), some(1, 3), some(0, 3), A.subtract)
+        tt(V("cs", 1, 8 * NL, 4), V("su", NL), V("su", 0, 2 * NL), A.subtract)
         tt(V("d3"), V("cs", 4 * NL + 1, 8 * NL, 4), V("cs", 1, 4 * NL, 4), A.subtract)
         move(V("cs", 0, 4 * NL, 4), V("d3"), scale=1.0 / 3.0)
         tt(V("sf"), some(2, 1), some(0, 1), A.subtract)
         tt(V("cs", 2, 4 * NL, 4), V("sf"), V("cs", 0, 4 * NL, 4), A.subtract)
+        move(V("cs", 3, 4 * NL, 4), some(0, 1), scale=2.0, rows=16)
 
     for lo, hi in ((0, 224), (224, C)):
         move(V("tb", 2 * lo + 1, 2 * hi, 2), V("place"), lst=V("lpw", lo // 16, hi // 16))
-    if TUNE["twice"]:
-        ts(V("lpp"), PG, 2.0, 1.0, A.mult, A.add)
-        for lo, hi in ((0, 224), (224, C)):
-            move(V("p2", 2 * lo + 1, 2 * hi, 2), V("tb"), lst=V("lpp", lo // 16, hi // 16))
-        lists((("tb", 0), ("p2", 0), ("p2", 1)))
-    else:
-        lists()
+    lists(TP1)
     move(V("pair", 1, 2 * C, 2), V("tb", 1, 2 * C, 2), qs="V")
     tt(V("pair", 0, 2 * C, 2), V("tb"), V("pair", 1, 2 * C, 2), A.subtract, lst=V("lm2"))
-    ts(V("swap", 0, 2 * C, 2), V("ones", 0, C), 0.0, None, A.mult)
+    fill(V("swap", 0, 2 * C, 2), 0.0)
     quant(V("uq"), V("uqs"), V("ut"))
     iota(V("iu"), [[16, 8]], 0, 0)
-    if TUNE["two"]:
-        move(V("lu0"), V("iu"), qs="V")
-    else:
-        ts(col(7), V("kb", 1, 2), 0.0, None, A.is_equal)
-        ts(V("lu0"), V("iu"), col(7), None, A.add)
-        fill(V("bw", 0, 2 * C, 2), 0.0)
-    add(costs("V", V("uc"), (), V("lu0")), [V("uq"), V("lu0")], [V("uc")], lambda e, q: e.tensor_copy(ap(V("uc")).bitcast(dt.uint32), ap(V("uq")).bitcast(dt.uint32).indirect(ap(V("lu0")))))
-    add(costs("VA", V("ucs"), (), V("lu0")), [V("uqs"), V("lu0")], [V("ucs")],
-        lambda e, q: e.tensor_copy(ap(V("ucs")), src(V("uqs"), V("lu0"))) if q == "V" else e.activation(ap(V("ucs")), src(V("uqs"), V("lu0")), AF.Copy))
+    iota(V("ip", 0, 1), [[0, 1]], 0, 1)
+    for k, bits in enumerate((1, 124, 14, 13)):
+        ts(V("ip", k + 1, k + 2), V("ip", 0, 1), bits, None, A.bitwise_and)
+    ts(ODD, V("ip", 4, 5), 1.0, None, A.is_equal)
+    ts(V("lu1"), V("iu"), ODD, None, A.add)
+    add(costs("V", V("ud"), (), V("lu1")), [V("uq"), V("lu1")], [V("ud")], lambda e, q: e.tensor_copy(ap(V("ud")).bitcast(dt.uint32), ap(V("uq")).bitcast(dt.uint32).indirect(ap(V("lu1")))))
+    move(V("uds"), V("uqs"), lst=V("lu1"))
     keep(V("w1"), V("ones", 0, 520), [[1, 520]], A.is_equal, -4, -4)
     for b in range(4):
         quant(V("e%d" % b), V("es%d" % b), V("w1", 4 - b, 516 - b))
-    iota(V("sp0"), [[-16, 7], [256, 4], [-256, 4]], 1, 1)
-    keep(V("sp1"), V("sp0"), [[-16, 7], [256, 4], [-256, 4]], A.is_ge, 0, 1)
-    keep(V("sp"), V("sp1"), [[16, 7], [-256, 4], [256, 4]], A.is_ge, 1, -1)
-    for s, val in enumerate((-1.0, 3.0, -6.0, 6.0)):
-        move(V("w2", 4 * GT * s, 4 * GT * (s + 1)), V("sp"), scale=val)
-    fill(V("w2", 16 * GT), 0.0)
+    iota(V("sp", 0, 4 * GT), [[-16, 6], [256, 4], [-256, 4]], 96, 0)
+    iota(V("sp", 4 * GT), [[0, 3], [256, 4], [-256, 4]], 0, 0)
+    ts(WEIGHT, V("ip", 1, 2), 3.0, -1.0, A.mult, A.add)
+    move(FIRST, V("ip", 2, 3), qs="V")
+    ts(HIGH, V("ip", 3, 4), 2.0, None, A.is_equal)
+    ts(LOW, V("ip", 3, 4), 2.0, None, A.not_equal)
+    ts(V("sw"), V("sp"), FIRST, WEIGHT, A.is_equal, A.mult)
+    move(V("w2", 4 * B2 - 48), V("sw", 4 * GT), scale=HIGH)
+    for k, (n, s) in enumerate([(n, s) for n in (0, 1) for s in range(len(POLY[2 * n]))]):
+        low, high, at = POLY[2 * n][s], (POLY[2 * n + 1] + (0.0,))[s], 4 * BW * n + 4 * GT * s
+        if (low, high) != (1.0, 0.0):
+            move(V("fw", k, k + 1), HIGH, scale=high - low, plus=low)
+        move(V("w2", at, at + 4 * GT), V("sw", 0, 4 * GT), scale=V("fw", k, k + 1) if (low, high) != (1.0, 0.0) else LOW)
+    fill(V("w2", 16 * GT, 4 * BW), 0.0)
+    fill(V("w2", 4 * BW + 12 * GT, 4 * B2 - 48), 0.0)
     quant(V("b2"), V("b2s"), V("w2"))
     keep(V("w3", 0, C), V("ones", 0, C), [[4, NL], [0, 4], [1, 4]], A.is_equal, 0, -1)
     fill(V("w3", C), 0.0)
     for t in range(4):
         fill(V("w3", t, C, 16), 0.0)
     quant(V("b3"), V("b3s"), V("w3"))
-    fill(V("dv"), 0.0)
-    fill(V("sc", 0, 64), 0.0)
-    for k in range(3):
-        fill(V("sc", 64 + 4 * L + k, None, 64), 0.0)
-    for lo, hi, val in ((4, 24 * L, -2.0), (5, 24 * L, 1.0), (6, 24 * L, 1.0), (7, GT * L, 1.0 / 36.0), (8, GT * L, 1.0), (9, GT * L, 1.0)):
-        fill(V("chain", lo, hi, L), val, "V" if lo == 7 else "VAG")
-    iota(V("f0"), [[0, 4], [L, 4], [0, 4]], 5, 0)
-    keep(V("f1"), V("f0"), [[1, 4], [0, 4], [-1, 4]], A.is_equal, 0, 0, 10.0)
+    fill(V("chain"), 1.0)
+    for t in range(4):
+        fill(V("chain", 28 + t, 24 * L, 4 * L), 1.0 / 6.0)
+    fill(V("sc", 36, None, 4 * L), 0.0)
+    iota(V("f0"), [[0, 4], [1, 4], [0, 4]], 12, 0)
+    keep(V("f1"), V("f0"), [[1, 4], [0, 4], [-1, 4]], A.is_equal, 0, 0, 36.0)
     scan(V("f2"), V("kb", 0, 64), V("f1"))
     for k in range(max(hi - lo for lo, hi in AT)):
-        ts(V("la4", 4 * k, 4 * k + 4), V("f2", 15, 64, 16), SC, 64 * k + 0.25, A.mult, A.add)
+        ts(V("la4", 4 * k, 4 * k + 4), V("f2", 15, 64, 16), SC, 4 * L * k + 0.25, A.mult, A.add)
     fill(V("at", 0, 64), 0.0)
-    for n in range(4):
+    fill(V("at", 448, 512), 0.0)
+    for n in range(2):
         fill(V("mt", 512 * n + C, 512 * n + 512), 0.0)
 
-    def unpack(to, c, s, pieces, banks, skip=(), every=False):
+    def unpack(to, c, s, pieces, banks, skip=()):
         k = 0
         for lo, hi in pieces:
             for b in range(4):
                 bank = V("pb%d" % (HOLD[b] if b in skip else banks[k % len(banks)]), 0, hi - lo)
-                mm(bank, [(V("e%d" % b), V("es%d" % b), V(c, lo, hi), V(s, lo, hi))])
-                if every or b not in skip:
+                mm(bank, V("e%d" % b), V("es%d" % b), V(c, lo, hi), V(s, lo, hi))
+                if b not in skip:
                     cuts = [(hi - lo) * u // CUTS[to][b] for u in range(CUTS[to][b] + 1)]
                     for u, w in zip(cuts, cuts[1:]):
                         move(V("%s%d" % (to, b), lo + u, lo + w), V(bank[0], u, w))
                 k += b not in skip
 
     for r in (1, 2, 3):
+        phase[0] = r
         x, qc, qs, la = ("xt", "x2", "x3")[r - 1], "qc%d" % r, "qs%d" % r, "la%d" % r
         for i, (lo, hi) in enumerate(XP[r - 1]):
             quant(V(qc, lo, hi), V(qs, lo, hi), V(x, 4 * lo, 4 * hi))
-            mm(V("pb%d" % i, 0, hi - lo), [(V("uq" if TUNE["two"] else "uc"), V("uqs" if TUNE["two"] else "ucs"), V(qc, lo, hi), V(qs, lo, hi))])
-            signs(V("bw", 2 * lo + 1, 2 * hi, 2), V("pb%d" % i, 0, hi - lo), TUNE["two"], "VA" if TUNE["two"] else TUNE["sq"])
-        j, home = (), HOME[r - 1]
-        for i, (codes, lo, hi) in enumerate(() if home else ((True,) + XP[r - 1][0], (False, 0, C), (True,) + XP[r - 1][1])):
+            for bank, out, mask in ((i, V("bw", 2 * lo + 1, 2 * hi, 2), HIGH), (6 + i, V("bo", lo, hi), LOW)):
+                mm(V("pb%d" % bank, 0, hi - lo), V("ud"), V("uds"), V(qc, lo, hi), V(qs, lo, hi))
+                signs(out, V("pb%d" % bank, 0, hi - lo), mask)
+        j = ()
+        for i, (codes, lo, hi) in enumerate(((True,) + XP[r - 1][0], (False, 0, C), (True,) + XP[r - 1][1])):
             j = (send(r, "r_%d_%d" % (r, i), V(("rc%d" if codes else "rs%d") % r, lo, hi), V(qc if codes else qs, lo, hi), codes, j),)
-        term = lambda n, at: (V("mq", 128 * n, 128 * n + 128), V("mqs", 128 * n, 128 * n + 128), V("b2", GT * at, GT * at + 128), V("b2s", GT * at, GT * at + 128))
-        done = {}
+        tt(V("bp", 1, 2 * C, 2), V("bw"), V("bo"), A.add, lst=V("lpp"))
+        dma("S", [], [V("bo")], lambda: [(T["bo"][k::16, :], T["bo"][0::16, :]) for k in (1, 2, 3)], 48 * C)
+        term = lambda n, lo, hi: (V("mq", 128 * n, 128 * n + 128), V("mqs", 128 * n, 128 * n + 128), V("b2", lo, hi), V("b2s", lo, hi))
+        done = ()
         for rows in MQ:
             lo, hi = 128 * rows[0], 128 * rows[-1] + 128
             for n in rows:
                 for a, b in RP[n]:
-                    move(V("mt", 512 * n + a, 512 * n + b), V("bw"), lst=V("l%d" % n, a // 16, b // 16), scale=(6.0, 6.0, 3.0, 1.0)[n], relu=True)
-            quant(V("mq", lo, hi), V("mqs", lo, hi), V("mt", 4 * lo, 4 * hi))
-            if 1 in rows:
-                mm(V("pb0", 0, 128), [term(1, 3)])
-                for s in range(3):
-                    move(V("sc", 4 + s, 4 * L, L), V("pb0", 0, 4), scale=1.0 / 36.0, plus=s - 2.0 or None)
-            for bank, last in (("pb1", 2), ("pb6", 3)):
-                some = [n for n in rows if n <= last]
-                if some:
-                    done[bank] = (mm(V(bank, 0, 128), [term(n, n) for n in some], start=bank not in done, stop=last in some, behind=done.get(bank, ())),)
-        for s in range(4):
-            move(V("dv", s, None, L), V("pb1" if s else "pb6", GT * s + 4, GT * (s + 1)))
+                    move(V("mt", 512 * n + a, 512 * n + b), V("bp"), lst=V("l%d" % (2 * n), a // 16, b // 16), relu=True)
+            i = quant(V("mq", lo, hi), V("mqs", lo, hi), V("mt", 4 * lo, 4 * hi))
+            if 0 in rows:
+                for name in LATER[r - 1]:
+                    ops[dma("S", [], [loads[name][0]], loads[name][1], loads[name][2])[0]]["deps"][i] = True
+                mm(V("pb0", 0, 128), *term(0, B2 - 128, B2))
+                tt(V("sc", 12, 24), V("pb0", 116, 128), V("six"), A.mult)
+            for n in rows:
+                done += (mm(V("pb1", 0, BW), *term(n, BW * n, BW * (n + 1)), start=not done, stop=n == MQ[-1][-1], behind=done),)
         for k in range(1, 7):
-            scan(V("sc", 64 * k, 64 * k + 4 * L), V("sc", 64 * k - 61, 64 * k - 61 + 4 * L), V("dv", 4 * L * (k - 1), 4 * L * k))
+            for t in range(4):
+                at, c = 4 * L * (k - 1) + t, 4 * (6 - k) + t
+                if k < 6:
+                    scan(V("sc", at + 4 * L, at + 4 * L + 21, 4), V("sc", at + 8, at + 29, 4), V("pb1", c, c + 5 * GT + 1, GT))
+                else:
+                    scan(V("at", 448 + 4 * t, 448 + 4 * t + 103, 17) + (True,), V("sc", at + 8, at + 33, 4), V("pb1", c, c + 6 * GT + 1, GT))
         for lo, hi in AT:
-            move(V("at", 64 * lo + 64, 64 * hi + 64), V("sc", 64 * lo, 64 * hi), lst=V("la4", 0, 4 * (hi - lo)))
-        quant(V("aq"), V("aqs"), V("at"))
-        mm(V("pb7", 0, 128), [(V("aq"), V("aqs"), V("b3"), V("b3s"))])
+            move(V("at", 64 * lo + 64, 64 * hi + 64), V("sc", 4 * L * lo, 4 * L * hi), lst=V("la4", 0, 4 * (hi - lo)))
+        quant(V("aq"), V("aqs"), V("at", 0, 512))
+        mm(V("pb7", 0, 128), V("aq"), V("aqs"), V("b3"), V("b3s"))
         scan(V("sl"), V("pb7", 0, 4 * NL), V("cs", 0, 4 * NL))
         ts(V(la), V("sl", 3, 4 * NL, 4), HALF, MID + 0.25, A.mult, A.add)
-        if not home:
-            send(r, "r_l%d" % r, V("lp%d" % r), V(la), False, j)
+        send(r, "r_l%d" % r, V("lp%d" % r), V(la), False, j)
         lent = LENT[r - 1]
-        banks = [k for k in (2, 3, 4, 5, 1, 0, 6, 7) if k not in [HOLD[b] for b in lent]]
-        sw, lz = V("scw"), V(la)
-        if TUNE["two"]:
-            mm(V("pb0", 0, C), [(V("uc"), V("ucs"), V(qc), V(qs))])
-            if TUNE["xor"]:
-                for lo, hi in zip(TUNE["xor"], TUNE["xor"][1:]):
-                    ts(V("scw", lo, hi), V("pb0", lo, hi), 0.0, None, A.is_gt)
-            else:
-                signs(sw, V("pb0", 0, C))
-        else:
-            sw, lz = V("bw"), V("lz")
-            dma("S", [], [sw], lambda: [(T["bw"][1::16, :], T["bw"][0::16, :])], 32 * C)
-            ts(lz, V("sl", 3, 4 * NL, 4), SC, 2 * MID + 1.25, A.mult, A.add)
-        unpack("fb", qc, qs, ((0, C),), banks[:-3], lent, home)
-        if not home:
-            unpack("fp", "rc%d" % r, "rs%d" % r, FP, banks[:-2])
-        z = V("z%d" % r)
-        if TUNE["xor"]:
-            move(z, sw, lst=lz)
-            if r == 1:
-                move(V("zc"), sw, lst=lz)
-            else:
-                tt(V("zc"), sw, V("swap", 1, 2 * C, 2), A.not_equal, lst=lz)
-        else:
-            if r == 1:
-                move(z, sw, lst=lz)
-            else:
-                tt(z, sw, V("z%d" % (r - 1)), A.mult, lst=lz)
+        banks = BANKS["h"]
+        unpack("fb", qc, qs, ((0, C),), BANKS["fb"], lent)
+        unpack("fp", "rc%d" % r, "rs%d" % r, FP, BANKS["fp"])
+        z = V("z")
+        move(z, V("bo"), lst=V(la))
+        if r == 1:
             move(V("zc"), z)
+        else:
+            tt(V("zc"), V("bo"), V("swap", 1, 2 * C, 2), A.not_equal, lst=V(la))
         tt(V("swap", 1, 2 * C, 2), z, V("zc"), A.not_equal, lst=V("lm"))
         scan(V("tb"), V("swap"), V("pair"))
         if r == 3:
@@ -464,36 +487,38 @@ def rank_program(g, core, T, topo):
             move(V("pl_t"), V("tb", 1, 2 * C, 2), plus=float(MID))
             dma("S", [V("pl_t")], [], lambda: [(T.pl[:, C:2 * C], T["pl_t"][0::16, :])], 32 * C)
         k = 0
-        for i, (lo, hi) in enumerate(HP if home else ZP):
+        for i, (lo, hi) in enumerate(ZP):
             for t in range(4):
-                move(V("zt", 4 * lo + t, 4 * hi, 4), V(("fb%d" if home else "fp%d") % t), lst=V(la if home else "lp%d" % r, lo // 16, hi // 16))
+                move(V("zt", 4 * lo + t, 4 * hi, 4), V("fp%d" % t), lst=V("lp%d" % r, lo // 16, hi // 16))
             zq, zs = V("zq%d" % r, lo, hi), V("zs%d" % r, lo, hi)
             quant(zq, zs, V("zt", 4 * lo, 4 * hi))
-            if home:
-                j = (send(r, "r_%d_%d" % (r, 2 * i), V("rs%d" % r, lo, hi), zs, False, j),)
-                j = (send(r, "r_%d_%d" % (r, 2 * i + 1), V("rc%d" % r, lo, hi), zq, True, j),)
-                zq, zs = V("rc%d" % r, lo, hi), V("rs%d" % r, lo, hi)
             for b in range(4):
                 bank = V("pb%d" % banks[k % len(banks)], 0, hi - lo)
                 k += 1
-                mm(bank, [(V("wq", 128 * b, 128 * b + 128), V("wqs", 128 * b, 128 * b + 128), zq, zs)])
+                mm(bank, V("wq", 128 * b, 128 * b + 128), V("wqs", 128 * b, 128 * b + 128), zq, zs)
                 move(V("hs%d" % b, lo, hi), bank, scale=0.03125)
-        nx = ("x2", "x3", "x4")[r - 1]
-        for lo, hi in NP[r - 1]:
+        nx, made = ("x2", "x3", "x4")[r - 1], {}
+        for i, (lo, hi) in enumerate(NP[r - 1]):
             for b in range(4):
                 out, lst = V(nx, 4 * lo + b, 4 * hi, 4), V(la, lo // 16, hi // 16)
                 if b in lent:
                     move(V("kk%d" % b, lo, hi), V("hs%d" % b), lst=lst, qs="A")
-                    tt(out, V("pb%d" % HOLD[b], lo, hi), V("kk%d" % b, lo, hi), A.add)
+                    made[i, b] = tt(out, V("pb%d" % HOLD[b], lo, hi), V("kk%d" % b, lo, hi), A.add)
                 else:
-                    tt(out, V("hs%d" % b), V("fb%d" % b, lo, hi), A.add, lst=lst)
+                    made[i, b] = tt(out, V("hs%d" % b), V("fb%d" % b, lo, hi), A.add, lst=lst)
         if r < 3:
-            lists()
+            as_list(V("lpp"), V("tp"), V("tb", 1, 2 * C, 2))
+            lists(TP)
+    phase[0] = 0
     quant(V("vq"), V("vqs"), V("vt"))
+    phase[0] = 4
     for i, (a, b) in enumerate(XP[3]):
-        quant(V("qc4", a, b), V("qs4", a, b), V("x4", 4 * a, 4 * b))
+        j = quant(V("qc4", a, b), V("qs4", a, b), V("x4", 4 * a, 4 * b))
+        for (k, t), u in made.items():
+            if k > i and t >= TUNE["late"]:
+                ops[u]["deps"][j] = False
         dma("S", [V("qc4", a, b)], [], lambda a=a, b=b: [(T.oc[:, 4 * a:4 * b], T["qc4"][:, a:b].bitcast(dt.uint8))], 512 * (b - a))
-        mm(V("pb%d" % i, 0, b - a), [(V("vq"), V("vqs"), V("qc4", a, b), V("qs4", a, b))])
+        mm(V("pb%d" % i, 0, b - a), V("vq"), V("vqs"), V("qc4", a, b), V("qs4", a, b))
         move(V("yt", a, b), V("pb%d" % i, 0, b - a))
         dma("S", [V("yt", a, b)], [], lambda a=a, b=b: [(T.y[:, a:b], T["yt"][:, a:b])], 512 * (b - a))
     dma("S", [V("qs4")], [], lambda: [(T.osc[4 * k:4 * k + 4, :], T["qs4"][32 * k:32 * k + 4, :]) for k in range(4)], 16 * C)
@@ -503,8 +528,14 @@ def rank_program(g, core, T, topo):
     for i, o in enumerate(ops):
         for j in o["deps"]:
             users[j].append(i)
+    left, topo_order = [len(o["deps"]) for o in ops], [i for i, o in enumerate(ops) if not o["deps"]]
+    for i in topo_order:
+        for u in users[i]:
+            left[u] -= 1
+            if not left[u]:
+                topo_order.append(u)
 
-    def place(rank_of, before, after, back):
+    def place(rank_of, before, after):
         busy = {k: [] for k in "VAPGSD"}
         start, end, free, qof = [None] * n, [None] * n, [None] * n, [None] * n
         left = [len(before[i]) for i in range(n)]
@@ -514,7 +545,9 @@ def rank_program(g, core, T, topo):
             ready.remove(i)
             lag, best = late[0][i], None
             for q, c in cost[0][i].items():
-                t = max([(free[j] + lag if back else end[j]) + CASES[0]["same" if qof[j] == q else "wake"] if wait is True or (wait and qof[j] != q) else free[j] for j, wait in before[i].items()] + [lag if back else 0.0])
+                if home.get(i, q) != q:
+                    continue
+                t = max([end[j] + CASES[0]["same" if qof[j] == q else "wake"] if wait is True or (wait and qof[j] != q) else free[j] for j, wait in before[i].items()] + [0.0])
                 taken = busy.get(q, ())
                 k, hi = 0, len(taken)
                 while k < hi:
@@ -529,7 +562,7 @@ def rank_program(g, core, T, topo):
                 if best is None or worth < best[0]:
                     best = (worth, t + c, t, q, k)
             free[i], start[i], qof[i] = best[1:4]
-            end[i] = free[i] + (0.0 if back else lag)
+            end[i] = free[i] + lag
             if qof[i] in busy:
                 busy[qof[i]].insert(best[4], (start[i], free[i]))
             for u in after[i]:
@@ -541,8 +574,8 @@ def rank_program(g, core, T, topo):
     def refine(plan):
         qof, seq = list(plan[3]), sorted(range(n), key=lambda j: (plan[1][j], j))
         seq = [k for j in seq if qof[j] != "D" for k in ([j, landing[j]] if j in landing else [j])]
-        above, hard, soft = [0] * n, [None] * n, [None] * n
-        for i in range(n):
+        above, hard, soft, every = [0] * n, [None] * n, [None] * n, [0] * n
+        for i in topo_order:
             firm = [j for j, wait in fore[i].items() if wait is True]
             implied = 0
             for j in firm:
@@ -550,59 +583,16 @@ def rank_program(g, core, T, topo):
             hard[i] = [j for j in firm if not implied >> j & 1]
             soft[i] = [(j, wait) for j, wait in fore[i].items() if wait is not True and not implied >> j & 1]
             above[i] = implied | sum(1 << j for j in firm)
-        every = [0] * n
-        for i in range(n):
             for j in fore[i]:
                 every[i] |= every[j] | 1 << j
-
-        def replay(case, p, left, end):
-            free, wake, same, dear, lag = dict.fromkeys("VAPGSRD"), CASES[case]["wake"], CASES[case]["same"], cost[case], late[case]
-            k, missing = p - 1, 7
-            while k >= 0 and missing:
-                if free[qof[seq[k]]] is None:
-                    free[qof[seq[k]]] = left[seq[k]]
-                    missing -= 1
-                k -= 1
-            for i in seq[p:]:
-                q = qof[i]
-                t = free[q] or 0.0
-                for j in hard[i]:
-                    e = end[j] + (same if qof[j] == q else wake)
-                    if e > t:
-                        t = e
-                for j, wait in soft[i]:
-                    e = end[j] + wake if wait and qof[j] != q else left[j]
-                    if e > t:
-                        t = e
-                left[i] = free[q] = t = t + dear[i][q]
-                end[i] = t + lag[i]
-            return max(end)
-
-        def behind(case, i, q, tail, among):
-            wake, same, lag, far = CASES[case]["wake"], CASES[case]["same"], late[case][i], late[case][i]
-            for j, wait in uses[i]:
-                if among(j):
-                    far = max(far, tail[j] + (lag + (same if qof[j] == q else wake) if wait is True or (wait and qof[j] != q) else 0.0))
-            return far
-
-        def stretch(case, lo, hi):
-            left, tail, follows, after = state[case][0], [0.0] * n, {}, {}
-            for k in range(n - 1, -1, -1):
-                if k == hi - 1:
-                    after = dict(follows)
-                i = seq[k]
-                tail[i] = follows[qof[i]] = cost[case][i][qof[i]] + max(behind(case, i, qof[i], tail, lambda j: True), follows.get(qof[i], 0.0))
-            out = lambda j: pos[j] >= hi
-            free, fixed = dict.fromkeys("VAPGSRD", 0.0), 0.0
-            for i in seq[:lo]:
-                free[qof[i]] = left[i]
-                fixed = max(fixed, left[i] + behind(case, i, qof[i], tail, out))
-            span = max(left[i] - cost[case][i][qof[i]] + tail[i] for i in seq[lo:hi])
-            way = [i for i in seq[lo:hi] if left[i] - cost[case][i][qof[i]] + tail[i] > span - TUNE["near"]]
-            return free, fixed, after, {i: {q: behind(case, i, q, tail, out) for q in cost[case][i]} for i in seq[lo:hi]}, way
+        uses = [[] for _ in range(n)]
+        for i in range(n):
+            for j, wait in [(j, True) for j in hard[i]] + soft[i]:
+                uses[j].append((i, wait))
+        state, pos, each = [([0.0] * n, [0.0] * n, [0.0] * n) for case in CASES], [0] * n, range(len(CASES))
 
         def whole(case, lo, hi, free, far, after, ways, way):
-            (left, end), free, wake, same, dear, lag = state[case], dict(free), CASES[case]["wake"], CASES[case]["same"], cost[case], late[case]
+            (left, end, tail), free, wake, same, dear, lag = state[case], dict(free), CASES[case]["wake"], CASES[case]["same"], cost[case], late[case]
             for i in seq[lo:hi]:
                 q = qof[i]
                 t = free[q]
@@ -622,32 +612,73 @@ def rank_program(g, core, T, topo):
             for q, t in after.items():
                 if free[q] + t > far:
                     far = free[q] + t
-            return far
+            return far * WORTH[case]
+
+        lags = [[dict.fromkeys(cost[case][i], late[case][i]) for i in range(n)] for case in each]
+
+        def replay(case):
+            return whole(case, 0, n, dict.fromkeys("VAPGSRD", 0.0), 0.0, {}, lags[case], None)
+
+        def firsts(hi):
+            return {qof[j]: j for j in reversed(seq[hi:])}
+
+        def tails(case, lo, hi):
+            tail, wake, same, dear, lags = state[case][2], CASES[case]["wake"], CASES[case]["same"], cost[case], late[case]
+            follows = {q: tail[j] for q, j in firsts(hi).items()}
+            for i in reversed(seq[lo:hi]):
+                q = qof[i]
+                lag = lags[i]
+                far = max(lag, follows.get(q, 0.0))
+                for j, wait in uses[i]:
+                    t = tail[j] + (lag + (same if qof[j] == q else wake) if wait is True or (wait and qof[j] != q) else 0.0)
+                    if t > far:
+                        far = t
+                tail[i] = follows[q] = far + dear[i][q]
+
+        def stretch(lo, hi):
+            lasts, nexts = {qof[i]: i for i in seq[:lo]}, firsts(hi)
+            over = [(i, j, wait) for i in seq[:lo] for j, wait in uses[i] if pos[j] >= hi]
+            out = {i: [(j, wait) for j, wait in uses[i] if pos[j] >= hi] for i in seq[lo:hi]}
+            known = []
+            for case in each:
+                tails(case, lo, hi)
+                (left, end, tail), wake, same, lag = state[case], CASES[case]["wake"], CASES[case]["same"], late[case]
+                reach = lambda i, q, j, wait: tail[j] + (lag[i] + (same if qof[j] == q else wake) if wait is True or (wait and qof[j] != q) else 0.0)
+                free = dict.fromkeys("VAPGSRD", 0.0)
+                free.update((q, left[i]) for q, i in lasts.items())
+                fixed = max([left[i] + reach(i, qof[i], j, wait) for i, j, wait in over] + [0.0])
+                span = max(left[i] - cost[case][i][qof[i]] + tail[i] for i in seq[lo:hi])
+                way = [i for i in seq[lo:hi] if left[i] - cost[case][i][qof[i]] + tail[i] > span - TUNE["near"]]
+                ways = {i: {q: max([lag[i]] + [reach(i, q, j, wait) for j, wait in out[i]]) for q in cost[case][i]} for i in out}
+                known.append((free, fixed, {q: tail[j] for q, j in nexts.items()}, ways, way))
+            return known
 
         seed = [TUNE["seed"]]
 
         def rnd():
             seed[0] = (seed[0] * 1103515245 + 12345) % 2 ** 31
             return seed[0] / 2.0 ** 31
-        uses = [[] for _ in range(n)]
-        for i in range(n):
-            for j, wait in [(j, True) for j in hard[i]] + soft[i]:
-                uses[j].append((i, wait))
-        state, pos, each = [([0.0] * n, [0.0] * n) for case in CASES], [0] * n, range(len(CASES))
-        now = sum(replay(k, 0, *state[k]) for k in each)
-        best = (now, list(seq), list(qof))
+        best, last = (sum(replay(k) for k in each), list(seq), list(qof)), n
         for turn in range(TUNE["tries"]):
             heat = TUNE["heat"] * (1.0 - turn / TUNE["tries"]) ** 2 + 1.0
             if turn % TUNE["stay"] == 0:
-                for k in each:
-                    replay(k, 0, *state[k])
-                left = state[0][0]
-                seq.sort(key=lambda j: left[j] - cost[0][j][qof[j]])
-                for k in range(n):
-                    pos[seq[k]] = k
-                first = max(0, min(n - TUNE["wide"], int(rnd() * (n + TUNE["wide"] // 2)) - TUNE["wide"] * 3 // 4))
+                if last >= n:
+                    for k in each:
+                        replay(k)
+                    left = state[0][0]
+                    seq.sort(key=lambda j: left[j] - cost[0][j][qof[j]])
+                    for k in range(n):
+                        pos[seq[k]] = k
+                    for k in each:
+                        tails(k, 0, n)
+                    first = 0
+                else:
+                    for k in each:
+                        whole(k, first, last, *known[k])
+                    first = min(n - TUNE["wide"], first + 1 + int(rnd() * TUNE["wide"] * TUNE["pace"]))
                 last = first + TUNE["wide"]
-                known = [stretch(k, first, last) for k in each]
+                known = stretch(first, last)
+                ends = [whole(k, first, last, *known[k]) for k in each]
             way = known[int(rnd() * len(CASES))][4]
             i = way[int(rnd() * len(way))] if rnd() < TUNE["way"] else seq[first + int(rnd() * TUNE["wide"])]
             q, at = qof[i], pos[i]
@@ -686,41 +717,69 @@ def rank_program(g, core, T, topo):
                     continue
                 moved = [k for j in moved if j not in own for k in ([j, landing[j]] if j in landing else [j])]
             seq[lo:hi] = moved
-            mark = sum(whole(k, first, last, *known[k]) for k in each)
-            if mark <= now - heat * math.log(1.0 - rnd()):
-                now = mark
+            room, trial, worse = -heat * math.log(1.0 - rnd()), [], 0.0
+            for k in each:
+                trial.append(whole(k, first, last, *known[k]))
+                worse += trial[k] - ends[k]
+                if worse > room + TUNE["quit"]:
+                    break
+            if worse <= room:
+                ends = trial
                 for k in range(lo, hi):
                     pos[seq[k]] = k
-                if now < best[0]:
-                    best = (now, list(seq), list(qof))
+                if sum(ends) < best[0]:
+                    best = (sum(ends), list(seq), list(qof))
             else:
                 seq[lo:hi] = was
                 if mate is not None:
                     qof[mate] = qof[i]
                 qof[i] = q
-        now, seq, qof = best
-        spans = [replay(k, 0, *state[k]) for k in range(len(CASES))]
-        TUNE["mark"] = [round(v) for v in spans]
+        seq[:], qof[:] = best[1:]
+        spans = [replay(k) for k in each]
+        TUNE["mark"] = [round(v / w) for v, w in zip(spans, WORTH)]
         start = [0] * n
         for k, i in enumerate(seq):
             start[i] = k
         return spans[0], start, state[0][1], qof
 
-    cost = [[{q: sum(_price(m, *part) for part in (c if isinstance(c, list) else [c])) for q, c in o["cost"].items()} for o in ops] for m in CASES]
+    cost = [[{q: _price(m, *c) for q, c in o["cost"].items()} for o in ops] for m in CASES]
     late = [[_price(m, *o.get("late", ("none",))) for o in ops] for m in CASES]
     fore = [o["deps"] for o in ops]
-    aft = [{u: ops[u]["deps"][i] for u in users[i]} for i in range(n)]
+    home, lead = {}, [dict(d) for d in fore]
+    for q in "VAPGS":
+        before = None
+        for r, names in ORDER:
+            for name in names.get(q, "").split():
+                name, _, k = name.partition(".")
+                i = named.get((0 if name[0] == "-" else r + name.count("+"), name.strip("+-"), int(k or 0)))
+                if i is not None and i not in home and q in ops[i]["cost"]:
+                    home[i] = q
+                    ahead, todo = set(), [] if before is None else [before]
+                    while todo:
+                        fresh = [j for j in lead[todo.pop()] if j not in ahead]
+                        ahead.update(fresh)
+                        todo += fresh
+                    if i in ahead:
+                        continue
+                    if before is not None:
+                        lead[i].setdefault(before, False)
+                    before = i
+    aft = [{} for _ in range(n)]
+    for i in range(n):
+        for j, wait in lead[i].items():
+            aft[j][i] = wait
+    left, order = [len(d) for d in lead], [i for i in range(n) if not lead[i]]
+    for i in order:
+        for u in aft[i]:
+            left[u] -= 1
+            if not left[u]:
+                order.append(u)
     prio = [0.0] * n
-    for i in range(n - 1, -1, -1):
-        prio[i] = min(cost[0][i].values()) + late[0][i] + max([prio[u] + CASES[0]["wake"] for u in users[i]] + [0.0])
-    plans = PLANS
-    for turn in range(0 if plans else TUNE["turns"]):
-        plans.append(place(prio, fore, aft, False))
-        prio = place(plans[-1][2], aft, fore, True)[2]
-    if len(plans) == TUNE["turns"]:
-        plans.append(refine(min(plans, key=lambda p: p[0])))
-    span, start, end, qof = plans[-1]
-    TUNE["span"] = [round(p[0]) for p in plans]
+    for i in reversed(order):
+        prio[i] = min(cost[0][i].values()) + late[0][i] + max([prio[u] + (CASES[0]["wake"] if wait else 0.0) for u, wait in aft[i].items()] + [0.0])
+    if not PLANS:
+        PLANS.append(refine(place(prio, lead, aft)))
+    span, start, end, qof = PLANS[0]
 
     eng = {"V": g.vector, "A": g.scalar, "P": g.tensor, "G": g, "S": g.sync}
     csem = {"V": "s_v", "A": "s_a", "P": "s_p", "G": "s_g"}
@@ -745,14 +804,12 @@ def rank_program(g, core, T, topo):
             count[q] += 1
             call.then_inc(T.sem[csem[q]], 1)
             token[i] = (csem[q], count[q])
-        elif o["kind"] == "d":
-            token[i] = (o["sem"], o["amount"])
         if token[i]:
             clock[i] = dict(known[q])
             clock[i][token[i][0]] = max(clock[i].get(token[i][0], 0), token[i][1])
     for q in csem:
         g.wait_ge(T.sem[csem[q]], count[q])
     for o in ops:
-        if o["kind"] in "dr":
+        if o["kind"] == "r":
             g.wait_ge(T.sem[o["sem"]], o["amount"])
     g.wait_ge(T.sem["loc"], sent[0])

import math
from concourse.mybir import dt, AluOpType, ActivationFunctionType, AxisListType

C = 416
NL = C // 16
MID = C // 2
L = 10
GT = 24
BW = 6 * GT + 4
B2 = BW + 3 * GT + 128
POLY = ((3.0, -6.0, -3.0, 1.0), (-1.0, 3.0, -2.0), (1.0, 0.0, -1.0), (-3.0, 3.0, 6.0))
STEP = (1, 2, 3)
LOADS = ("pkuxXm", "SAASAS")
LATER = ("ws", "v", "")
XP = (((0, 288), (288, C)),) * 3 + (((0, 160), (160, 288), (288, C)),)
NP = XP[1:]
ZP = ((0, 224), (224, C))
CUTS = {"fb": (1, 1, 1, 1), "fp": (1, 1, 1, 1)}
FP = ((0, 288), (288, C))
MQ = ((0,), (1,))
RP = (((0, 224), (224, C)),) * 2
TP = (((0, C),),) * 3
TP1 = (((0, 192), (192, C)),) * 3
AT = ((0, 2), (2, 4), (4, 5), (5, 6))
HOLD = (3, 3, 4, 5)
LENT = ((3,),) * 3
BANKS = {"fb": (2, 3, 4), "fp": (2, 3, 4, 6), "h": (2, 3, 4, 1, 0, 6, 7)}
F32, BF16, F16, I32, U16, CODE, U8 = "float32", "bfloat16", "float16", "int32", "uint16", "float8_e4m3fn_x4", "uint8"
MW = 256

SCRATCH, PART = {}, {}


def _buf(cols, dtype, *names, where="sbuf"):
    for name in names:
        SCRATCH[name] = (where, [128, cols], dtype)


def _parts(whole, cols, dtype, *names):
    SCRATCH[whole] = ("sbuf", [128, cols * len(names)], dtype)
    for i, name in enumerate(names):
        PART[name] = (whole, i * cols, cols)


_buf(512, F32, *["pb%d" % i for i in range(8)], where="psum")
_buf(16, F32, "cols")
_buf(128, BF16, "k0", "k1")
_buf(4 * GT + 48, BF16, "sp", "sw")
_buf(6, I32, "ip")
_buf(8, F32, "fw")
_buf(8, I32, "iu")
_buf(8, U16, "lu1")
_buf(7, U16, "lq")
_parts("li", NL, I32, "kgw", "pgw", "mgw")
_parts("lu", NL, U16, "l0", "lpw", "lm", "lm2", "lpp")
_parts("lists", NL, U16, "l1", "l2")
_buf(C, BF16, "place", "kb", "z", "zc", "tp", "bo")
_buf(2 * C, BF16, "tb", "bw", "bp", "swap")
_buf(2 * C, F16, "pair")
_buf(C, F32, "yt", "kk0", "kk1", "kk2", "kk3")
_buf(520, BF16, "w1", "ones")
_buf(4 * B2, BF16, "w2")
_buf(512, BF16, "w3", "ut", "vt")
_buf(576, BF16, "at")
_buf(28 * L, F32, "chain")
PART.update(six=("chain", 20, 12), sc=("chain", 4 * L, GT * L))
_buf(64, BF16, "f0", "f1", "f2")
_buf(24, U16, "la4")
_buf(C, F32, "pl_t")
_buf(32, F32, "lw", "lt")
_buf(4 * NL, F32, "sl")
_buf(8 * NL, F32, "cs")
_buf(3 * NL, F32, "su")
_buf(NL, F32, "sf", "d3")
_buf(4 * C, BF16, "xt", "x2", "x3", "x4", "zt")
_buf(4 * MW, BF16, "mt")
for _c, _s, _n in (("uq", "uqs", 128), ("vq", "vqs", 128), ("wq", "wqs", 512), ("ud", "uds", 128), ("b2", "b2s", B2), ("b3", "b3s", 128), ("mq", "mqs", MW), ("aq", "aqs", 128), ("zq1", "zs1", C), ("zq2", "zs2", C), ("zq3", "zs3", C)):
    _buf(_n, CODE, _c)
    _buf(_n, U8, _s)
_parts("ec", 128, CODE, *["e%d" % i for i in range(4)])
_parts("ep", 128, U8, *["es%d" % i for i in range(4)])
_parts("hs", C, F32, *["hs%d" % i for i in range(4)])
_parts("fb", C, BF16, *["fb%d" % i for i in range(4)])
_parts("fp", C, BF16, *["fp%d" % i for i in range(4)])
_parts("tg", C, BF16, "tg1", "tg2", "tg3")
_parts("tsum", C, BF16, "ts1", "ts0", "ts3", "ts2")
for _i in (1, 2, 3, 4):
    _buf(C, CODE, "qc%d" % _i)
    _buf(C, U8, "qs%d" % _i)
for _i in (1, 2, 3):
    _buf(C, CODE, "rc%d" % _i)
    _buf(C, U8, "rs%d" % _i)
    _buf(NL, U16, "la%d" % _i, "lp%d" % _i)

SEMAPHORES = ["s_v", "s_a", "s_p", "s_g", "loc"] + ["d_%d" % i for i in range(40)] + ["r_%d_%d" % (r, i) for r in (1, 2, 3) for i in range(8)] + ["r_l%d" % r for r in (1, 2, 3)]

NAMES = ("f", "g", "wake", "same", "vfix", "afix", "least", "aleast", "gv", "ar", "pe", "pfix", "rem", "remb", "first", "issue", "dma", "dmab", "start", "rrow")
CASES = [dict(zip(NAMES, c)) for c in (
    (1.05, 1.05, 207.0, 212.0, 29.0, 55.0, 30.0, 55.0, 30.0, 0.95, 0.49, 77.0, 1040.0, 74.0, 530.0, 210.0, 2025.0, 235.0, 30.0, 1.0),
    (1.00, 0.86, 188.0, 212.0, 27.0, 56.0, 30.0, 4.0, 30.0, 0.96, 0.49, 72.0, 980.0, 75.0, 960.0, 120.0, 1980.0, 267.0, 30.0, 2.0),
    (1.06, 1.54, 58.0, 194.0, 35.0, 92.0, 33.0, 42.0, 30.0, 0.99, 0.63, 117.0, 920.0, 70.0, 1580.0, 364.0, 1000.0, 350.0, 105.0, 1.0),
    (1.50, 1.61, 256.0, 265.0, 30.0, 74.0, 30.0, 48.0, 51.0, 0.99, 0.63, 58.0, 1630.0, 62.0, 520.0, 223.0, 2710.0, 350.0, 39.0, 5.0),
    (1.08, 2.06, 140.0, 280.0, 43.0, 49.0, 31.0, 22.0, 74.0, 1.11, 0.64, 95.0, 1580.0, 50.0, 2430.0, 294.0, 1830.0, 350.0, 30.0, 0.0))]
WORTH = (1.0, 0.6, 1.6, 0.8, 1.2)
CHAIN = " ".join("+sc.%d" % k for k in range(1, 21)) + " +at +at.1 +at.2 +at.3"
START = {"S": "dma dma.3 dma.5 +dma +dma.1 +dma.2",
         "A": "dma.1 dma.2 dma.4 mt chain w2.8 six six.2 fw.1 fw.4 fw.3 kb tb.1 tb uds tg1 tg1.1 w2 w2.2 w2.3 cols.4 +bw +bw.1 tg2.1 tg2 w2.5 +mt +mt.1 +mt.2 tg3.1 tg3 cols.3 +fb0 cs at.1 +fb2 +at.4 +at.5 +at.6 cs.4 +at.7 cs.2 +fp3 +fb1",
         "V": "ones ip.3 ip.4 ip.2 ip.1 mt.1 cols.8 w2.9 lq cols.5 fw cols.6 place fw.5 six.3 cols.9 fw.2 six.1 cols.7 lu1 lpw l0 lpp sw kb.1 uq w2.1 cols.1 w2.4 w2.7 ud kb.2 +qc cols.2 pair +qc.1 e3 ts1 +bo l1 +bo.1 "
              "f2 e2 +bp w2.6 ts2 la4.1 e0 l2 b2 +mt.3 +mq ts0 +mq.1 e1 lm2 la4 +sc ts3 +sc.1 +sc.2 +sc.3 +sc.4 sf +sc.5 +sc.6 +sc.7 +sc.8 su +sc.9 +sc.10 +sc.11 +sc.12 +sc.13 +sc.14 +sc.15 +sc.16 "
              "+sc.17 +sc.18 +sc.19 +sc.20 cs.1 +at +at.1 +at.2 +at.3 d3 b3 +aq cs.3 +fp2 +sl lm +la",
         "G": "ip iu cols k0 sp k1 sp.1 w1 f0 sc f1 +send at +send.1 w3 w3.3 w3.1 +send.2 swap w3.5 w3.2 w3.4 lw",
         "P": "+ud*qc.1 +ud*qc +ud*qc.2 +ud*qc.3 +e0*qc +mq*b2 +mq*b2.1 +mq*b2.2 +e2*qc +e3*qc +e1*qc +e3*rc +e2*rc +aq*b3 +e0*rc +e3*rc.1 +e1*rc"}
ROUND = {"S": "+dma", "G": "send.3 +send +send.1 +send.2",
         "A": "z fp1 fp2.1 fp3.1 fp1.1 zt zt.2 zt.4 zt.5 zt.6 tg1 hs3 hs1 hs1.1 hs3.1 hs0.1 kk3 kk3.1 tg2 +bw +bw.1 tg3 +mt +mt.2 +fb1 +fb0 +fb2 +at.4 cs.3 +at.5 +at.6 +at.7 cs.1 +fp0 +fp1 +fp3",
         "V": "-pair.1 zc fp0.1 swap zt.3 zt.1 zt.7 zq tb zq.1 hs0 hs2 hs2.1 ts1 x.2 x.6 x.1 l1 x x.3 x.7 x.4 +qc x.5 tp +qc.1 ts2 +bo l2 lpp +bo.1 +bp ts3 +mt.1 +mt.3 +mq +mq.1 su +sc sf cs " + CHAIN + " d3 +aq cs.2 +fp2 +sl +la",
         "P": "e1*rc e3*rc.1 e0*rc.1 e1*rc.1 e2*rc.1 wq*zq.3 wq*zq wq*zq.2 wq*zq.6 wq*zq.1 wq*zq.5 wq*zq.7 wq*zq.4 +ud*qc.1 +ud*qc +ud*qc.2 +ud*qc.3 +e1*qc +e0*qc +e2*qc +mq*b2 +mq*b2.1 +mq*b2.2 +e3*qc +e0*rc +e3*rc +e1*rc +e2*rc +aq*b3 +e0*rc.1"}
END = {"S": "dma.1 dma.2 +dma +dma.1 +dma.2 +dma.3 +dma.4 +dma.6 +dma.5", "G": "send.3",
       "A": "z fp2.1 fp3.1 fp1.1 zt.2 zt zt.7 zt.5 hs0 hs1 hs0.1 hs2.1 hs3.1 hs2 kk3 kk3.1 pl_t kk3.2 +yt +yt.1",
       "V": "fp0.1 zc lw swap -vq zt.3 zt.1 zt.4 zq zt.6 lt zq.1 hs3 tb hs1.1 x.8 x.5 x x.1 x.2 x.3 x.4 +qc x.6 x.7 x.9 +qc.1 x.10 x.11 +qc.2 +yt.2",
       "P": "e3*rc.1 e1*rc.1 e2*rc.1 wq*zq wq*zq.3 wq*zq.1 wq*zq.4 wq*zq.5 wq*zq.6 wq*zq.7 wq*zq.2 +vq*qc +vq*qc.1 +vq*qc.2"}
ORDER = [(0, START), (1, ROUND), (2, ROUND), (3, END)]
PLANS = []
TUNE = {"late": 2, "trade": 0.4, "stay": 60, "wide": 60, "near": 250.0, "tries": 1200000, "heat": 110.0, "way": 0.5, "change": 0.3,
        "hops": 14, "spare": 0.1, "seed": 6, "pace": 0.7, "quit": 150.0}


def _price(m, kind, n=0.0):
    cycle = 0.83 * m["f"]
    return {"V": m["vfix"] + max(m["least"], n) * cycle, "A": m["afix"] + max(m["aleast"], n) * cycle * m["ar"],
            "gV": m["gv"] + n * m["g"], "gA": m["gv"] + 15.0 + n * m["g"] * m["ar"], "G": 150.0 + 2.0 * n * cycle,
            "quant": m["vfix"] + (12.0 + 0.22 * n) * m["f"], "P": m["pfix"] + (n + 16.0) * m["pe"], "start": m["start"] * n,
            "send": m["issue"] + n * m["first"], "fly": m["rem"] - m["wake"], "link": n / m["remb"] + 16.0 * m["rrow"], "dma": m["dma"] - m["wake"], "move": n / m["dmab"], "none": 0.0}[kind]


def _hit(a, b):
    if a[1] >= b[2] or b[1] >= a[2]:
        return False
    common = min(a[3], b[3])
    if common > 1 and max(a[3], b[3]) % common == 0:
        return a[1] % common == b[1] % common
    return True


def rank_program(g, core, T, topo):
    rank = T.rank_of(core)
    if rank is None:
        return
    A = AluOpType
    AF = ActivationFunctionType
    ops, seen, loading, phase, named = [], {}, [], [0], {}

    def V(name, lo=0, hi=None, st=1):
        whole, at, cols = PART.get(name, (name, 0, SCRATCH.get(name, (0, (0, 0)))[1][1]))
        return (whole, at + lo, at + (cols if hi is None else hi), st)

    def ap(v):
        if not isinstance(v, tuple):
            return v
        if len(v) > 4:
            return T[v[0]][:, v[2] - 1:v[1] - 1:-v[3]]
        return T[v[0]][:, v[1]:v[2]] if v[3] == 1 else T[v[0]][:, v[1]:v[2]:v[3]]

    def src(v, l):
        return ap(v) if l is None else ap(v).indirect(ap(l))

    def n_of(v):
        return -(-(v[2] - v[1]) // v[3])

    def label(v):
        name = ([p for p, (whole, at, cols) in PART.items() if whole == v[0] and at <= v[1] < at + cols] + [v[0]])[0]
        return name[:-1] if name[:-1] in ("qc", "rc", "zq", "x", "z") and name[-1].isdigit() or name in ("la1", "la2", "la3") else name

    def add(cost, reads, writes, emit, kind="c", sem=None, amount=0, after=(), behind=()):
        i = len(ops)
        deps = {}
        for mode, views in ((0, reads), (1, writes)):
            for v in views:
                if not isinstance(v, tuple):
                    continue
                psum = v[0].startswith("pb")
                for (j, m, w) in seen.setdefault(v[0], []):
                    if j != i and (m or mode) and (psum or _hit(v, w)):
                        deps[j] = True
                    elif j != i and psum:
                        deps.setdefault(j, "read")
                seen[v[0]].append((i, mode, v))
        for j in after:
            deps[j] = True
        for j in list(behind) + (loading[-1:] if "A" in cost else []):
            deps[j] = False
        if kind != "r":
            name = label(reads[0]) + "*" + label(reads[2]) if "P" in cost else label(writes[0]) if kind == "c" else "send" if "G" in cost else "dma"
            k = 0
            while (phase[0], name, k) in named:
                k += 1
            named[phase[0], name, k] = i
        ops.append({"cost": cost, "deps": deps, "emit": emit, "kind": kind, "sem": sem, "amount": amount})
        return i

    def narrow(*views):
        return all(SCRATCH[v[0]][2] in (BF16, F16, U16) for v in views if isinstance(v, tuple) and n_of(v) > 1)

    def costs(qs, out, ins, lst, both=False):
        n = n_of(out)
        if lst is not None:
            c = {"V": ("gV", n), "A": ("gA", n)}
        else:
            c = {"V": ("V", n * (2.0 if both else 0.5 if narrow(out, *ins) else 1.0)), "A": ("A", n)}
        return {q: c[q] for q in qs}

    def ts(out, in0, s1, s2, op0, op1=None, lst=None):
        def emit(e, q):
            if op1 is None:
                return e.tensor_scalar(ap(out), src(in0, lst), ap(s1), None, op0)
            return e.tensor_scalar(ap(out), src(in0, lst), ap(s1), ap(s2), op0, op1)
        return add(costs("V", out, (in0, s1, s2), lst), [in0, lst, s1, s2], [out], emit)

    def tt(out, in0, in1, op, lst=None):
        both = not (in0[0].startswith("pb") or in1[0].startswith("pb"))
        return add(costs("V", out, (in0, in1, V("cols")), lst, both), [in0, in1, lst], [out], lambda e, q: e.tensor_tensor(ap(out), src(in0, lst), ap(in1), op))

    def scan(out, d0, d1, first=0.0):
        return add(costs("V", out, (d0, d1), None), [d0, d1], [out], lambda e, q: e.tensor_tensor_scan(ap(out), ap(d0), ap(d1), first, A.mult, A.add))

    def move(out, in_, lst=None, scale=None, plus=None, relu=False, qs="VA", rows=128):
        def emit(e, q):
            o, i = (ap(out), src(in_, lst)) if rows == 128 else (T[out[0]][0:rows, out[1]:out[2]:out[3]], T[in_[0]][0:rows, in_[1]:in_[2]:in_[3]])
            if q == "V":
                if relu:
                    return e.tensor_scalar(o, i, 0.0, None, A.is_gt)
                if scale is None and plus is None:
                    return e.tensor_copy(o, i)
                if plus is None:
                    return e.tensor_scalar(o, i, ap(scale), None, A.mult)
                if scale is None:
                    return e.tensor_scalar(o, i, ap(plus), None, A.add)
                return e.tensor_scalar(o, i, ap(scale), ap(plus), A.mult, A.add)
            if relu:
                return e.activation(o, i, AF.Relu)
            if plus is not None:
                return e.activation(o, i, AF.Identity, bias=ap(plus), scale=1.0 if scale is None else ap(scale))
            if scale is not None:
                return e.activation(o, i, AF.Copy, scale=ap(scale))
            return e.activation(o, i, AF.Copy)
        return add(costs(qs, out, (in_, scale, plus), lst), [in_, lst, scale, plus], [out], emit)

    def signs(out, in_, mask):
        return add(costs("VA" if mask == HIGH else "V", out, (in_,), None), [in_, mask], [out],
                   lambda e, q: e.tensor_scalar(ap(out), ap(in_), 0.0, ap(mask), A.is_gt, A.mult) if q == "V" else e.activation(ap(out), ap(in_), AF.Sign, scale=ap(mask)))

    def fill(out, val, qs="VAG"):
        ones = V("ones", 0, n_of(out))
        if val != int(val):
            qs = qs.replace("G", "")
        def emit(e, q):
            if q == "V":
                return e.memset(ap(out), val)
            if q == "G":
                return e.iota(ap(out), [[0, n_of(out)]], int(val), 0, allow_small_or_imprecise_dtypes=True)
            return e.activation(ap(out), ap(ones), AF.Copy, scale=val)
        cost = costs(qs.replace("G", ""), out, (), None)
        if "G" in qs:
            cost["G"] = ("G", n_of(out))
        return add(cost, [ones] if "A" in qs else [], [out], emit)

    def quant(c, s, t):
        return add({"V": ("quant", n_of(t))}, [t], [c, s], lambda e, q: e.quantize_mx(ap(c), ap(s), ap(t)))

    def mm(out, a, b, c, d, start=True, stop=True, behind=()):
        return add({"P": ("P", n_of(out))}, [a, b, c, d], [out], lambda e, q: e.matmul_mx(ap(out), ap(a), ap(b), ap(c), ap(d), start, stop), behind=behind)

    def iota(out, pattern, base, cm):
        def emit(e, q):
            if SCRATCH[out[0]][2] != I32:
                return e.iota(ap(out), pattern, base, cm, allow_small_or_imprecise_dtypes=True)
            return e.iota(ap(out), pattern, base, cm)
        return add({"G": ("G", n_of(out))}, [], [out], emit)

    def keep(out, in_, pattern, op, base, cm, other=0.0):
        return add({"G": ("G", n_of(out) + 20)}, [in_], [out], lambda e, q: e.affine_select(ap(out), ap(in_), pattern, op, other, base, cm))

    dcount, lands, sent, landing = [0], [], [0], {}

    def dma(q, reads, writes, pairs, size, behind=()):
        sem = "d_%d" % dcount[0]
        dcount[0] += 1
        def emit(e, q):
            for o, i in pairs():
                e.dma_start(o, i).then_inc(T.sem[sem], 16)
        i = add({q: ("start", len(pairs()))}, reads, writes, emit, "s", behind=[j for j in behind if q in ops[j]["cost"]])
        ops[i]["late"] = ("dma",)
        j = add({"D": ("move", size)}, reads, writes, None, "r", sem, 16 * len(pairs()), after=(i,), behind=[j for j in behind if "D" in ops[j]["cost"]])
        landing[i] = j
        return i, j

    def send(r, sem, dst_v, src_v, codes, behind=()):
        to = T.cores[rank ^ STEP[r - 1]]
        def emit(e, q):
            o, i = (ap(dst_v).bitcast(dt.uint8), ap(src_v).bitcast(dt.uint8)) if codes else (ap(dst_v), ap(src_v))
            e.remote_dma(o, i, T.sem[sem], T.sem["loc"], topo.addr(to)[1], topo.addr(to)[0], topo.mask(core, to))
            sent[0] += len(topo.engines(core, to))
        j = add({"G": ("send", 0 if lands else 1)}, [src_v], [], emit, "s", behind=behind)
        ops[j]["late"] = ("fly",)
        lands.append(add({"R": ("link", 128 * n_of(src_v) * (4 if codes else 2 if SCRATCH[src_v[0]][2] == U16 else 1))}, [], [dst_v], None, "r", sem, len(topo.engines(to, core)), after=(j,), behind=lands[-1:]))
        return j

    col = lambda i: V("cols", i, i + 1)
    SC, ISC, HALF, OWN, TWICE, WEIGHT, FIRST, HIGH, LOW, ODD = [col(i) for i in range(10)]
    KG, PG, MG = V("kgw", 0, NL), V("pgw", 0, NL), V("mgw", 0, NL)

    a, b = XP[0][0][1], C
    loads = {"p": (PG, lambda: [(ap(PG), T.pg[:, :])], 512 * NL), "k": (KG, lambda: [(ap(KG), T.kg[:, :])], 512 * NL), "m": (MG, lambda: [(ap(MG), T.mg[:, :])], 512 * NL),
             "u": (V("ut"), lambda: [(T["ut"][:, :], T.u[:, :])], 128 * 1024), "v": (V("vt"), lambda: [(T["vt"][:, :], T.v[:, :])], 128 * 1024),
             "x": (V("xt", 0, 4 * a), lambda: [(T["xt"][:, 0:4 * a], T.x[:, 0:4 * a])], 1024 * a),
             "X": (V("xt", 4 * a), lambda: [(T["xt"][:, 4 * a:4 * b], T.x[:, 4 * a:4 * b])], 1024 * (b - a)),
             "w": (V("wq"), lambda: [(T["wq"][:, :].bitcast(dt.uint8), T.wc[:, :])], 128 * 2048), "s": (V("wqs"), lambda: [(T["wqs"][:, :], T.ws[:, :])], 128 * 512)}
    done = []
    for name, q in zip(*LOADS):
        done.extend(dma(q, [], [loads[name][0]], loads[name][1], loads[name][2], done))
        if q == "A":
            loading.append(done[-2])

    fill(V("ones"), 1.0, "V")
    scan(V("place"), V("ones", 0, C), V("ones", 0, C), -MID - 1.0)
    fill(V("lw", NL), 0.0)
    iota(OWN, [[0, 1]], 0, 1)
    ts(V("lq"), V("ones", 0, 7), OWN, None, A.mult)
    keep(V("k0"), V("ones", 0, 128), [[1, 128]], A.not_equal, 0, -1)
    keep(V("k1"), V("k0"), [[1, 128]], A.not_equal, -1, -1, 2.0 ** 20)
    move(V("kb", 0, 112), V("k1"), lst=V("lq"))
    move(V("kb", 112, 224), V("kb", 0, 112))
    move(V("kb", 224), V("kb", 0, C - 224))
    add(costs("V", ISC, (), None), [V("kb", 0, 16)], [ISC], lambda e, q: e.tensor_reduce(ap(ISC), ap(V("kb", 0, 16)), AxisListType.X, A.max))
    ts(SC, ISC, 1.0, 2.0 ** -20, A.is_equal, A.max)
    move(HALF, SC, scale=0.5)
    move(TWICE, SC, scale=2.0)
    move(V("lpw"), PG, qs="V")
    ts(V("l0"), KG, 2.0, 1.0, A.mult, A.add)
    move(V("lm"), MG, qs="V")
    ts(V("lm2"), MG, 2.0, 1.0, A.mult, A.add)
    ts(V("lpp"), PG, 2.0, 1.0, A.mult, A.add)
    ts(V("ts0", 15, C, 16), KG, -float(MID), ISC, A.add, A.mult)
    move(V("cs", 3, 4 * NL, 4), V("ts0", 15, C, 16), scale=2.0)

    def as_list(out, sums, flat):
        scan(sums, V("kb"), flat)
        if out:
            ts(out, V(sums[0], sums[1] + 15, sums[2], 16), TWICE, 2 * MID + 1.25, A.mult, A.add)

    def lists(pieces):
        for n in (1, 2, 3):
            for lo, hi in pieces[n - 1]:
                move(V("tg%d" % n, lo, hi), V("tb"), lst=V("l%d" % (n - 1), lo // 16, hi // 16))
            as_list(V("l%d" % n) if n < 3 else None, V("ts%d" % n), V("tg%d" % n))
        some = lambda n, k: V("tsum", n * C + 15, (n + k) * C, 16)
        tt(V("su"), some(1, 3), some(0, 3), A.subtract)
        tt(V("cs", 1, 8 * NL, 4), V("su", NL), V("su", 0, 2 * NL), A.subtract)
        tt(V("d3"), V("cs", 4 * NL + 1, 8 * NL, 4), V("cs", 1, 4 * NL, 4), A.subtract)
        move(V("cs", 0, 4 * NL, 4), V("d3"), scale=1.0 / 3.0)
        tt(V("sf"), some(2, 1), some(0, 1), A.subtract)
        tt(V("cs", 2, 4 * NL, 4), V("sf"), V("cs", 0, 4 * NL, 4), A.subtract)
        move(V("cs", 3, 4 * NL, 4), some(0, 1), scale=2.0, rows=16)

    for lo, hi in ((0, 224), (224, C)):
        move(V("tb", 2 * lo + 1, 2 * hi, 2), V("place"), lst=V("lpw", lo // 16, hi // 16))
    lists(TP1)
    move(V("pair", 1, 2 * C, 2), V("tb", 1, 2 * C, 2), qs="V")
    tt(V("pair", 0, 2 * C, 2), V("tb"), V("pair", 1, 2 * C, 2), A.subtract, lst=V("lm2"))
    fill(V("swap", 0, 2 * C, 2), 0.0)
    quant(V("uq"), V("uqs"), V("ut"))
    iota(V("iu"), [[16, 8]], 0, 0)
    iota(V("ip", 0, 1), [[0, 1]], 0, 1)
    for k, bits in enumerate((1, 124, 14, 13)):
        ts(V("ip", k + 1, k + 2), V("ip", 0, 1), bits, None, A.bitwise_and)
    ts(ODD, V("ip", 4, 5), 1.0, None, A.is_equal)
    ts(V("lu1"), V("iu"), ODD, None, A.add)
    add(costs("V", V("ud"), (), V("lu1")), [V("uq"), V("lu1")], [V("ud")], lambda e, q: e.tensor_copy(ap(V("ud")).bitcast(dt.uint32), ap(V("uq")).bitcast(dt.uint32).indirect(ap(V("lu1")))))
    move(V("uds"), V("uqs"), lst=V("lu1"))
    keep(V("w1"), V("ones", 0, 520), [[1, 520]], A.is_equal, -4, -4)
    for b in range(4):
        quant(V("e%d" % b), V("es%d" % b), V("w1", 4 - b, 516 - b))
    iota(V("sp", 0, 4 * GT), [[-16, 6], [256, 4], [-256, 4]], 96, 0)
    iota(V("sp", 4 * GT), [[0, 3], [256, 4], [-256, 4]], 0, 0)
    ts(WEIGHT, V("ip", 1, 2), 3.0, -1.0, A.mult, A.add)
    move(FIRST, V("ip", 2, 3), qs="V")
    ts(HIGH, V("ip", 3, 4), 2.0, None, A.is_equal)
    ts(LOW, V("ip", 3, 4), 2.0, None, A.not_equal)
    ts(V("sw"), V("sp"), FIRST, WEIGHT, A.is_equal, A.mult)
    move(V("w2", 4 * B2 - 48), V("sw", 4 * GT), scale=HIGH)
    for k, (n, s) in enumerate([(n, s) for n in (0, 1) for s in range(len(POLY[2 * n]))]):
        low, high, at = POLY[2 * n][s], (POLY[2 * n + 1] + (0.0,))[s], 4 * BW * n + 4 * GT * s
        if (low, high) != (1.0, 0.0):
            move(V("fw", k, k + 1), HIGH, scale=high - low, plus=low)
        move(V("w2", at, at + 4 * GT), V("sw", 0, 4 * GT), scale=V("fw", k, k + 1) if (low, high) != (1.0, 0.0) else LOW)
    fill(V("w2", 16 * GT, 4 * BW), 0.0)
    fill(V("w2", 4 * BW + 12 * GT, 4 * B2 - 48), 0.0)
    quant(V("b2"), V("b2s"), V("w2"))
    keep(V("w3", 0, C), V("ones", 0, C), [[4, NL], [0, 4], [1, 4]], A.is_equal, 0, -1)
    fill(V("w3", C), 0.0)
    for t in range(4):
        fill(V("w3", t, C, 16), 0.0)
    quant(V("b3"), V("b3s"), V("w3"))
    fill(V("chain"), 1.0)
    for t in range(4):
        fill(V("chain", 28 + t, 24 * L, 4 * L), 1.0 / 6.0)
    fill(V("sc", 36, None, 4 * L), 0.0)
    iota(V("f0"), [[0, 4], [1, 4], [0, 4]], 12, 0)
    keep(V("f1"), V("f0"), [[1, 4], [0, 4], [-1, 4]], A.is_equal, 0, 0, 36.0)
    scan(V("f2"), V("kb", 0, 64), V("f1"))
    for k in range(max(hi - lo for lo, hi in AT)):
        ts(V("la4", 4 * k, 4 * k + 4), V("f2", 15, 64, 16), SC, 4 * L * k + 0.25, A.mult, A.add)
    fill(V("at", 0, 64), 0.0)
    fill(V("at", 448, 512), 0.0)
    for n in range(2):
        fill(V("mt", 512 * n + C, 512 * n + 512), 0.0)

    def unpack(to, c, s, pieces, banks, skip=()):
        k = 0
        for lo, hi in pieces:
            for b in range(4):
                bank = V("pb%d" % (HOLD[b] if b in skip else banks[k % len(banks)]), 0, hi - lo)
                mm(bank, V("e%d" % b), V("es%d" % b), V(c, lo, hi), V(s, lo, hi))
                if b not in skip:
                    cuts = [(hi - lo) * u // CUTS[to][b] for u in range(CUTS[to][b] + 1)]
                    for u, w in zip(cuts, cuts[1:]):
                        move(V("%s%d" % (to, b), lo + u, lo + w), V(bank[0], u, w))
                k += b not in skip

    for r in (1, 2, 3):
        phase[0] = r
        x, qc, qs, la = ("xt", "x2", "x3")[r - 1], "qc%d" % r, "qs%d" % r, "la%d" % r
        for i, (lo, hi) in enumerate(XP[r - 1]):
            quant(V(qc, lo, hi), V(qs, lo, hi), V(x, 4 * lo, 4 * hi))
            for bank, out, mask in ((i, V("bw", 2 * lo + 1, 2 * hi, 2), HIGH), (6 + i, V("bo", lo, hi), LOW)):
                mm(V("pb%d" % bank, 0, hi - lo), V("ud"), V("uds"), V(qc, lo, hi), V(qs, lo, hi))
                signs(out, V("pb%d" % bank, 0, hi - lo), mask)
        j = ()
        for i, (codes, lo, hi) in enumerate(((True,) + XP[r - 1][0], (False, 0, C), (True,) + XP[r - 1][1])):
            j = (send(r, "r_%d_%d" % (r, i), V(("rc%d" if codes else "rs%d") % r, lo, hi), V(qc if codes else qs, lo, hi), codes, j),)
        tt(V("bp", 1, 2 * C, 2), V("bw"), V("bo"), A.add, lst=V("lpp"))
        dma("S", [], [V("bo")], lambda: [(T["bo"][k::16, :], T["bo"][0::16, :]) for k in (1, 2, 3)], 48 * C)
        term = lambda n, lo, hi: (V("mq", 128 * n, 128 * n + 128), V("mqs", 128 * n, 128 * n + 128), V("b2", lo, hi), V("b2s", lo, hi))
        done = ()
        for rows in MQ:
            lo, hi = 128 * rows[0], 128 * rows[-1] + 128
            for n in rows:
                for a, b in RP[n]:
                    move(V("mt", 512 * n + a, 512 * n + b), V("bp"), lst=V("l%d" % (2 * n), a // 16, b // 16), relu=True)
            i = quant(V("mq", lo, hi), V("mqs", lo, hi), V("mt", 4 * lo, 4 * hi))
            if 0 in rows:
                for name in LATER[r - 1]:
                    ops[dma("S", [], [loads[name][0]], loads[name][1], loads[name][2])[0]]["deps"][i] = True
                mm(V("pb0", 0, 128), *term(0, B2 - 128, B2))
                tt(V("sc", 12, 24), V("pb0", 116, 128), V("six"), A.mult)
            for n in rows:
                done += (mm(V("pb1", 0, BW), *term(n, BW * n, BW * (n + 1)), start=not done, stop=n == MQ[-1][-1], behind=done),)
        for k in range(1, 7):
            for t in range(4):
                at, c = 4 * L * (k - 1) + t, 4 * (6 - k) + t
                if k < 6:
                    scan(V("sc", at + 4 * L, at + 4 * L + 21, 4), V("sc", at + 8, at + 29, 4), V("pb1", c, c + 5 * GT + 1, GT))
                else:
                    scan(V("at", 448 + 4 * t, 448 + 4 * t + 103, 17) + (True,), V("sc", at + 8, at + 33, 4), V("pb1", c, c + 6 * GT + 1, GT))
        for lo, hi in AT:
            move(V("at", 64 * lo + 64, 64 * hi + 64), V("sc", 4 * L * lo, 4 * L * hi), lst=V("la4", 0, 4 * (hi - lo)))
        quant(V("aq"), V("aqs"), V("at", 0, 512))
        mm(V("pb7", 0, 128), V("aq"), V("aqs"), V("b3"), V("b3s"))
        scan(V("sl"), V("pb7", 0, 4 * NL), V("cs", 0, 4 * NL))
        ts(V(la), V("sl", 3, 4 * NL, 4), HALF, MID + 0.25, A.mult, A.add)
        send(r, "r_l%d" % r, V("lp%d" % r), V(la), False, j)
        lent = LENT[r - 1]
        banks = BANKS["h"]
        unpack("fb", qc, qs, ((0, C),), BANKS["fb"], lent)
        unpack("fp", "rc%d" % r, "rs%d" % r, FP, BANKS["fp"])
        z = V("z")
        move(z, V("bo"), lst=V(la))
        if r == 1:
            move(V("zc"), z)
        else:
            tt(V("zc"), V("bo"), V("swap", 1, 2 * C, 2), A.not_equal, lst=V(la))
        tt(V("swap", 1, 2 * C, 2), z, V("zc"), A.not_equal, lst=V("lm"))
        scan(V("tb"), V("swap"), V("pair"))
        if r == 3:
            move(V("lw", 0, NL), V(la), qs="V")
            add(costs("V", V("lt"), (), None), [V("lw")], [V("lt")], lambda e, q: e.transpose(ap(V("lt")), ap(V("lw"))))
            dma("S", [V("lt")], [], lambda: [(T.pl[k:k + 1, 0:C], T["lt"][32 * (k // 2):32 * (k // 2) + NL, 16 * (k % 2):16 * (k % 2) + 16]) for k in range(8)], 64 * C)
            move(V("pl_t"), V("tb", 1, 2 * C, 2), plus=float(MID))
            dma("S", [V("pl_t")], [], lambda: [(T.pl[:, C:2 * C], T["pl_t"][0::16, :])], 32 * C)
        k = 0
        for i, (lo, hi) in enumerate(ZP):
            for t in range(4):
                move(V("zt", 4 * lo + t, 4 * hi, 4), V("fp%d" % t), lst=V("lp%d" % r, lo // 16, hi // 16))
            zq, zs = V("zq%d" % r, lo, hi), V("zs%d" % r, lo, hi)
            quant(zq, zs, V("zt", 4 * lo, 4 * hi))
            for b in range(4):
                bank = V("pb%d" % banks[k % len(banks)], 0, hi - lo)
                k += 1
                mm(bank, V("wq", 128 * b, 128 * b + 128), V("wqs", 128 * b, 128 * b + 128), zq, zs)
                move(V("hs%d" % b, lo, hi), bank, scale=0.03125)
        nx, made = ("x2", "x3", "x4")[r - 1], {}
        for i, (lo, hi) in enumerate(NP[r - 1]):
            for b in range(4):
                out, lst = V(nx, 4 * lo + b, 4 * hi, 4), V(la, lo // 16, hi // 16)
                if b in lent:
                    move(V("kk%d" % b, lo, hi), V("hs%d" % b), lst=lst, qs="A")
                    made[i, b] = tt(out, V("pb%d" % HOLD[b], lo, hi), V("kk%d" % b, lo, hi), A.add)
                else:
                    made[i, b] = tt(out, V("hs%d" % b), V("fb%d" % b, lo, hi), A.add, lst=lst)
        if r < 3:
            as_list(V("lpp"), V("tp"), V("tb", 1, 2 * C, 2))
            lists(TP)
    phase[0] = 0
    quant(V("vq"), V("vqs"), V("vt"))
    phase[0] = 4
    for i, (a, b) in enumerate(XP[3]):
        j = quant(V("qc4", a, b), V("qs4", a, b), V("x4", 4 * a, 4 * b))
        for (k, t), u in made.items():
            if k > i and t >= TUNE["late"]:
                ops[u]["deps"][j] = False
        dma("S", [V("qc4", a, b)], [], lambda a=a, b=b: [(T.oc[:, 4 * a:4 * b], T["qc4"][:, a:b].bitcast(dt.uint8))], 512 * (b - a))
        mm(V("pb%d" % i, 0, b - a), V("vq"), V("vqs"), V("qc4", a, b), V("qs4", a, b))
        move(V("yt", a, b), V("pb%d" % i, 0, b - a))
        dma("S", [V("yt", a, b)], [], lambda a=a, b=b: [(T.y[:, a:b], T["yt"][:, a:b])], 512 * (b - a))
    dma("S", [V("qs4")], [], lambda: [(T.osc[4 * k:4 * k + 4, :], T["qs4"][32 * k:32 * k + 4, :]) for k in range(4)], 16 * C)

    n = len(ops)
    users = [[] for _ in range(n)]
    for i, o in enumerate(ops):
        for j in o["deps"]:
            users[j].append(i)
    left, topo_order = [len(o["deps"]) for o in ops], [i for i, o in enumerate(ops) if not o["deps"]]
    for i in topo_order:
        for u in users[i]:
            left[u] -= 1
            if not left[u]:
                topo_order.append(u)

    def place(rank_of, before, after):
        busy = {k: [] for k in "VAPGSD"}
        start, end, free, qof = [None] * n, [None] * n, [None] * n, [None] * n
        left = [len(before[i]) for i in range(n)]
        ready = [i for i in range(n) if not left[i]]
        while ready:
            i = max(ready, key=lambda j: rank_of[j])
            ready.remove(i)
            lag, best = late[0][i], None
            for q, c in cost[0][i].items():
                if home.get(i, q) != q:
                    continue
                t = max([end[j] + CASES[0]["same" if qof[j] == q else "wake"] if wait is True or (wait and qof[j] != q) else free[j] for j, wait in before[i].items()] + [0.0])
                taken = busy.get(q, ())
                k, hi = 0, len(taken)
                while k < hi:
                    if taken[(k + hi) // 2][1] <= t:
                        k = (k + hi) // 2 + 1
                    else:
                        hi = (k + hi) // 2
                while k < len(taken) and t + c > taken[k][0]:
                    t = max(t, taken[k][1])
                    k += 1
                worth = t + c + (TUNE["spare"] * c if q == "V" else 0.0)
                if best is None or worth < best[0]:
                    best = (worth, t + c, t, q, k)
            free[i], start[i], qof[i] = best[1:4]
            end[i] = free[i] + lag
            if qof[i] in busy:
                busy[qof[i]].insert(best[4], (start[i], free[i]))
            for u in after[i]:
                left[u] -= 1
                if not left[u]:
                    ready.append(u)
        return max(end), start, end, qof

    def refine(plan):
        qof, seq = list(plan[3]), sorted(range(n), key=lambda j: (plan[1][j], j))
        seq = [k for j in seq if qof[j] != "D" for k in ([j, landing[j]] if j in landing else [j])]
        above, hard, soft, every = [0] * n, [None] * n, [None] * n, [0] * n
        for i in topo_order:
            firm = [j for j, wait in fore[i].items() if wait is True]
            implied = 0
            for j in firm:
                implied |= above[j]
            hard[i] = [j for j in firm if not implied >> j & 1]
            soft[i] = [(j, wait) for j, wait in fore[i].items() if wait is not True and not implied >> j & 1]
            above[i] = implied | sum(1 << j for j in firm)
            for j in fore[i]:
                every[i] |= every[j] | 1 << j
        uses = [[] for _ in range(n)]
        for i in range(n):
            for j, wait in [(j, True) for j in hard[i]] + soft[i]:
                uses[j].append((i, wait))
        state, pos, each = [([0.0] * n, [0.0] * n, [0.0] * n) for case in CASES], [0] * n, range(len(CASES))

        def whole(case, lo, hi, free, far, after, ways, way):
            (left, end, tail), free, wake, same, dear, lag = state[case], dict(free), CASES[case]["wake"], CASES[case]["same"], cost[case], late[case]
            for i in seq[lo:hi]:
                q = qof[i]
                t = free[q]
                for j in hard[i]:
                    e = end[j] + (same if qof[j] == q else wake)
                    if e > t:
                        t = e
                for j, wait in soft[i]:
                    e = end[j] + wake if wait and qof[j] != q else left[j]
                    if e > t:
                        t = e
                left[i] = free[q] = t = t + dear[i][q]
                end[i] = t + lag[i]
                t += ways[i][q]
                if t > far:
                    far = t
            for q, t in after.items():
                if free[q] + t > far:
                    far = free[q] + t
            return far * WORTH[case]

        lags = [[dict.fromkeys(cost[case][i], late[case][i]) for i in range(n)] for case in each]

        def replay(case):
            return whole(case, 0, n, dict.fromkeys("VAPGSRD", 0.0), 0.0, {}, lags[case], None)

        def firsts(hi):
            return {qof[j]: j for j in reversed(seq[hi:])}

        def tails(case, lo, hi):
            tail, wake, same, dear, lags = state[case][2], CASES[case]["wake"], CASES[case]["same"], cost[case], late[case]
            follows = {q: tail[j] for q, j in firsts(hi).items()}
            for i in reversed(seq[lo:hi]):
                q = qof[i]
                lag = lags[i]
                far = max(lag, follows.get(q, 0.0))
                for j, wait in uses[i]:
                    t = tail[j] + (lag + (same if qof[j] == q else wake) if wait is True or (wait and qof[j] != q) else 0.0)
                    if t > far:
                        far = t
                tail[i] = follows[q] = far + dear[i][q]

        def stretch(lo, hi):
            lasts, nexts = {qof[i]: i for i in seq[:lo]}, firsts(hi)
            over = [(i, j, wait) for i in seq[:lo] for j, wait in uses[i] if pos[j] >= hi]
            out = {i: [(j, wait) for j, wait in uses[i] if pos[j] >= hi] for i in seq[lo:hi]}
            known = []
            for case in each:
                tails(case, lo, hi)
                (left, end, tail), wake, same, lag = state[case], CASES[case]["wake"], CASES[case]["same"], late[case]
                reach = lambda i, q, j, wait: tail[j] + (lag[i] + (same if qof[j] == q else wake) if wait is True or (wait and qof[j] != q) else 0.0)
                free = dict.fromkeys("VAPGSRD", 0.0)
                free.update((q, left[i]) for q, i in lasts.items())
                fixed = max([left[i] + reach(i, qof[i], j, wait) for i, j, wait in over] + [0.0])
                span = max(left[i] - cost[case][i][qof[i]] + tail[i] for i in seq[lo:hi])
                way = [i for i in seq[lo:hi] if left[i] - cost[case][i][qof[i]] + tail[i] > span - TUNE["near"]]
                ways = {i: {q: max([lag[i]] + [reach(i, q, j, wait) for j, wait in out[i]]) for q in cost[case][i]} for i in out}
                known.append((free, fixed, {q: tail[j] for q, j in nexts.items()}, ways, way))
            return known

        seed = [TUNE["seed"]]

        def rnd():
            seed[0] = (seed[0] * 1103515245 + 12345) % 2 ** 31
            return seed[0] / 2.0 ** 31
        best, last = (sum(replay(k) for k in each), list(seq), list(qof)), n
        for turn in range(TUNE["tries"]):
            heat = TUNE["heat"] * (1.0 - turn / TUNE["tries"]) ** 2 + 1.0
            if turn % TUNE["stay"] == 0:
                if last >= n:
                    for k in each:
                        replay(k)
                    left = state[0][0]
                    seq.sort(key=lambda j: left[j] - cost[0][j][qof[j]])
                    for k in range(n):
                        pos[seq[k]] = k
                    for k in each:
                        tails(k, 0, n)
                    first = 0
                else:
                    for k in each:
                        whole(k, first, last, *known[k])
                    first = min(n - TUNE["wide"], first + 1 + int(rnd() * TUNE["wide"] * TUNE["pace"]))
                last = first + TUNE["wide"]
                known = stretch(first, last)
                ends = [whole(k, first, last, *known[k]) for k in each]
            way = known[int(rnd() * len(CASES))][4]
            i = way[int(rnd() * len(way))] if rnd() < TUNE["way"] else seq[first + int(rnd() * TUNE["wide"])]
            q, at = qof[i], pos[i]
            if q in "RD":
                continue
            mate = None
            if len(ops[i]["cost"]) > 1 and rnd() < TUNE["change"]:
                others = [k for k in ops[i]["cost"] if k != q]
                qof[i] = others[int(rnd() * len(others))]
                near = [j for j in seq[max(first, at - 6):min(last, at + 7)] if j != i and qof[j] == qof[i] and q in ops[j]["cost"]]
                if near and rnd() < TUNE["trade"]:
                    mate = near[int(rnd() * len(near))]
                    qof[mate] = q
            ahead, hops, to = rnd() < 0.5, int(rnd() ** 2 * TUNE["hops"]) + (qof[i] == q), at
            k = at
            while hops:
                k += -1 if ahead else 1
                if k < first or k >= last:
                    break
                if qof[seq[k]] == qof[i] and not (every[i] >> seq[k] & 1 if ahead else every[seq[k]] >> i & 1):
                    to, hops = k, hops - 1
            if to == at and qof[i] == q:
                continue
            lo, hi = min(at, to), max(at, to) + 1
            was = seq[lo:hi]
            tied = [j == i or (every[i] >> j & 1 if ahead else every[j] >> i & 1) for j in was]
            moved = [j for j, t in zip(was, tied) if bool(t) == ahead] + [j for j, t in zip(was, tied) if bool(t) != ahead]
            if [j for j in moved if j in landing] != [j for j in was if j in landing]:
                moved, lo, hi = seq[first:lo] + moved + seq[hi:last], first, last
                was = seq[lo:hi]
                own = {landing[j] for j in moved if j in landing}
                if max(pos[j] for j in own) >= last:
                    if mate is not None:
                        qof[mate] = qof[i]
                    qof[i] = q
                    continue
                moved = [k for j in moved if j not in own for k in ([j, landing[j]] if j in landing else [j])]
            seq[lo:hi] = moved
            room, trial, worse = -heat * math.log(1.0 - rnd()), [], 0.0
            for k in each:
                trial.append(whole(k, first, last, *known[k]))
                worse += trial[k] - ends[k]
                if worse > room + TUNE["quit"]:
                    break
            if worse <= room:
                ends = trial
                for k in range(lo, hi):
                    pos[seq[k]] = k
                if sum(ends) < best[0]:
                    best = (sum(ends), list(seq), list(qof))
            else:
                seq[lo:hi] = was
                if mate is not None:
                    qof[mate] = qof[i]
                qof[i] = q
        seq[:], qof[:] = best[1:]
        spans = [replay(k) for k in each]
        TUNE["mark"] = [round(v / w) for v, w in zip(spans, WORTH)]
        start = [0] * n
        for k, i in enumerate(seq):
            start[i] = k
        return spans[0], start, state[0][1], qof

    cost = [[{q: _price(m, *c) for q, c in o["cost"].items()} for o in ops] for m in CASES]
    late = [[_price(m, *o.get("late", ("none",))) for o in ops] for m in CASES]
    fore = [o["deps"] for o in ops]
    home, lead = {}, [dict(d) for d in fore]
    for q in "VAPGS":
        before = None
        for r, names in ORDER:
            for name in names.get(q, "").split():
                name, _, k = name.partition(".")
                i = named.get((0 if name[0] == "-" else r + name.count("+"), name.strip("+-"), int(k or 0)))
                if i is not None and i not in home and q in ops[i]["cost"]:
                    home[i] = q
                    ahead, todo = set(), [] if before is None else [before]
                    while todo:
                        fresh = [j for j in lead[todo.pop()] if j not in ahead]
                        ahead.update(fresh)
                        todo += fresh
                    if i in ahead:
                        continue
                    if before is not None:
                        lead[i].setdefault(before, False)
                    before = i
    aft = [{} for _ in range(n)]
    for i in range(n):
        for j, wait in lead[i].items():
            aft[j][i] = wait
    left, order = [len(d) for d in lead], [i for i in range(n) if not lead[i]]
    for i in order:
        for u in aft[i]:
            left[u] -= 1
            if not left[u]:
                order.append(u)
    prio = [0.0] * n
    for i in reversed(order):
        prio[i] = min(cost[0][i].values()) + late[0][i] + max([prio[u] + (CASES[0]["wake"] if wait else 0.0) for u, wait in aft[i].items()] + [0.0])
    if not PLANS:
        PLANS.append(refine(place(prio, lead, aft)))
    span, start, end, qof = PLANS[0]

    eng = {"V": g.vector, "A": g.scalar, "P": g.tensor, "G": g, "S": g.sync}
    csem = {"V": "s_v", "A": "s_a", "P": "s_p", "G": "s_g"}
    count = {k: 0 for k in csem}
    known = {k: {} for k in "VAPGS"}
    token, clock = [None] * n, [None] * n
    for i in sorted(range(n), key=lambda j: (start[j], j)):
        o, q = ops[i], qof[i]
        if o["kind"] == "r":
            token[i], clock[i] = (o["sem"], o["amount"]), {o["sem"]: o["amount"]}
            continue
        e = eng[q]
        for j in sorted((j for j, wait in o["deps"].items() if token[j] and (wait is True or (wait and qof[j] != q))), key=lambda j: -end[j]):
            s, v = token[j]
            if known[q].get(s, 0) >= v:
                continue
            e.wait_ge(T.sem[s], v)
            for s2, v2 in clock[j].items():
                known[q][s2] = max(known[q].get(s2, 0), v2)
        call = o["emit"](e, q)
        if o["kind"] == "c":
            count[q] += 1
            call.then_inc(T.sem[csem[q]], 1)
            token[i] = (csem[q], count[q])
        if token[i]:
            clock[i] = dict(known[q])
            clock[i][token[i][0]] = max(clock[i].get(token[i][0], 0), token[i][1])
    for q in csem:
        g.wait_ge(T.sem[csem[q]], count[q])
    for o in ops:
        if o["kind"] == "r":
            g.wait_ge(T.sem[o["sem"]], o["amount"])
    g.wait_ge(T.sem["loc"], sent[0])
